import numpy as np, ml_dtypes
CORES = [48,51,52,55]
N = 4
import mx_ref
BF = ml_dtypes.bfloat16
def gentries(a):
    return np.ascontiguousarray(a.reshape(8, 16, -1).transpose(0, 2, 1)).reshape(8, -1)
def gtable(e):
    e = np.asarray(e); return np.ascontiguousarray(e.reshape(8, -1, 16).transpose(0, 2, 1)).reshape(128, -1).astype(np.int32)
def gcols(t, e):
    v = np.concatenate([t.reshape(8, 16, -1, 4), np.zeros((8, 16, 1, 4), BF)], axis=2)
    return np.ascontiguousarray(np.stack([v[g][:, e[g]] for g in range(8)])).reshape(128, -1)
def gpick(z, e):
    return np.concatenate([z[16 * g:16 * g + 16][:, e[g]] for g in range(8)])
def tile(rs):
    return np.stack(rs, axis=2).reshape(128, -1).astype(BF)
def pick(q, e):
    c = np.concatenate([q[0].reshape(128, -1, 4), np.zeros((128, 1, 4), np.uint8)], axis=1); s = np.concatenate([q[1], np.ones((16, 1), np.uint8)], axis=1)
    return (np.ascontiguousarray(c[:, e].reshape(128, -1)), np.ascontiguousarray(s[:, e]))
def join(*qs):
    return (np.concatenate([q[0] for q in qs], axis=1), np.concatenate([q[1] for q in qs], axis=1))
def put(q, e, v):
    c, s = q[0].reshape(128, -1, 4).copy(), q[1].copy(); c[:, e] = v[0].reshape(128, -1, 4); s[:, e] = v[1]
    return (c.reshape(128, -1), s)
def pk(c, s):
    return (np.ascontiguousarray(c), mx_ref.live(s))
def emit(q):
    return q[0], q[1]
def packed(v, rng):
    q = [mx_ref.quantize(np.ascontiguousarray(v[r])) for r in range(N)]
    return np.stack([a for a, b in q]), np.stack([mx_ref.plane(b, rng) for a, b in q])
def values_of_codes():
    e, c = np.zeros((128, 128, 4), np.float32), np.zeros((128, 2, 4), np.uint8)
    e[np.arange(128), np.arange(128), 0] = 1
    c[:127, :, 0] = np.arange(256).reshape(2, 128).T[:127]
    return mx_ref.matmul(mx_ref.quantize(e.reshape(128, 512).astype(BF)), (c.reshape(128, 8), np.full((16, 2), 127, np.uint8))).T.reshape(-1).astype(np.float64)
CODE_VALUE, SCALE_VALUE = values_of_codes(), 2.0 ** (np.arange(256) - 127.0)
def decode(q):
    return (CODE_VALUE[q[0]].reshape(16, 8, -1, 4) * SCALE_VALUE[q[1]][:, None, :, None] + 0.0).reshape(128, -1).astype(np.float32)
def f(rng, *shape):
    return mx_ref.flush((rng.standard_normal(shape, dtype=np.float32) * np.exp2(rng.integers(-2, 3, shape[:-1] + (1,)))).astype(BF))
def wide(rng, *shape, cols=0):
    v = rng.standard_normal(shape, dtype=np.float32) * np.exp2(rng.integers(-12, 13, shape)).astype(np.float32)
    if cols: v *= np.repeat(np.exp2(rng.integers(-cols, cols + 1, shape[:-2] + (1, shape[-1] // 4))) * (rng.random(shape[:-2] + (1, shape[-1] // 4)) > 0.0625), 4, axis=-1).astype(np.float32)
    return mx_ref.flush(v.astype(BF))
C, K, P, R = 512, 128, 256, 2
def numbers_of(rng):
    return {"x": np.array(f(rng, N, 128, 4 * C)), "u": np.array(f(rng, N, 128, 512)), "v": np.array(f(rng, N, 128, 512))}
def mixed(rng):
    return rng.permuted(np.tile(np.arange(C), (N, 8, 1)), axis=2)
def links(e):
    return np.stack([gtable(e[r]) for r in range(N)])
def packedw(rng, w):
    c, p = packed(np.ascontiguousarray(w).reshape(N, 128, 2048), rng)
    return {"wc": c, "ws": p}
def weights(rng, still=()):
    w = np.array(f(rng, N, 128, 2048)).reshape(N, 8, 16, 4, 8, 16, 4)
    for i in still:
        w[:, :, i] = 0
        w[:, :, :, :, :, i] = 0
    return packedw(rng, w)
def setup_inputs(rng):
    return {**numbers_of(rng), "link": links(mixed(rng)), **weights(rng)}
def setup_inputs_ties(rng):
    d = numbers_of(rng)
    e = rng.permutation(N)
    x = d["x"].reshape(N, 8, 16, C, 4)
    for r in range(N):
        k = rng.permutation(C) % 3
        if r == e[0]: k = np.zeros(C, int)
        elif r in e[2::2]: k = rng.permutation(3)[np.arange(C) % 3]
        a = x[r][:, :8, :3].copy()
        a[:, :, 2] = 0
        x[r][:, :8] = a[:, :, k]
    x[e[1]] = 0
    u = d["u"].reshape(N, 8, 16, 128, 4)
    u[:, :, 8:, ::16] = 0
    u[:, :, 8:, 1::16] = 0
    t = mixed(rng)
    t[e[2]] = np.arange(C)
    t[e[3]] = t[e[3], :1].copy()
    return {"x": x.reshape(N, 128, 4 * C), "u": u.reshape(N, 128, 512), "v": d["v"], "link": links(t), **weights(rng, range(8))}
def setup_inputs_near(rng):
    d = numbers_of(rng)
    x = d["x"].astype(np.float32).reshape(N, 8, 16, C, 4)
    x[:, :, 0] = 0
    x[:, :, 8:] = 0
    u = d["u"].reshape(N, 128, 128, 4)
    u[:, :, ::16] = 0
    u[:, :, 1::16] = 0
    o = rng.permutation(N) % 4
    s = rng.integers(0, 256, (N, 8, C))
    for r in range(N):
        low = 2.0 ** -29 if o[r] == 3 else 2.0 ** -23
        for i in range(2): x[r, :, 8 + i] = ((s[r][:, :, None] >> (4 * i + np.arange(4))) & 1) * np.exp2(4.0 * i + np.arange(4)) * low
        x[r, :, 12, :, 0] = rng.integers(-1, 2, (8, C)) * (2.0 ** -29 if o[r] == 3 else 2.0 ** -20)
        if o[r] == 3: x[r, :, 13, :, 0] = x[r, :, 12, :, 0]
        if o[r] < 2:
            x[r, :, 0, :, 0] = rng.integers(0, 2, (8, C)) * 2.0 - 1.0
            x[r, :, 11, :, 0] = 2.0 ** -10
        if o[r] == 2:
            for g in range(8): x[r, g, 0, rng.permutation(C)[:2], 0] = np.array([1.0, -1.0])
        for g in rng.permutation(8)[:4]: x[r, g, 12, rng.integers(C), 0] = 2.0 ** 29 * rng.choice([-1.0, 1.0])
        k = 1.0 if o[r] == 0 else 2.0 ** -30
        for h in range(0, 128, 16):
            if o[r] < 2:
                u[r, h, h, 0] = k
                u[r, h + 11, h, 0] = k
            if o[r] == 2: u[r, h, h, 0] = 1.0
            u[r, h + 8, h] = k
            u[r, h + 9, h] = k
            u[r, h + 12, h + 1, 0] = 1.125 * 2.0 ** -30 if o[r] == 3 else 2.0 ** -30
            if o[r] == 3: u[r, h + 13, h + 1, 0] = -1.0 * 2.0 ** -30
    return {"x": x.reshape(N, 128, 4 * C).astype(BF), "u": u.reshape(N, 128, 512), "v": d["v"], "link": links(mixed(rng)), **weights(rng, [0, 8, 9, 10, 11, 12, 13, 14, 15])}
def setup_inputs_caps(rng):
    d = numbers_of(rng)
    x = np.zeros((N, 8, 16, C, 4))
    z = (N, 8, 8, C, 4)
    x[:, :, :8] = rng.choice([-1.0, 1.0], z) * (1.0 + (2 * rng.integers(0, 64, z) + 1) * 2.0 ** -7) * np.exp2(-1.0 * rng.integers(8, 15, z))
    x[:, :, 0, :, 0] = rng.choice([1.96875, 1.84375], (N, 8, C))
    s = mixed(rng)
    for i in range(3): x[:, :, 8 + i] = ((s[:, :, :, None] >> (4 * i + np.arange(4))) & 1) * np.exp2(4.0 * i + np.arange(4))
    side = rng.permutation(N) % 2 * 2 - 1
    q = np.argsort(-s * side[:, None, None], axis=2)[:, :, 1::2]
    one = rng.random((N, 8, C)) < 0.5
    a = rng.permutation(8)
    for i in range(6):
        g, t, k = a[i], i % R, 0
        for r in range(N):
            if (r >> t) & 1: one[r, g] = True
            else:
                n = K if i < 3 else K - 1 + 2 * (k % 2)
                k += 1
                one[r, g, q[r, g]] = rng.permutation(P) < n
    one[:, a[6]] = (((np.arange(N) >> (R - 1)) & 1) == 1)[:, None]
    one[:, a[7]] = ((np.arange(N) & 1) == 1)[:, None]
    x[:, :, 12, :, 0] = np.where(one, 1.0, -1.0 * rng.integers(0, 2, (N, 8, C)))
    u = d["u"].reshape(N, 128, 128, 4)
    u[:, :, ::16] = 0
    u[:, :, 1::16] = 0
    for r in range(N):
        for h in range(0, 128, 16):
            u[r, h + 8:h + 11, h] = float(side[r])
            u[r, h + 12, h + 1, 0] = 1.0
    return {"x": x.astype(np.float32).reshape(N, 128, 4 * C).astype(BF), "u": u.reshape(N, 128, 512), "v": d["v"], "link": links(mixed(rng)), **weights(rng, range(8, 16))}
def setup_inputs_huge(rng):
    d = numbers_of(rng)
    o = rng.permutation(N)
    c = rng.integers(0, 2, (N, 1, 1, C, 1)) * 2.0 - 1.0
    c[:, :, :, :2] = np.array([1.0, -1.0])[:, None]
    c[o == 1] = -1.0
    c[o == 2] = 1.0
    x = 0.6 + 0.09 * rng.random((N, 8, 16, C, 4))
    x[o == 0] = np.where(rng.random((1, 8, 16, C, 4)) < 0.125, 0.8125, 0.875)
    u = d["u"].reshape(N, 128, 128, 4)
    for i in range(2):
        a = 2.0 ** 29 * (1.0 - 0.1 * rng.random((N, 128, 8, 4)))
        a[o == 0] = 2.0 ** 30 * np.where(rng.random((1, 128, 8, 4)) < 0.03125, 0.875, 1.0)
        turned = (o % 2 == 1) if i else (o == 0) | (o > N // 2)
        for r in range(N):
            if turned[r]: a[r] *= (rng.permutation(8) % 2 * 2.0 - 1.0)[None, :, None]
        u[:, :, i::16] = a.astype(np.float32).astype(BF)
    w = np.zeros((N, 128, 4, 128, 4), np.float32)
    i = np.arange(128)
    for b in range(4): w[:, i, b, i, b] = 1
    return {"x": (2.0 ** 30 * x * c).astype(np.float32).reshape(N, 128, 4 * C).astype(BF), "u": u.reshape(N, 128, 512), "v": d["v"], "link": links(mixed(rng)), **packedw(rng, w.astype(BF))}
def setup_inputs_spread(rng):
    d = setup_inputs(rng)
    d["x"] = wide(rng, N, 128, 4 * C, cols=6)
    return d
def check_inputs(d):
    b = []
    for k in ("x", "u", "v"):
        a = np.abs(d[k].astype(np.float32))
        if not (np.isfinite(a).all() and ((a == 0) | (a >= 2.0 ** -30) & (a <= 2.0 ** 30)).all()): b.append("a value of " + k)
    none, least, most = [emit(mx_ref.quantize(np.full((128, 16), k, np.float32).astype(BF)))[1][0, 0] for k in (0.0, 2.0 ** -30, 2.0 ** 30)]
    for r in range(N):
        if (np.sort(gentries(d["link"][r]), axis=1) != np.arange(C)).any(): b.append("link: a group's entries are no permutation")
        if ((d["wc"][r] == 0x7F) | (d["wc"][r] == 0xFF)).any(): b.append("wc: a code that is no number")
        s = mx_ref.live(d["ws"][r])
        if ((s != none) & ((s < least) | (s > most))).any(): b.append("ws: a scale out of range")
    return b
def at(a, e):
    return np.take_along_axis(a, e, axis=1)
def reference(x, u, v, link, wc, ws):
    qu = [mx_ref.quantize(u[r]) for r in range(N)]
    lay = [pk(wc[r], ws[r]) for r in range(N)]
    now = [x[r] for r in range(N)]
    to = [gentries(link[r]) for r in range(N)]
    for t in range(R):
        d = 2 ** t
        own, order, bit = [], [], []
        for r in range(N):
            q = mx_ref.quantize(now[r])
            own.append(decode(q))
            s = mx_ref.matmul(qu[r], q)
            order.append(np.argsort(-(s[::16] + np.float32(0.0)), axis=1, kind="stable"))
            bit.append(s[1::16] > 0)
        kept, names, left, places, turned = [], [], [], [], []
        for r in range(N):
            k, q = order[r][:, 0::2], order[r][:, 1::2]
            there = at(to[r], q)
            fails = at(bit[r], q) != at(bit[(r + d) % N], there)
            j = np.argsort(fails.astype(np.int64), axis=1, kind="stable")
            k, q, there = at(k, j), at(q, j), at(there, j)
            h = own[r].astype(BF)
            a = ((gcols(h, k).astype(np.float32) + gcols(h, q).astype(np.float32)) * np.float32(0.5)).astype(BF)
            kept.append(mx_ref.quantize(np.ascontiguousarray(a[:, :4 * K])))
            left.append(mx_ref.quantize(np.ascontiguousarray(a[:, 4 * K:])))
            names.append(there[:, :K])
            places.append(q[:, K:])
            m = np.tile(np.arange(C), (8, 1))
            np.put_along_axis(m, k[:, K:], q[:, K:], axis=1)
            np.put_along_axis(m, q[:, K:], k[:, K:], axis=1)
            turned.append(at(to[r], m))
        to = [at(turned[(r + d) % N], to[r]) for r in range(N)]
        for r in range(N):
            c = (r - d) % N
            slots = join(kept[c], left[r])
            e = np.full((8, C), P)
            np.put_along_axis(e, places[r], np.tile(np.arange(K, P), (8, 1)), axis=1)
            np.put_along_axis(e, names[c], np.tile(np.arange(K), (8, 1)), axis=1)
            made = []
            for b in range(4):
                h = mx_ref.matmul(pick(lay[r], np.arange(128 * b, 128 * b + 128)), slots)
                h = np.concatenate([h, np.zeros((128, 1), np.float32)], axis=1)
                made.append(gpick(h, e) * np.float32(0.03125) + own[r][:, b::4])
            now[r] = tile(made)
    y, lk = np.zeros((N, 128, C), np.float32), np.zeros((N, 8, C), np.float32)
    oc, osc = np.zeros((N, 128, 4 * C), np.uint8), np.zeros((N, 16, C), np.uint8)
    for r in range(N):
        q = mx_ref.quantize(now[r])
        y[r] = mx_ref.matmul(mx_ref.quantize(v[r]), q)
        lk[r] = to[r]
        oc[r], osc[r] = emit(q)
    return {"y": y, "lk": lk, "oc": oc, "osc": osc}

@@ -1,0 +1,399 @@
+from concourse.mybir import dt, AluOpType as OP, ActivationFunctionType as AF
+
+N, ROUNDS = 4, 2
+HW = 264
+BIG = 2.0 ** 16
+TC = [max(128, 64 * (k + 1)) for k in range(8)]
+TO = [sum(TC[:k]) for k in range(9)]
+CODES, F32, BF = "float8_e4m3fn_x4", "float32", "bfloat16"
+
+SCRATCH = {}
+
+
+def buf(names, cols, dtype, where="sbuf"):
+    for n in names.split(): SCRATCH[n] = (where, [128, cols], dtype)
+
+
+buf("X0 XN0 XN1 EB FH FB", 2048, BF)
+buf("UB VB ON OB BS BR0 BR1 TB0 TB1 AK0 AK1 AL0 AL1", 512, BF)
+buf("UQ UR UT VQ OQ AKQ0 AKQ1 ALQ0 ALQ1 INQ0 INQ1", 128, CODES)
+buf("UQS URS UTS VQS OQS AKS0 AKS1 ALS0 ALS1 INS0 INS1", 128, "uint8")
+buf("WQ EQ", 512, CODES)
+buf("WS EQS", 512, "uint8")
+buf("XQ", 512 * 3, CODES)
+buf("XS", 512 * 3, "uint8")
+buf("QT", TO[8], CODES)
+buf("QS", TO[8], "uint8")
+buf("BT", 4 * TO[8], BF)
+buf("JUNK", 7936, BF)
+buf("KB", 1024, BF)
+buf("LINKI", 32, "int32")
+buf("CA", 2608, F32)
+buf("CT", 560, F32)
+buf("CB", 1280, F32)
+buf("SM", 16, F32)
+buf("INT", 20, "int32")
+buf("UO", 16, "uint16")
+buf("W3", 1568, F32)
+buf("RS", 32, F32)
+buf("WK", 160, F32)
+buf("EX", 2944, F32)
+buf("II", 48, "int32")
+buf("U16", 80, "uint16")
+buf("OWS PAY POS POSA FO EW YS LKO LR0 LR1 TR0 TR1 TRW0 TRW1", 512, F32)
+buf("FF", 1024, F32)
+buf("NMR", 128, F32)
+buf("LQK0 LQK1", 256, F32)
+buf("HS", 4 * HW, F32)
+buf("KQ0 KQ1 LL0 LL1", 32, "uint16")
+buf("NL0 NL1 NLI0 NLI1", 8, "uint16")
+buf("TRD0 TRD1 TRX0 TRX1", 32, F32, "dram")
+buf("BRD0 BRD1 BRX0 BRX1", 32, BF, "dram")
+buf("P0 P1 P2 P3 P4 P5 P6 P7", 512, F32, "psum")
+
+PIECE = {
+    "AROW": ("CA", 0, 512), "M1": ("CA", 512, 512), "MX": ("CA", 1024, 512), "CR": ("CA", 1536, 512), "CN": ("CA", 2048, 528),
+    "CX": ("CT", 0, 512), "R5": ("CT", 512, 32), "J16": ("CT", 544, 16),
+    "IOTA": ("CB", 0, 512), "I1": ("CB", 512, 512), "ONEF": ("CB", 1024, 256),
+    "PM": ("SM", 0, 2), "NPM": ("SM", 2, 1), "PMH": ("SM", 3, 1), "MC": ("SM", 4, 1),
+    "UOI": ("INT", 0, 16), "PI": ("INT", 16, 2), "PJ": ("INT", 18, 2),
+    "MSK": ("W3", 0, 528), "SCN": ("W3", 528, 528), "SBD": ("W3", 1056, 512),
+    "RSI": ("WK", 0, 32), "RK": ("WK", 32, 32), "NX1": ("WK", 64, 16), "NX2": ("WK", 80, 16), "NN": ("WK", 96, 16), "TOT": ("WK", 112, 1), "RSJ": ("WK", 128, 32),
+    "EXA": ("EX", 0, 512), "EXB": ("EX", 512, 256), "EXK": ("EX", 768, 512), "EXN": ("EX", 1280, 128), "EXE": ("EX", 1408, 512), "EXL": ("EX", 1920, 512), "DS": ("EX", 2432, 512),
+    "CSL": ("II", 0, 32), "VL": ("II", 32, 16),
+    "RKU": ("U16", 0, 32), "NU": ("U16", 32, 16), "EL": ("U16", 48, 32),
+    "FR": ("FF", 0, 256), "F5": ("FF", 256, 256), "FC": ("FF", 512, 256), "VP": ("FF", 768, 256),
+}
+SEMAPHORES = ["cv", "cs", "ct", "cg", "ldx0", "ldx1", "ldu", "ldk", "ldv", "ldw", "ldc", "st"]
+for _t in range(ROUNDS):
+    SEMAPHORES += [s + "%d" % _t for s in ("bro", "bra", "brl", "tbx", "nma", "nml", "cda", "cdl", "tro", "tra", "trl", "trx")]
+
+
+def rank_program(g, core, T, topo):
+    rank = T.rank_of(core)
+    if rank is None:
+        return
+    queue = {"v": g.vector, "s": g.scalar, "t": g.tensor, "g": g, "y": g.sync}
+    own = {"v": "cv", "s": "cs", "t": "ct", "g": "cg"}
+    count = {"cv": 0, "cs": 0, "ct": 0, "cg": 0}
+    total = {}
+    know = {q: {} for q in queue}
+    wrote, read = {}, {}
+
+    def w(n, a=0, b=None, step=1):
+        if n in PIECE: name, off, width = PIECE[n]
+        else: name, off, width = n, 0, SCRATCH[n][1][1]
+        if b is None: b = width
+        if step == 1: return T[name][:, off + a:off + b]
+        return T[name][:, off + a:off + b:step]
+
+    def settle(q, reads, writes):
+        need = []
+        for k in reads:
+            if k in wrote: need.append(wrote[k])
+            if k[0] == "P" and k[1:].isdigit():
+                need += [r for r in read.get(k, []) if r[0] != q]
+        for k in writes:
+            if k in wrote: need.append(wrote[k])
+            need += [r for r in read.get(k, []) if r[0] != q or r[1] not in count]
+        need.sort(key=lambda n: -n[2])
+        for _, sem, val, seen in need:
+            if know[q].get(sem, 0) >= val: continue
+            queue[q].wait_ge(T.sem[sem], val)
+            know[q][sem] = val
+            for s2 in seen: know[q][s2] = max(know[q].get(s2, 0), seen[s2])
+
+    def note(token, reads, writes):
+        for k in reads: read.setdefault(k, []).append(token)
+        for k in writes:
+            wrote[k] = token
+            read[k] = []
+
+    def op(q, call, reads, writes):
+        settle(q, reads, writes)
+        sem = own[q]
+        call().then_inc(T.sem[sem], 1)
+        count[sem] += 1
+        total[sem] = count[sem]
+        note((q, sem, count[sem], dict(know[q])), reads, writes)
+
+    def dma(q, out, in_, sem, of, reads, writes):
+        settle(q, reads, writes)
+        queue[q].dma_start(out, in_).then_inc(T.sem[sem], 16)
+        total[sem] = 16 * of
+        note((q, sem, 16 * of, dict(know[q])), reads, writes)
+
+    def send(dst, out, in_, rsem, lsem, reads, of=1):
+        settle("g", reads, [])
+        rid, pid = topo.addr(dst)[:2]
+        n = len(topo.engines(core, dst))
+        g.remote_dma(out, in_, T.sem[rsem], T.sem[lsem], pid, rid, topo.mask(core, dst))
+        total[lsem] = n * of
+        note(("g", lsem, n * of, dict(know["g"])), reads, [])
+
+    def lands(src, key, rsem, of=1):
+        n = len(topo.engines(src, core)) * of
+        total[rsem] = n
+        note(("far", rsem, n, {}), [], [key])
+
+    V, S, G = g.vector, g.scalar, g
+
+    def ts(out, in0, a, b, op0, op1, reads, writes):
+        if op1 is None: op("v", lambda: V.tensor_scalar(out, in0, a, None, op0), reads, writes)
+        else: op("v", lambda: V.tensor_scalar(out, in0, a, b, op0, op1), reads, writes)
+
+    def tt(out, in0, in1, o, reads, writes): op("v", lambda: V.tensor_tensor(out, in0, in1, o), reads, writes)
+    def cp(out, in_, reads, writes): op("v", lambda: V.tensor_copy(out, in_), reads, writes)
+    def fill(out, c, writes): op("v", lambda: V.memset(out, c), [], writes)
+    def act(out, in_, func, scale, reads, writes): op("s", lambda: S.activation(out, in_, func, scale=scale), reads, writes)
+    def actb(out, in_, func, bias, scale, reads, writes): op("s", lambda: S.activation(out, in_, func, bias=bias, scale=scale), reads, writes)
+    def scan(out, d0, d1, reads, writes): op("v", lambda: V.tensor_tensor_scan(out, d0, d1, 0.0, OP.mult, OP.add), reads, writes)
+    def quant(q, s, in_, reads, writes): op("v", lambda: V.quantize_mx(q, s, in_), reads, writes)
+    def mm(out, a, asc, b, bsc, start, stop, reads, writes): op("t", lambda: g.tensor.matmul_mx(out, a, asc, b, bsc, start, stop), reads, writes)
+    def iota(out, pattern, base, cm, keys): op("g", lambda: G.iota(out, pattern, base, cm, allow_small_or_imprecise_dtypes=True), [], keys)
+    def iotai(out, pattern, base, cm, keys): op("g", lambda: G.iota(out, pattern, base, cm), [], keys)
+    def select(out, in_, pattern, cmp, c, base, cm, reads, writes): op("g", lambda: G.affine_select(out, in_, pattern, cmp, c, base, cm), reads, writes)
+
+    CXK = ["CT0"] + ["CX%d" % i for i in range(1, 8)]
+
+    def lift(ex, a, row, n, key):
+        scan(w(ex, a, a + n), w("CX", 0, n), row, CXK + [key], ["%s.%d" % (ex, a)])
+
+    def down(out, ex, a, n, less, key):
+        ts(out, w(ex, a + 15, a + n, 16), w("MC"), less, OP.mult, OP.add if less else None, ["%s.%d" % (ex, a), "MC"], [key])
+
+    dma("s", w("UB"), T.u[:, :], "ldu", 1, [], ["UB"])
+    dma("y", w("X0", 0, 1024), T.x[:, 0:1024], "ldx0", 1, [], ["X0a"])
+    dma("s", w("X0", 1024, 2048), T.x[:, 1024:2048], "ldx1", 1, [], ["X0b"])
+    dma("y", w("LINKI"), T.link[:, :], "ldk", 1, [], ["LINKI"])
+    dma("y", w("WQ").bitcast(dt.uint8), T.wc[:, :], "ldw", 2, [], ["WQ"])
+    dma("y", w("WS"), T.ws[:, :], "ldw", 2, [], ["WS"])
+    dma("y", w("VB"), T.v[:, :], "ldv", 1, [], ["VB"])
+
+    iotai(w("PI"), [[0, 2]], 0, 1, ["PI"])
+    iota(w("AROW"), [[0, 32], [1, 16]], 0, 0, ["AROW"])
+    iotai(w("UOI"), [[1, 2], [16, 8]], 0, 0, ["UOI"])
+    ts(w("PJ"), w("PI"), 15, None, OP.bitwise_and, None, ["PI"], ["PJ"])
+    fill(w("ON"), 1.0, ["ON"])
+    cp(w("PM"), w("PJ"), ["PJ"], ["PM"])
+    pm = w("PM", 0, 1)
+    fill(w("MSK", 512, 528), 0.0, ["MSKp"])
+    fill(w("CN", 512, 528), 1.0, ["CNp"])
+    ts(w("NPM"), pm, -1.0, None, OP.mult, None, ["PM"], ["NPM"])
+    ts(w("PMH"), pm, 0.5, None, OP.subtract, None, ["PM"], ["PMH"])
+    for k in range(7, -1, -1):
+        fill(w("BT", 4 * TO[k] + 256 * k, 4 * TO[k + 1]), 0.0, ["BT%d.%d" % (k, s) for s in range(4)] + ["BT%dd" % k])
+    fill(w("RS", 0, 1), 0.0, ["RS0"])
+    cp(w("UO"), w("UOI"), ["UOI"], ["UO"])
+    actb(w("CN", 0, 512), w("AROW"), AF.Abs, w("NPM"), 1.0, ["AROW", "NPM"], ["CN"])
+    actb(w("M1"), w("CN", 0, 512), AF.Relu, 1.0, -1.0, ["CN"], ["M1"])
+    actb(w("MX"), w("AROW"), AF.Sign, w("PMH"), -1.0, ["AROW", "PMH"], ["MX"])
+    actb(w("CN", 0, 512), w("M1"), AF.Copy, 1.0, -1.0, ["M1"], ["CN"])
+    act(w("MX"), w("MX"), AF.Copy, 1e25, ["MX"], ["MX"])
+    act(w("CR"), w("AROW"), AF.Sign, 1.0, ["AROW"], ["CR"])
+    select(w("OB"), w("ON"), [[-16, 8], [0, 64]], OP.is_ge, 0.0, 0, 1, ["ON"], ["OB"])
+    select(w("OB"), w("OB"), [[16, 8], [0, 64]], OP.is_ge, 0.0, 15, -1, ["OB"], ["OB"])
+    for b in range(4): select(w("EB", 512 * b, 512 * b + 512), w("ON"), [[-4, 128], [-1, 4]], OP.is_equal, 0.0, b, 4, ["ON"], ["EB%d" % b])
+    iota(w("IOTA"), [[1, 512]], 0, 0, ["IOTA"])
+    quant(w("UQ"), w("UQS"), w("UB"), ["UB"], ["UQ"])
+
+    def pick_u(q, o):
+        cp(w(q).bitcast(dt.uint32), w("UQ").bitcast(dt.uint32).indirect(w("UO", o, o + 8)), ["UQ", "UO"], [q])
+        cp(w(q + "S"), w("UQS").indirect(w("UO", o, o + 8)), ["UQ", "UO"], [q + "S"])
+
+    def later_constants():
+        iota(T.CT[0:16, 0:512], [[0, 512]], 1, 0, ["CTx"])
+        select(T.CT[0:16, 0:512], T.CT[0:16, 0:512], [[0, 32], [1, 16]], OP.is_gt, 0.0, 0, -1, ["CTx"], ["CTx"])
+        select(T.CT[0:16, 0:512], T.CT[0:16, 0:512], [[0, 32], [1, 16]], OP.not_equal, BIG, -1, -1, ["CTx"], ["CTx"])
+        iota(T.CT[0:16, 512:544], [[-16, 32]], 511, -1, ["CTy"])
+        iota(T.CT[0:16, 544:560], [[16, 16]], 0, 1, ["CTz", "CT0"])
+        for i in range(1, 8): dma("y", T.CT[16 * i:16 * i + 16, :], T.CT[0:16, :], "ldc", 7, ["CTx", "CTy", "CTz"], ["CX%d" % i])
+        iota(w("I1"), [[1, 512]], 1, 0, ["I1"])
+        iota(w("ONEF"), [[0, 256]], 1, 0, ["ONEF"])
+        for b in range(4): iota(w("HS", HW * b + 256, HW * b + HW), [[0, 8]], 0, 0, ["HSZ%d" % b])
+        iota(w("TRW1"), [[0, 512]], 0, 0, ["TRW1"])
+
+    def turn_rows(t):
+        n, lr = "LQK%d" % t, "LR%d" % t
+        act(w(n, 0, 128), w(lr).indirect(w("KQ%d" % t, 24, 32)), AF.Copy, 1.0, [lr, "QL%d" % t], [n + "a"])
+        act(w(n, 128, 256), w(lr).indirect(w("KQ%d" % t, 16, 24)), AF.Copy, 1.0, [lr, "KL%d" % t], [n + "b"])
+
+    def turn_send(t, back):
+        n, tr = "LQK%d" % t, "TR%d" % t
+        cp(w(tr).indirect(w("KQ%d" % t, 16, 32)), w(n), [n + "a", n + "b", "QL%d" % t, "KL%d" % t], [tr])
+        dma("y", w("TRD%d" % t), T[tr][0:128:16, :], "tro%d" % t, 1, [tr], ["TRD%d" % t])
+        send(back, w("TRX%d" % t), w("TRD%d" % t), "tra%d" % t, "trl%d" % t, ["TRD%d" % t])
+
+    def spread(n, src, sem):
+        for a in range(16): dma("y", T[n][a:128:16, :], w(src), sem, 16, [src], ["%s.%d" % (n, a)])
+
+    for t in range(ROUNDS):
+        d = 2 ** t
+        nxt, prv = T.cores[(rank + d) % N], T.cores[(rank - d) % N]
+        last = t == ROUNDS - 1
+        X, xk = ("X0", ["X0a", "X0b"]) if t == 0 else ("XN%d" % (t - 1), ["XN%d.%d" % (t - 1, b) for b in range(4)])
+        xq, xs = w("XQ", 512 * t, 512 * t + 512), w("XS", 512 * t, 512 * t + 512)
+        kx = "XQ%d" % t
+        ll, lr, kq, br, tb = ("%s%d" % (n, t) for n in ("LL", "LR", "KQ", "BR", "TB"))
+        if t == 0: pick_u("UR", 0)
+        quant(xq, xs, w(X), xk, [kx])
+        if t == 0: pick_u("UT", 8)
+        mm(w("P0"), w("UR"), w("URS"), xq, xs, True, True, ["UR", "URS", kx], ["P0"])
+        mm(w("P1"), w("UT"), w("UTS"), xq, xs, True, True, ["UT", "UTS", kx], ["P1"])
+        if t: turn_send(t - 1, T.cores[(rank - d // 2) % N])
+        act(w("BS"), w("P1"), AF.Sign, 1.0, ["P1"], ["BS"])
+        actb(w(br), w("BS"), AF.Sign, -0.5, 1.0, ["BS"], [br])
+        tt(w("MSK", 0, 512), w("P0"), w("M1"), OP.mult, ["P0", "M1"], ["MSK"])
+        tt(w("SBD"), w("P0"), w("MX"), OP.min, ["P0", "MX"], ["SBD"])
+        scan(w("SCN"), w("CN"), w("MSK"), ["CN", "CNp", "MSK", "MSKp"], ["SCN"])
+        dma("y", w("BRD%d" % t), T[br][0:128:16, :], "bro%d" % t, 1, [br], ["BRD%d" % t])
+        send(prv, w("BRX%d" % t), w("BRD%d" % t), "bra%d" % t, "brl%d" % t, ["BRD%d" % t])
+        if t:
+            p = t - 1
+            lands(T.cores[(rank + d // 2) % N], "TRX%d" % p, "tra%d" % p)
+            spread("TRW%d" % p, "TRX%d" % p, "trx%d" % p)
+        lands(nxt, "BRX%d" % t, "bra%d" % t)
+        spread(tb, "BRX%d" % t, "tbx%d" % t)
+        if t == 0: later_constants()
+        iota(w("EW"), [[0, 512]], 256, 0, ["EW"])
+
+        def colsum(k):
+            q, s = w("QT", TO[k], TO[k + 1]), w("QS", TO[k], TO[k + 1])
+            quant(q, s, w("BT", 4 * TO[k], 4 * TO[k + 1]), ["BT%d.%d" % (k, i) for i in range(4)] + ["BT%dd" % k], ["QT%d" % k])
+            mm(w("P6", 0, TC[k]), w("OQ"), w("OQS"), q, s, k == 7, k == 0, ["OQ", "QT%d" % k], ["P6"])
+
+        for k in range(7, -1, -1):
+            o = 4 * TO[k]
+            for i in range(3, -1, -1):
+                c = 4 * k + i
+                key = "BT%d.%d" % (k, i)
+                sc = w("SCN", 16 * c + 15, 16 * c + 16)
+                if c:
+                    ts(w("BT", o + i, o + 64 * c, 4), w("P0", 0, 16 * c), sc, None, OP.is_ge, None, ["P0", "SCN"], [key])
+                    j = 8 * c * (c - 1)
+                    op("s", lambda: S.activation(w("JUNK", j, j + 16 * c), w("BT", o + i, o + 64 * c, 4), AF.Copy, accum_out=w("RS", c, c + 1)), [key], ["JUNK%d" % c, "RS%d" % c])
+                if i == 3:
+                    tt(w("BT", o + 256 * k, o + 256 * k + 256, 4), w("SBD", 64 * k, 64 * k + 64), w("SCN", 64 * k + 16, 64 * k + 80), OP.is_ge, ["SBD", "SCN"], ["BT%dd" % k])
+                    if k < 7: colsum(k + 1)
+                if i == 1: scan(w("DS", 64 * k, 64 * k + 64), w("CR", 64 * k, 64 * k + 64), w("BT", o + 256 * k, o + 256 * k + 256, 4), ["CR", "BT%dd" % k], ["DS%d" % k])
+            if k == 7 and t == 0:
+                quant(w("OQ"), w("OQS"), w("OB"), ["OB"], ["OQ"])
+                cp(w("LL0"), w("LINKI"), ["LINKI"], ["LL0"])
+            if k == 6 and t == 0:
+                quant(w("EQ"), w("EQS"), w("EB"), ["EB%d" % b for b in range(4)], ["EQ"])
+                ts(w("MC"), pm, 15.0, 1.0 - 1.0 / BIG, OP.is_equal, OP.mult, ["PM"], ["MC"])
+            if k == 7 and t or k == 6 and not t:
+                for b in range(4):
+                    mm(w("P%d" % (2 + b)), w("EQ", 128 * b, 128 * b + 128), w("EQS", 128 * b, 128 * b + 128), xq, xs, True, True, ["EQ", kx], ["P%d" % (2 + b)])
+            if k == 5:
+                if t == 0: ts(w("MC"), w("MC"), 1.0 / BIG, None, OP.add, None, ["MC"], ["MC"])
+                if t == 0: act(w(lr), w("IOTA").indirect(w(ll)), AF.Copy, 1.0, ["IOTA", ll], [lr])
+            if k == 3:
+                if t: act(w(lr), w("TRW%d" % (t - 1)).indirect(w("LL%d" % (t - 1))), AF.Copy, 1.0, ["TRW%d.%d" % (t - 1, a) for a in range(16)] + ["LL%d" % (t - 1)], [lr])
+                tt(w("OWS"), w(br), w("I1"), OP.mult, [br, "I1"], ["OWS"])
+            if k == 1 and t: lift("EXL", 0, w(lr), 512, lr)
+        if t: down(w(ll), "EXL", 0, 512, None, ll)
+        else: quant(w("VQ"), w("VQS"), w("VB"), ["VB"], ["VQ"])
+        colsum(0)
+        for b in range(4): act(w("FH", 512 * b, 512 * b + 512), w("P%d" % (2 + b)), AF.Copy, 0.5, ["P%d" % (2 + b)], ["FH%d" % b])
+        act(w("TR%d" % t), w(lr), AF.Copy, 1.0, [lr], ["TR%d" % t])
+        tt(w("RSJ"), w("DS", 15, 512, 16), w("R5"), OP.add, ["DS%d" % c for c in range(8)] + CXK, ["RSJ"])
+        tt(w("PAY"), w(tb).indirect(w(ll)), w("OWS"), OP.mult, ["%s.%d" % (tb, a) for a in range(16)] + [ll, "OWS"], ["PAY"])
+        lift("EXA", 0, w("P6"), 512, "P6")
+        tt(w("RSI"), w("RS"), w("RSJ"), OP.add, ["RS%d" % c for c in range(32)] + ["RSJ"], ["RSI"])
+        down(w("CSL"), "EXA", 0, 512, None, "CSL")
+        tt(w("RK"), w("RSI"), w("CSL"), OP.subtract, ["RSI", "CSL"], ["RK"])
+        cp(w("RKU"), w("RK"), ["RK"], ["RKU"])
+        cp(w("POS").indirect(w("RKU")), w("PAY"), ["RKU", "PAY"], ["POS"])
+        act(w("POSA"), w("POS"), AF.Abs, 1.0, ["POS"], ["POSA"])
+        ts(w("FR"), w("POS", 1, 512, 2), 0.0, None, OP.is_lt, None, ["POS"], ["FR"])
+        ts(w("F5"), w("POS", 1, 512, 2), 0.0, 512.0, OP.is_lt, OP.mult, ["POS"], ["F5"])
+        scan(w("FC"), w("ONEF"), w("FR"), ["ONEF", "FR"], ["FC"])
+        tt(w("VP"), w("FC"), w("F5"), OP.add, ["FC", "F5"], ["VP"])
+        ts(w("TOT"), w("FC", 255, 256), -1.0, -257.0, OP.mult, OP.add, ["FC"], ["TOT"])
+        lift("EXB", 0, w("VP"), 256, "VP")
+        down(w("VL"), "EXB", 0, 256, None, "VL")
+        tt(w("NX1"), w("J16"), w("VL"), OP.subtract, CXK + ["VL"], ["NX1"])
+        ts(w("NX2"), w("VL"), w("TOT"), None, OP.add, None, ["VL", "TOT"], ["NX2"])
+        tt(w("NN"), w("NX1"), w("NX2"), OP.max, ["NX1", "NX2"], ["NN"])
+        cp(w("NU"), w("NN"), ["NN"], ["NU"])
+        cp(w("FO", 0, 256).indirect(w("NU")), w("POSA", 0, 512, 2), ["NU", "POSA"], ["FOk"])
+        cp(w("FO", 256, 512).indirect(w("NU")), w("POSA", 1, 512, 2), ["NU", "POSA"], ["FOq"])
+        for b in range(4): act(w("FB", 512 * b, 512 * b + 512), w("P%d" % (2 + b)), AF.Copy, 1.0, ["P%d" % (2 + b)], ["FB%d" % b])
+
+        def lists(h):
+            o = 128 if h == "L" else 0
+            lift("EXK", o, w("FO", o, o + 128), 128, "FOk")
+            lift("EXK", o + 256, w("FO", o + 256, o + 384), 128, "FOq")
+            down(w(kq, o // 8, o // 8 + 8), "EXK", o, 128, -1.0, "K%s%d" % (h, t))
+            down(w(kq, o // 8 + 8, o // 8 + 16), "EXK", o + 256, 128, -1.0, "Q%s%d" % (h, t))
+
+        def firsts(h):
+            o, i = (16, 512) if h == "L" else (0, 0)
+            for b in range(4):
+                act(w("KB", i + 128 * b, i + 128 * b + 128), w("FH", 512 * b, 512 * b + 512).indirect(w(kq, o, o + 8)), AF.Copy, 1.0, ["FH%d" % b, "K%s%d" % (h, t)], ["KB%s%d" % (h, b)])
+
+        def second(h, b):
+            o, i = (24, 512) if h == "L" else (8, 0)
+            tt(w("A%s%d" % (h, t), b, 512, 4), w("FH", 512 * b, 512 * b + 512).indirect(w(kq, o, o + 8)), w("KB", i + 128 * b, i + 128 * b + 128), OP.add, ["FH%d" % b, "Q%s%d" % (h, t), "KB%s%d" % (h, b)], ["A%s%d.%d" % (h, t, b)])
+
+        def pack(h):
+            quant(w("A%sQ%d" % (h, t)), w("A%sS%d" % (h, t)), w("A%s%d" % (h, t)), ["A%s%d.%d" % (h, t, b) for b in range(4)], ["A%sQ%d" % (h, t)])
+
+        lists("K")
+        firsts("K")
+        cp(w("NMR"), w(lr).indirect(w(kq, 8, 16)), [lr, "QK%d" % t], ["NMR"])
+        second("K", 0)
+        lift("EXN", 0, w("NMR"), 128, "NMR")
+        second("K", 1)
+        down(w("NL%d" % t), "EXN", 0, 128, None, "NL%d" % t)
+        second("K", 2)
+        second("K", 3)
+        pack("K")
+        send(nxt, w("NLI%d" % t), w("NL%d" % t), "nma%d" % t, "nml%d" % t, ["NL%d" % t])
+        send(nxt, w("INQ%d" % t).bitcast(dt.uint8), w("AKQ%d" % t).bitcast(dt.uint8), "cda%d" % t, "cdl%d" % t, ["AKQ%d" % t], 2)
+        send(nxt, w("INS%d" % t), w("AKS%d" % t), "cda%d" % t, "cdl%d" % t, ["AKQ%d" % t], 2)
+        lists("L")
+        if last: turn_rows(t)
+        firsts("L")
+        if last: turn_send(t, prv)
+        for b in range(4): second("L", b)
+        pack("L")
+        lands(prv, "NLI%d" % t, "nma%d" % t)
+        lands(prv, "INQ%d" % t, "cda%d" % t, 2)
+
+        def layer(b, P, q, s, key, o, h):
+            mm(w(P, 0, 128), w("WQ", 128 * b, 128 * b + 128), w("WS", 128 * b, 128 * b + 128), w(q), w(s), True, True, ["WQ", "WS", key], [P])
+            act(w("HS", HW * b + o, HW * b + o + 128), w(P, 0, 128), AF.Copy, 0.03125, [P], ["HS%d%s" % (b, h)])
+
+        for b in range(4): layer(b, "P%d" % (0, 1, 6, 7)[b], "ALQ%d" % t, "ALS%d" % t, "ALQ%d" % t, 128, "L")
+        cp(w("EW").indirect(w(kq, 24, 32)), w("IOTA", 128, 256), ["QL%d" % t, "IOTA"], ["EW"])
+        cp(w("EW").indirect(w("NLI%d" % t)), w("IOTA", 0, 128), ["NLI%d" % t, "IOTA"], ["EW"])
+        lift("EXE", 0, w("EW"), 512, "EW")
+        down(w("EL"), "EXE", 0, 512, None, "EL")
+        for b in range(4): layer(b, "P%d" % (2 + b), "INQ%d" % t, "INS%d" % t, "INQ%d" % t, 0, "K")
+        for b in range(4):
+            tt(w("XN%d" % t, b, 2048, 4), w("HS", HW * b, HW * b + HW).indirect(w("EL")), w("FB", 512 * b, 512 * b + 512), OP.add, ["HS%dK" % b, "HS%dL" % b, "HSZ%d" % b, "EL", "FB%d" % b], ["XN%d.%d" % (t, b)])
+        if not last: turn_rows(t)
+
+    t = ROUNDS - 1
+    lands(T.cores[(rank + 2 ** t) % N], "TRX%d" % t, "tra%d" % t)
+    dma("y", T["TRW%d" % t][0:128:16, :], w("TRX%d" % t), "trx%d" % t, 1, ["TRX%d" % t], ["TRW%d" % t])
+    stores, e = 13, 512 * ROUNDS
+    for h in range(2):
+        o = e + 256 * h
+        quant(w("XQ", o, o + 256), w("XS", o, o + 256), w("XN%d" % t, 1024 * h, 1024 * h + 1024), ["XN%d.%d" % (t, b) for b in range(4)], ["XQe%d" % h])
+        mm(w("P%d" % (6 + h), 0, 256), w("VQ"), w("VQS"), w("XQ", o, o + 256), w("XS", o, o + 256), True, True, ["VQ", "XQe%d" % h], ["P%d" % (6 + h)])
+        dma("y", T.oc[:, 1024 * h:1024 * h + 1024], w("XQ", o, o + 256).bitcast(dt.uint8), "st", stores, ["XQe%d" % h], ["oc%d" % h])
+    act(w("YS", 0, 256), w("P6", 0, 256), AF.Copy, 1.0, ["P6"], ["YSa"])
+    cp(w("YS", 256, 512), w("P7", 0, 256), ["P7"], ["YSb"])
+    dma("s", T.y[:, 0:256], w("YS", 0, 256), "st", stores, ["YSa"], ["ya"])
+    dma("y", T.y[:, 256:512], w("YS", 256, 512), "st", stores, ["YSb"], ["yb"])
+    act(w("LKO"), w("TRW%d" % t).indirect(w("LL%d" % t)), AF.Copy, 1.0, ["TRW%d" % t, "LL%d" % t], ["LKO"])
+    dma("s", T.lk[:, :], T.LKO[0:128:16, :], "st", stores, ["LKO"], ["lk"])
+    for k in range(4):
+        for h in range(2):
+            o = e + 256 * h
+            dma("y", T.osc[4 * k:4 * k + 4, 256 * h:256 * h + 256], T.XS[32 * k:32 * k + 4, o:o + 256], "st", stores, ["XQe%d" % h], ["osc%d%d" % (k, h)])
+    for sem in total:
+        if know["g"].get(sem, 0) < total[sem]: g.wait_ge(T.sem[sem], total[sem])

@@ -1,11 +1,17 @@
+import numpy as np
 from concourse.mybir import dt, AluOpType as OP, ActivationFunctionType as AF
 
 N, ROUNDS = 4, 2
 HW = 264
-BIG = 2.0 ** 16
+BIG = 2.0 ** 26
+FAR = 1e25
+C0 = 23
+JL = 8 * C0
+NS = (3, 2)
+AT7, AT6 = 16, 4
 TC = [max(128, 64 * (k + 1)) for k in range(8)]
 TO = [sum(TC[:k]) for k in range(9)]
-CODES, F32, BF = "float8_e4m3fn_x4", "float32", "bfloat16"
+CODES, F32, BF, F16 = "float8_e4m3fn_x4", "float32", "bfloat16", "float16"
 
 SCRATCH = {}
 
@@ -14,8 +20,9 @@ def buf(names, cols, dtype, where="sbuf"):
     for n in names.split(): SCRATCH[n] = (where, [128, cols], dtype)
 
 
-buf("X0 XN0 XN1 EB FH FB", 2048, BF)
-buf("UB VB ON OB BS BR0 BR1 TB0 TB1 AK0 AK1 AL0 AL1", 512, BF)
+buf("X0 XN0 XN1 EB FH", 2048, BF)
+buf("FB", 1024, BF)
+buf("UB VB ON OB AROW KM RZ RD0 BR0 BR1 TB0 TB1 AK0 AK1 AL0 AL1", 512, BF)
 buf("UQ UR UT VQ OQ AKQ0 AKQ1 ALQ0 ALQ1 INQ0 INQ1", 128, CODES)
 buf("UQS URS UTS VQS OQS AKS0 AKS1 ALS0 ALS1 INS0 INS1", 128, "uint8")
 buf("WQ EQ", 512, CODES)
@@ -25,48 +32,46 @@ buf("XS", 512 * 3, "uint8")
 buf("QT", TO[8], CODES)
 buf("QS", TO[8], "uint8")
 buf("BT", 4 * TO[8], BF)
-buf("JUNK", 7936, BF)
+buf("SG", 3 * 512, BF)
+buf("JK", C0 * JL, F16)
+buf("I1 OWS RD", 512, F16)
+buf("F5 FM VP", 264, F16)
 buf("KB", 1024, BF)
 buf("LINKI", 32, "int32")
-buf("CA", 2608, F32)
-buf("CT", 560, F32)
-buf("CB", 1280, F32)
+buf("CT", 528, F32)
 buf("SM", 16, F32)
-buf("INT", 20, "int32")
+buf("INT", 24, "int32")
 buf("UO", 16, "uint16")
-buf("W3", 1568, F32)
 buf("RS", 32, F32)
-buf("WK", 160, F32)
-buf("EX", 2944, F32)
+buf("WK", 192, F32)
+buf("EX", 1920, F32)
 buf("II", 48, "int32")
 buf("U16", 80, "uint16")
-buf("OWS PAY POS POSA FO EW YS LKO LR0 LR1 TR0 TR1 TRW0 TRW1", 512, F32)
-buf("FF", 1024, F32)
+buf("IOTA PK MSK H PAY POS POSA PKD EW YS LR0 LR1 TR0 TR1 NR0 NR1", 512, F32)
+buf("FO LQK0 LQK1", 256, F32)
 buf("NMR", 128, F32)
-buf("LQK0 LQK1", 256, F32)
 buf("HS", 4 * HW, F32)
-buf("KQ0 KQ1 LL0 LL1", 32, "uint16")
+buf("GB", 3 * 512, F32)
+buf("KQ0 KQ1 LL0 LL1 LI0 LI1", 32, "uint16")
 buf("NL0 NL1 NLI0 NLI1", 8, "uint16")
 buf("TRD0 TRD1 TRX0 TRX1", 32, F32, "dram")
 buf("BRD0 BRD1 BRX0 BRX1", 32, BF, "dram")
-buf("P0 P1 P2 P3 P4 P5 P6 P7", 512, F32, "psum")
+buf("PA PB PC PD P0 P1 P2 P3", 512, F32, "psum")
 
 PIECE = {
-    "AROW": ("CA", 0, 512), "M1": ("CA", 512, 512), "MX": ("CA", 1024, 512), "CR": ("CA", 1536, 512), "CN": ("CA", 2048, 528),
-    "CX": ("CT", 0, 512), "R5": ("CT", 512, 32), "J16": ("CT", 544, 16),
-    "IOTA": ("CB", 0, 512), "I1": ("CB", 512, 512), "ONEF": ("CB", 1024, 256),
-    "PM": ("SM", 0, 2), "NPM": ("SM", 2, 1), "PMH": ("SM", 3, 1), "MC": ("SM", 4, 1),
-    "UOI": ("INT", 0, 16), "PI": ("INT", 16, 2), "PJ": ("INT", 18, 2),
-    "MSK": ("W3", 0, 528), "SCN": ("W3", 528, 528), "SBD": ("W3", 1056, 512),
-    "RSI": ("WK", 0, 32), "RK": ("WK", 32, 32), "NX1": ("WK", 64, 16), "NX2": ("WK", 80, 16), "NN": ("WK", 96, 16), "TOT": ("WK", 112, 1), "RSJ": ("WK", 128, 32),
-    "EXA": ("EX", 0, 512), "EXB": ("EX", 512, 256), "EXK": ("EX", 768, 512), "EXN": ("EX", 1280, 128), "EXE": ("EX", 1408, 512), "EXL": ("EX", 1920, 512), "DS": ("EX", 2432, 512),
-    "CSL": ("II", 0, 32), "VL": ("II", 32, 16),
+    "CX": ("CT", 0, 512), "J16": ("CT", 512, 16),
+    "PM": ("SM", 0, 2), "MC": ("SM", 2, 1), "UP": ("SM", 3, 1), "NUP": ("SM", 4, 1), "NUQ": ("SM", 5, 1), "R15": ("SM", 6, 1),
+    "GM": ("SM", 8, 2), "E4": ("SM", 12, 4),
+    "UOI": ("INT", 0, 16), "PI": ("INT", 16, 2), "PJ": ("INT", 18, 2), "PG": ("INT", 20, 2),
+    "T1": ("WK", 0, 32), "T3": ("WK", 32, 32), "RK": ("WK", 64, 32), "NA": ("WK", 96, 16), "NB": ("WK", 112, 16), "NN": ("WK", 128, 16),
+    "JS": ("WK", 144, 16), "TOT": ("WK", 160, 1),
+    "EXA": ("EX", 0, 512), "EXB": ("EX", 512, 256), "EXK": ("EX", 768, 256), "EXN": ("EX", 1024, 128), "EXE": ("EX", 1152, 512),
+    "KQV": ("II", 0, 16), "KQI": ("II", 16, 32),
     "RKU": ("U16", 0, 32), "NU": ("U16", 32, 16), "EL": ("U16", 48, 32),
-    "FR": ("FF", 0, 256), "F5": ("FF", 256, 256), "FC": ("FF", 512, 256), "VP": ("FF", 768, 256),
 }
 SEMAPHORES = ["cv", "cs", "ct", "cg", "ldx0", "ldx1", "ldu", "ldk", "ldv", "ldw", "ldc", "st"]
 for _t in range(ROUNDS):
-    SEMAPHORES += [s + "%d" % _t for s in ("bro", "bra", "brl", "tbx", "nma", "nml", "cda", "cdl", "tro", "tra", "trl", "trx")]
+    SEMAPHORES += [s + "%d" % _t for s in ("bro", "bra", "brl", "tbx", "nma", "nml", "cda", "cdl", "tro", "tra", "trl", "trx", "lia", "lil")]
 
 
 def rank_program(g, core, T, topo):
@@ -78,322 +83,373 @@ def rank_program(g, core, T, topo):
     count = {"cv": 0, "cs": 0, "ct": 0, "cg": 0}
     total = {}
     know = {q: {} for q in queue}
-    wrote, read = {}, {}
+    tokens = []
+    wrote = {n: np.full(SCRATCH[n][1][1], -1) for n in SCRATCH}
+    read = {n: [] for n in SCRATCH}
 
-    def w(n, a=0, b=None, step=1):
+    def w(n, a=0, b=None, step=1, rows=None):
         if n in PIECE: name, off, width = PIECE[n]
         else: name, off, width = n, 0, SCRATCH[n][1][1]
         if b is None: b = width
-        if step == 1: return T[name][:, off + a:off + b]
-        return T[name][:, off + a:off + b:step]
+        cols = slice(off + a, off + b) if step == 1 else slice(off + a, off + b, step)
+        return (T[name][slice(None) if rows is None else rows, cols], [(name, np.arange(off + a, off + b, step))], [])
 
-    def settle(q, reads, writes):
-        need = []
-        for k in reads:
-            if k in wrote: need.append(wrote[k])
-            if k[0] == "P" and k[1:].isdigit():
-                need += [r for r in read.get(k, []) if r[0] != q]
-        for k in writes:
-            if k in wrote: need.append(wrote[k])
-            need += [r for r in read.get(k, []) if r[0] != q or r[1] not in count]
-        need.sort(key=lambda n: -n[2])
-        for _, sem, val, seen in need:
-            if know[q].get(sem, 0) >= val: continue
-            queue[q].wait_ge(T.sem[sem], val)
-            know[q][sem] = val
+    def ind(win, off): return (win[0].indirect(off[0]), win[1], off[1])
+    def cast(v, d): return (v[0].bitcast(d), v[1], v[2])
+    def hbm(ap): return (ap, [], [])
+    def raw(x): return x[0] if isinstance(x, tuple) else x
+
+    def sides(ins, outs):
+        r, o = [], []
+        for x in ins:
+            if isinstance(x, tuple): r += x[1] + x[2]
+        for x in outs:
+            if isinstance(x, tuple):
+                o += x[1]
+                r += x[2]
+        return r, o
+
+    def settle(q, r, o, sem):
+        need = set()
+        for n, c in r:
+            need |= set(wrote[n][c].tolist())
+            if SCRATCH[n][0] == "psum":
+                need |= set(wrote[n].tolist()) | set(i for i, _ in read[n] if tokens[i][0] != q)
+        for n, c in o:
+            if SCRATCH[n][0] == "psum": need |= set(i for i, _ in read[n])
+            if q != "t": need |= set(wrote[n][c].tolist())
+            need |= set(i for i, d in read[n] if np.intersect1d(c, d).size)
+        need.discard(-1)
+        for i in sorted(need, key=lambda i: -tokens[i][2]):
+            _, s, val, seen = tokens[i]
+            if s == sem and s not in count: continue
+            if know[q].get(s, 0) >= val: continue
+            queue[q].wait_ge(T.sem[s], val)
+            know[q][s] = val
             for s2 in seen: know[q][s2] = max(know[q].get(s2, 0), seen[s2])
 
-    def note(token, reads, writes):
-        for k in reads: read.setdefault(k, []).append(token)
-        for k in writes:
-            wrote[k] = token
-            read[k] = []
+    def note(token, r, o):
+        tokens.append(token)
+        for n, c in o:
+            wrote[n][c] = len(tokens) - 1
+            read[n] = [] if SCRATCH[n][0] == "psum" else [(i, np.setdiff1d(d, c)) for i, d in read[n] if np.setdiff1d(d, c).size]
+        for n, c in r: read[n].append((len(tokens) - 1, c))
 
-    def op(q, call, reads, writes):
-        settle(q, reads, writes)
+    def op(q, call, ins, outs):
+        r, o = sides(ins, outs)
+        settle(q, r, o, None)
         sem = own[q]
         call().then_inc(T.sem[sem], 1)
         count[sem] += 1
         total[sem] = count[sem]
-        note((q, sem, count[sem], dict(know[q])), reads, writes)
+        note((q, sem, count[sem], dict(know[q])), r, o)
 
-    def dma(q, out, in_, sem, of, reads, writes):
-        settle(q, reads, writes)
-        queue[q].dma_start(out, in_).then_inc(T.sem[sem], 16)
+    def dma(q, out, in_, sem, of, after=()):
+        r, o = sides([in_] + list(after), [out])
+        settle(q, r, o, sem)
+        queue[q].dma_start(out[0], in_[0]).then_inc(T.sem[sem], 16)
         total[sem] = 16 * of
-        note((q, sem, 16 * of, dict(know[q])), reads, writes)
+        note((q, sem, 16 * of, dict(know[q])), sides([in_], [])[0], o)
 
-    def send(dst, out, in_, rsem, lsem, reads, of=1):
-        settle("g", reads, [])
+    def send(dst, out, in_, rsem, lsem, of=1):
+        r, _ = sides([in_], [])
+        settle("g", r, [], None)
         rid, pid = topo.addr(dst)[:2]
         n = len(topo.engines(core, dst))
-        g.remote_dma(out, in_, T.sem[rsem], T.sem[lsem], pid, rid, topo.mask(core, dst))
+        g.remote_dma(out[0], in_[0], T.sem[rsem], T.sem[lsem], pid, rid, topo.mask(core, dst))
         total[lsem] = n * of
-        note(("g", lsem, n * of, dict(know["g"])), reads, [])
+        note(("g", lsem, n * of, dict(know["g"])), r, [])
 
-    def lands(src, key, rsem, of=1):
-        n = len(topo.engines(src, core)) * of
+    def lands(src, views, rsem):
+        n = len(topo.engines(src, core)) * len(views)
         total[rsem] = n
-        note(("far", rsem, n, {}), [], [key])
+        note(("far", rsem, n, {}), [], sides([], views)[1])
 
     V, S, G = g.vector, g.scalar, g
 
-    def ts(out, in0, a, b, op0, op1, reads, writes):
-        if op1 is None: op("v", lambda: V.tensor_scalar(out, in0, a, None, op0), reads, writes)
-        else: op("v", lambda: V.tensor_scalar(out, in0, a, b, op0, op1), reads, writes)
+    def ts(out, in0, a, b, op0, op1=None):
+        if op1 is None: op("v", lambda: V.tensor_scalar(out[0], in0[0], raw(a), None, op0), [in0, a], [out])
+        else: op("v", lambda: V.tensor_scalar(out[0], in0[0], raw(a), raw(b), op0, op1), [in0, a, b], [out])
 
-    def tt(out, in0, in1, o, reads, writes): op("v", lambda: V.tensor_tensor(out, in0, in1, o), reads, writes)
-    def cp(out, in_, reads, writes): op("v", lambda: V.tensor_copy(out, in_), reads, writes)
-    def fill(out, c, writes): op("v", lambda: V.memset(out, c), [], writes)
-    def act(out, in_, func, scale, reads, writes): op("s", lambda: S.activation(out, in_, func, scale=scale), reads, writes)
-    def actb(out, in_, func, bias, scale, reads, writes): op("s", lambda: S.activation(out, in_, func, bias=bias, scale=scale), reads, writes)
-    def scan(out, d0, d1, reads, writes): op("v", lambda: V.tensor_tensor_scan(out, d0, d1, 0.0, OP.mult, OP.add), reads, writes)
-    def quant(q, s, in_, reads, writes): op("v", lambda: V.quantize_mx(q, s, in_), reads, writes)
-    def mm(out, a, asc, b, bsc, start, stop, reads, writes): op("t", lambda: g.tensor.matmul_mx(out, a, asc, b, bsc, start, stop), reads, writes)
-    def iota(out, pattern, base, cm, keys): op("g", lambda: G.iota(out, pattern, base, cm, allow_small_or_imprecise_dtypes=True), [], keys)
-    def iotai(out, pattern, base, cm, keys): op("g", lambda: G.iota(out, pattern, base, cm), [], keys)
-    def select(out, in_, pattern, cmp, c, base, cm, reads, writes): op("g", lambda: G.affine_select(out, in_, pattern, cmp, c, base, cm), reads, writes)
+    def tt(out, in0, in1, o): op("v", lambda: V.tensor_tensor(out[0], in0[0], in1[0], o), [in0, in1], [out])
+    def cp(out, in_): op("v", lambda: V.tensor_copy(out[0], in_[0]), [in_], [out])
+    def fill(out, c): op("v", lambda: V.memset(out[0], c), [], [out])
+    def scan(out, d0, d1, op0, op1): op("v", lambda: V.tensor_tensor_scan(out[0], d0[0], d1[0], 0.0, op0, op1), [d0, d1], [out])
+    def quant(q, s, in_): op("v", lambda: V.quantize_mx(q[0], s[0], in_[0]), [in_], [q, s])
+    def mm(out, a, asc, b, bsc, start=True, stop=True): op("t", lambda: g.tensor.matmul_mx(out[0], a[0], asc[0], b[0], bsc[0], start, stop), [a, asc, b, bsc], [out])
+    def iota(out, pattern, base, cm): op("g", lambda: G.iota(out[0], pattern, base, cm, allow_small_or_imprecise_dtypes=True), [], [out])
+    def iotai(out, pattern, base, cm): op("g", lambda: G.iota(out[0], pattern, base, cm), [], [out])
+    def select(out, in_, pattern, cmp, c, base, cm): op("g", lambda: G.affine_select(out[0], in_[0], pattern, cmp, c, base, cm), [in_], [out])
 
-    CXK = ["CT0"] + ["CX%d" % i for i in range(1, 8)]
+    def act(out, in_, func, scale=1.0, bias=None, accum=None):
+        if accum is not None: op("s", lambda: S.activation(out[0], in_[0], func, accum_out=accum[0]), [in_], [out, accum])
+        elif bias is None and scale == 1.0: op("s", lambda: S.activation(out[0], in_[0], func), [in_], [out])
+        elif bias is None: op("s", lambda: S.activation(out[0], in_[0], func, scale=scale), [in_], [out])
+        else: op("s", lambda: S.activation(out[0], in_[0], func, bias=raw(bias), scale=scale), [in_, bias], [out])
 
-    def lift(ex, a, row, n, key):
-        scan(w(ex, a, a + n), w("CX", 0, n), row, CXK + [key], ["%s.%d" % (ex, a)])
+    def lift(ex, row, n): scan(w(ex, 0, n), w("CX", 0, n), row, OP.mult, OP.add)
+    def top(ex, n): return w(ex, 15, n, 16)
+    def down(out, ex, n, more=None): ts(out, top(ex, n), w("MC"), more, OP.mult, None if more is None else OP.add)
 
-    def down(out, ex, a, n, less, key):
-        ts(out, w(ex, a + 15, a + n, 16), w("MC"), less, OP.mult, OP.add if less else None, ["%s.%d" % (ex, a), "MC"], [key])
+    rows8 = slice(0, 128, 16)
+    nxt = [T.cores[(rank + 2 ** t) % N] for t in range(ROUNDS)]
+    prv = [T.cores[(rank - 2 ** t) % N] for t in range(ROUNDS)]
 
-    dma("s", w("UB"), T.u[:, :], "ldu", 1, [], ["UB"])
-    dma("y", w("X0", 0, 1024), T.x[:, 0:1024], "ldx0", 1, [], ["X0a"])
-    dma("s", w("X0", 1024, 2048), T.x[:, 1024:2048], "ldx1", 1, [], ["X0b"])
-    dma("y", w("LINKI"), T.link[:, :], "ldk", 1, [], ["LINKI"])
-    dma("y", w("WQ").bitcast(dt.uint8), T.wc[:, :], "ldw", 2, [], ["WQ"])
-    dma("y", w("WS"), T.ws[:, :], "ldw", 2, [], ["WS"])
-    dma("y", w("VB"), T.v[:, :], "ldv", 1, [], ["VB"])
+    dma("y", w("X0", 1024, 2048), hbm(T.x[:, 1024:2048]), "ldx1", 1)
+    dma("s", w("UB"), hbm(T.u[:, :]), "ldu", 1)
+    dma("s", w("LINKI"), hbm(T.link[:, :]), "ldk", 1)
+    dma("y", w("X0", 0, 1024), hbm(T.x[:, 0:1024]), "ldx0", 1)
+    dma("y", w("VB"), hbm(T.v[:, :]), "ldv", 1, [w("X0")])
+    dma("y", cast(w("WQ"), dt.uint8), hbm(T.wc[:, :]), "ldw", 2)
+    dma("y", w("WS"), hbm(T.ws[:, :]), "ldw", 2)
 
-    iotai(w("PI"), [[0, 2]], 0, 1, ["PI"])
-    iota(w("AROW"), [[0, 32], [1, 16]], 0, 0, ["AROW"])
-    iotai(w("UOI"), [[1, 2], [16, 8]], 0, 0, ["UOI"])
-    ts(w("PJ"), w("PI"), 15, None, OP.bitwise_and, None, ["PI"], ["PJ"])
-    fill(w("ON"), 1.0, ["ON"])
-    cp(w("PM"), w("PJ"), ["PJ"], ["PM"])
+    iotai(w("PI"), [[0, 2]], 0, 1)
+    iotai(w("UOI"), [[1, 2], [16, 8]], 0, 0)
+    iota(w("AROW"), [[0, 32], [1, 16]], 0, 0)
+    iota(w("I1"), [[1, 512]], 1, 0)
+    iota(w("E4"), [[1, 4]], 1, 4)
+    iota(w("IOTA"), [[1, 512]], 0, 0)
+    for k in range(8): fill(w("BT", 4 * TO[k] + 64 * (4 * k + 1), 4 * TO[k + 1]), 0.0)
+    ts(w("PJ"), w("PI"), 15, None, OP.bitwise_and)
+    ts(w("PG"), w("PI"), 112, None, OP.bitwise_and)
+    cp(w("UO"), w("UOI"))
+    cp(w("PM"), w("PJ"))
     pm = w("PM", 0, 1)
-    fill(w("MSK", 512, 528), 0.0, ["MSKp"])
-    fill(w("CN", 512, 528), 1.0, ["CNp"])
-    ts(w("NPM"), pm, -1.0, None, OP.mult, None, ["PM"], ["NPM"])
-    ts(w("PMH"), pm, 0.5, None, OP.subtract, None, ["PM"], ["PMH"])
-    for k in range(7, -1, -1):
-        fill(w("BT", 4 * TO[k] + 256 * k, 4 * TO[k + 1]), 0.0, ["BT%d.%d" % (k, s) for s in range(4)] + ["BT%dd" % k])
-    fill(w("RS", 0, 1), 0.0, ["RS0"])
-    cp(w("UO"), w("UOI"), ["UOI"], ["UO"])
-    actb(w("CN", 0, 512), w("AROW"), AF.Abs, w("NPM"), 1.0, ["AROW", "NPM"], ["CN"])
-    actb(w("M1"), w("CN", 0, 512), AF.Relu, 1.0, -1.0, ["CN"], ["M1"])
-    actb(w("MX"), w("AROW"), AF.Sign, w("PMH"), -1.0, ["AROW", "PMH"], ["MX"])
-    actb(w("CN", 0, 512), w("M1"), AF.Copy, 1.0, -1.0, ["M1"], ["CN"])
-    act(w("MX"), w("MX"), AF.Copy, 1e25, ["MX"], ["MX"])
-    act(w("CR"), w("AROW"), AF.Sign, 1.0, ["AROW"], ["CR"])
-    select(w("OB"), w("ON"), [[-16, 8], [0, 64]], OP.is_ge, 0.0, 0, 1, ["ON"], ["OB"])
-    select(w("OB"), w("OB"), [[16, 8], [0, 64]], OP.is_ge, 0.0, 15, -1, ["OB"], ["OB"])
-    for b in range(4): select(w("EB", 512 * b, 512 * b + 512), w("ON"), [[-4, 128], [-1, 4]], OP.is_equal, 0.0, b, 4, ["ON"], ["EB%d" % b])
-    iota(w("IOTA"), [[1, 512]], 0, 0, ["IOTA"])
-    quant(w("UQ"), w("UQS"), w("UB"), ["UB"], ["UQ"])
+    ts(w("GM"), w("PG"), -4.0, -31.5, OP.mult, OP.add)
+    fill(w("JK", JL - 2, JL), 0.0)
+    fill(w("F5"), 0.0)
+    fill(w("FM", 0, 2), 0.0)
+    ts(w("KM"), w("AROW"), pm, -2.0 * FAR, OP.not_equal, OP.mult)
+    ts(w("RZ"), w("AROW"), 0.5, 2.0 * FAR, OP.subtract, OP.mult)
+    fill(w("ON", rows=slice(0, 32)), 1.0)
+    ts(w("MC"), pm, 15.0, 1.0 - 1.0 / BIG, OP.is_equal, OP.mult)
+    ts(w("UP"), pm, 15.0, BIG, OP.not_equal, OP.mult)
+    ts(w("R15"), pm, -1.0, 15.25, OP.mult, OP.add)
+    quant(w("UQ"), w("UQS"), w("UB"))
+    ts(w("MC"), w("MC"), 1.0 / BIG, None, OP.max)
+    ts(w("UP"), w("UP"), 1.0, None, OP.max)
 
     def pick_u(q, o):
-        cp(w(q).bitcast(dt.uint32), w("UQ").bitcast(dt.uint32).indirect(w("UO", o, o + 8)), ["UQ", "UO"], [q])
-        cp(w(q + "S"), w("UQS").indirect(w("UO", o, o + 8)), ["UQ", "UO"], [q + "S"])
+        cp(cast(w(q), dt.uint32), ind(cast(w("UQ"), dt.uint32), w("UO", o, o + 8)))
+        act(w(q + "S"), ind(w("UQS"), w("UO", o, o + 8)), AF.Copy)
+
+    def unit(b): ts(w("EB", 512 * b, 512 * b + 512), w("I1"), w("E4", b, b + 1), None, OP.is_equal)
+    def xq(t, h): return w("XQ", 512 * t + 256 * h, 512 * t + 256 * h + 256), w("XS", 512 * t + 256 * h, 512 * t + 256 * h + 256)
+    def pack_x(t, h): quant(*xq(t, h), w("XN%d" % (t - 1) if t else "X0", 1024 * h, 1024 * h + 1024))
+
+    pick_u("UR", 0)
+    pack_x(0, 1)
+    cp(w("LL0"), w("LINKI"))
+    send(nxt[0], w("LI0"), w("LL0"), "lia0", "lil0")
+    pick_u("UT", 8)
+    act(w("SG", 0, 512), w("IOTA"), AF.Abs, 1.0, w("GM", 0, 1))
+    act(w("LR0"), ind(w("IOTA"), w("LL0")), AF.Copy)
+    act(w("TR0"), w("LR0"), AF.Copy)
+    ts(w("NUP"), w("UP"), -1.0, None, OP.mult)
+    ts(w("NUQ"), w("UP"), -256.0, None, OP.mult)
+    for b in range(4): fill(w("HS", HW * b + 256, HW * b + HW), 0.0)
+    for b in range(4): unit(b)
 
     def later_constants():
-        iota(T.CT[0:16, 0:512], [[0, 512]], 1, 0, ["CTx"])
-        select(T.CT[0:16, 0:512], T.CT[0:16, 0:512], [[0, 32], [1, 16]], OP.is_gt, 0.0, 0, -1, ["CTx"], ["CTx"])
-        select(T.CT[0:16, 0:512], T.CT[0:16, 0:512], [[0, 32], [1, 16]], OP.not_equal, BIG, -1, -1, ["CTx"], ["CTx"])
-        iota(T.CT[0:16, 512:544], [[-16, 32]], 511, -1, ["CTy"])
-        iota(T.CT[0:16, 544:560], [[16, 16]], 0, 1, ["CTz", "CT0"])
-        for i in range(1, 8): dma("y", T.CT[16 * i:16 * i + 16, :], T.CT[0:16, :], "ldc", 7, ["CTx", "CTy", "CTz"], ["CX%d" % i])
-        iota(w("I1"), [[1, 512]], 1, 0, ["I1"])
-        iota(w("ONEF"), [[0, 256]], 1, 0, ["ONEF"])
-        for b in range(4): iota(w("HS", HW * b + 256, HW * b + HW), [[0, 8]], 0, 0, ["HSZ%d" % b])
-        iota(w("TRW1"), [[0, 512]], 0, 0, ["TRW1"])
+        r16 = slice(0, 16)
+        select(w("CX", rows=r16), w("ON", rows=r16), [[0, 32], [1, 16]], OP.is_gt, 0.0, 0, -1)
+        select(w("CX", rows=r16), w("CX", rows=r16), [[0, 32], [1, 16]], OP.not_equal, BIG, -1, -1)
+        iota(w("J16", rows=r16), [[16, 16]], 0, 1)
+        iota(w("RD0"), [[-16, 32], [1024, 16]], 0, 0)
 
-    def turn_rows(t):
-        n, lr = "LQK%d" % t, "LR%d" % t
-        act(w(n, 0, 128), w(lr).indirect(w("KQ%d" % t, 24, 32)), AF.Copy, 1.0, [lr, "QL%d" % t], [n + "a"])
-        act(w(n, 128, 256), w(lr).indirect(w("KQ%d" % t, 16, 24)), AF.Copy, 1.0, [lr, "KL%d" % t], [n + "b"])
-
-    def turn_send(t, back):
-        n, tr = "LQK%d" % t, "TR%d" % t
-        cp(w(tr).indirect(w("KQ%d" % t, 16, 32)), w(n), [n + "a", n + "b", "QL%d" % t, "KL%d" % t], [tr])
-        dma("y", w("TRD%d" % t), T[tr][0:128:16, :], "tro%d" % t, 1, [tr], ["TRD%d" % t])
-        send(back, w("TRX%d" % t), w("TRD%d" % t), "tra%d" % t, "trl%d" % t, ["TRD%d" % t])
+    def copy_constants():
+        for i in range(1, 8): dma("y", w("CT", rows=slice(16 * i, 16 * i + 16)), w("CT", rows=slice(0, 16)), "ldc", 7)
 
     def spread(n, src, sem):
-        for a in range(16): dma("y", T[n][a:128:16, :], w(src), sem, 16, [src], ["%s.%d" % (n, a)])
+        for a in range(16): dma("y", w(n, rows=slice(a, 128, 16)), w(src), sem, 16)
 
+    def turn(t):
+        kq, n = "KQ%d" % t, "LQK%d" % t
+        cp(ind(w("TR%d" % t), w(kq, 8, 16)), w(n, 0, 128))
+        cp(ind(w("TR%d" % t), w(kq, 24, 32)), w(n, 128, 256))
+
+    def turned(t):
+        lands(prv[t], [w("LI%d" % t)], "lia%d" % t)
+        act(w("NR%d" % t), ind(w("TR%d" % t), w("LI%d" % t)), AF.Copy)
+        dma("y", w("TRD%d" % t), w("NR%d" % t, rows=rows8), "tro%d" % t, 1)
+        send(prv[t], w("TRX%d" % t), w("TRD%d" % t), "tra%d" % t, "trl%d" % t)
+
+    later_constants()
     for t in range(ROUNDS):
-        d = 2 ** t
-        nxt, prv = T.cores[(rank + d) % N], T.cores[(rank - d) % N]
         last = t == ROUNDS - 1
-        X, xk = ("X0", ["X0a", "X0b"]) if t == 0 else ("XN%d" % (t - 1), ["XN%d.%d" % (t - 1, b) for b in range(4)])
-        xq, xs = w("XQ", 512 * t, 512 * t + 512), w("XS", 512 * t, 512 * t + 512)
-        kx = "XQ%d" % t
+        xc, xs = w("XQ", 512 * t, 512 * t + 512), w("XS", 512 * t, 512 * t + 512)
         ll, lr, kq, br, tb = ("%s%d" % (n, t) for n in ("LL", "LR", "KQ", "BR", "TB"))
-        if t == 0: pick_u("UR", 0)
-        quant(xq, xs, w(X), xk, [kx])
-        if t == 0: pick_u("UT", 8)
-        mm(w("P0"), w("UR"), w("URS"), xq, xs, True, True, ["UR", "URS", kx], ["P0"])
-        mm(w("P1"), w("UT"), w("UTS"), xq, xs, True, True, ["UT", "UTS", kx], ["P1"])
-        if t: turn_send(t - 1, T.cores[(rank - d // 2) % N])
-        act(w("BS"), w("P1"), AF.Sign, 1.0, ["P1"], ["BS"])
-        actb(w(br), w("BS"), AF.Sign, -0.5, 1.0, ["BS"], [br])
-        tt(w("MSK", 0, 512), w("P0"), w("M1"), OP.mult, ["P0", "M1"], ["MSK"])
-        tt(w("SBD"), w("P0"), w("MX"), OP.min, ["P0", "MX"], ["SBD"])
-        scan(w("SCN"), w("CN"), w("MSK"), ["CN", "CNp", "MSK", "MSKp"], ["SCN"])
-        dma("y", w("BRD%d" % t), T[br][0:128:16, :], "bro%d" % t, 1, [br], ["BRD%d" % t])
-        send(prv, w("BRX%d" % t), w("BRD%d" % t), "bra%d" % t, "brl%d" % t, ["BRD%d" % t])
+        mm(w("PD", 0, 256), w("UR"), w("URS"), *xq(t, 1))
+        pack_x(t, 0)
+        mm(w("PA"), w("UR"), w("URS"), xc, xs)
+        mm(w("PC"), w("UR"), w("URS"), xc, xs)
+        mm(w("PB"), w("UT"), w("UTS"), xc, xs)
+        tt(w("MSK", 256, 512), w("PD", 0, 256), w("KM", 256, 512), OP.add)
+        if t == 0: ts(w("OB"), w("SG", 0, 512), 32.0, None, OP.is_lt)
+        scan(w("H", 256, 512), w("RZ", 256, 512), w("MSK", 256, 512), OP.min, OP.max)
+        tt(w("MSK", 0, 256), w("PA", 0, 256), w("KM", 0, 256), OP.add)
+        if t == 0: quant(w("OQ"), w("OQS"), w("OB"))
+        scan(w("H", 0, 256), w("RZ", 0, 256), w("MSK", 0, 256), OP.min, OP.max)
+
+        def row(c, a, b): return w("BT", 4 * (TO[(c - 1) // 4] + a) + (c - 1) % 4, 4 * (TO[(c - 1) // 4] + b), 4)
+        def mine(c): return w("H", 16 * c + 15, 16 * c + 16)
+        def sign(c): act(w("SG", 512 * (c % 3), 512 * (c % 3) + 16 * c), w("PC", 0, 16 * c), AF.Sign, -1.0, mine(c))
+        def beats(c): act(row(c, 0, 16 * c), w("SG", 512 * (c % 3), 512 * (c % 3) + 16 * c), AF.Relu, accum=w("RS", c, c + 1))
+        def below(c): ts(row(c, 0, 16 * c), w("PA", 0, 16 * c), mine(c), None, OP.is_lt)
+        def rowsum(c): scan(w("JK", JL * (c + 1) - 8 * c, JL * (c + 1)), row(c, 0, 8 * c), row(c, 8 * c, 16 * c), OP.add, OP.add)
+        def pack_b(k): quant(w("QT", TO[k], TO[k + 1]), w("QS", TO[k], TO[k + 1]), w("BT", 4 * TO[k], 4 * TO[k + 1]))
+        def colsum(k, first, end): mm(w("PD", 0, TC[k]), w("OQ"), w("OQS"), w("QT", TO[k], TO[k + 1]), w("QS", TO[k], TO[k + 1]), first, end)
+
+        below(C0 - 1)
+        ts(w(br), w("PB"), 0.0, 0.5, OP.is_gt, OP.subtract)
+        if t: turned(t - 1)
+        dma("y", w("BRD%d" % t), w(br, rows=rows8), "bro%d" % t, 1)
+        send(prv[t], w("BRX%d" % t), w("BRD%d" % t), "bra%d" % t, "brl%d" % t)
+        if t == 0: copy_constants()
         if t:
-            p = t - 1
-            lands(T.cores[(rank + d // 2) % N], "TRX%d" % p, "tra%d" % p)
-            spread("TRW%d" % p, "TRX%d" % p, "trx%d" % p)
-        lands(nxt, "BRX%d" % t, "bra%d" % t)
+            lands(nxt[t - 1], [w("TRX%d" % (t - 1))], "tra%d" % (t - 1))
+            spread(lr, "TRX%d" % (t - 1), "trx%d" % (t - 1))
+        lands(nxt[t], [w("BRX%d" % t)], "bra%d" % t)
         spread(tb, "BRX%d" % t, "tbx%d" % t)
-        if t == 0: later_constants()
-        iota(w("EW"), [[0, 512]], 256, 0, ["EW"])
+        if t == 0: iota(w("PK"), [[0, 256], [512, 2]], 0, 0)
 
-        def colsum(k):
-            q, s = w("QT", TO[k], TO[k + 1]), w("QS", TO[k], TO[k + 1])
-            quant(q, s, w("BT", 4 * TO[k], 4 * TO[k + 1]), ["BT%d.%d" % (k, i) for i in range(4)] + ["BT%dd" % k], ["QT%d" % k])
-            mm(w("P6", 0, TC[k]), w("OQ"), w("OQS"), q, s, k == 7, k == 0, ["OQ", "QT%d" % k], ["P6"])
+        sign(31)
+        for c in range(30, C0 - 1, -1):
+            sign(c)
+            beats(c + 1)
+        beats(C0)
+        tt(row(32, 0, 512), w("PA"), w("H"), OP.is_le)
+        waiting = []
+        started = [False]
 
-        for k in range(7, -1, -1):
-            o = 4 * TO[k]
-            for i in range(3, -1, -1):
-                c = 4 * k + i
-                key = "BT%d.%d" % (k, i)
-                sc = w("SCN", 16 * c + 15, 16 * c + 16)
-                if c:
-                    ts(w("BT", o + i, o + 64 * c, 4), w("P0", 0, 16 * c), sc, None, OP.is_ge, None, ["P0", "SCN"], [key])
-                    j = 8 * c * (c - 1)
-                    op("s", lambda: S.activation(w("JUNK", j, j + 16 * c), w("BT", o + i, o + 64 * c, 4), AF.Copy, accum_out=w("RS", c, c + 1)), [key], ["JUNK%d" % c, "RS%d" % c])
-                if i == 3:
-                    tt(w("BT", o + 256 * k, o + 256 * k + 256, 4), w("SBD", 64 * k, 64 * k + 64), w("SCN", 64 * k + 16, 64 * k + 80), OP.is_ge, ["SBD", "SCN"], ["BT%dd" % k])
-                    if k < 7: colsum(k + 1)
-                if i == 1: scan(w("DS", 64 * k, 64 * k + 64), w("CR", 64 * k, 64 * k + 64), w("BT", o + 256 * k, o + 256 * k + 256, 4), ["CR", "BT%dd" % k], ["DS%d" % k])
-            if k == 7 and t == 0:
-                quant(w("OQ"), w("OQS"), w("OB"), ["OB"], ["OQ"])
-                cp(w("LL0"), w("LINKI"), ["LINKI"], ["LL0"])
-            if k == 6 and t == 0:
-                quant(w("EQ"), w("EQS"), w("EB"), ["EB%d" % b for b in range(4)], ["EQ"])
-                ts(w("MC"), pm, 15.0, 1.0 - 1.0 / BIG, OP.is_equal, OP.mult, ["PM"], ["MC"])
-            if k == 7 and t or k == 6 and not t:
-                for b in range(4):
-                    mm(w("P%d" % (2 + b)), w("EQ", 128 * b, 128 * b + 128), w("EQS", 128 * b, 128 * b + 128), xq, xs, True, True, ["EQ", kx], ["P%d" % (2 + b)])
-            if k == 5:
-                if t == 0: ts(w("MC"), w("MC"), 1.0 / BIG, None, OP.add, None, ["MC"], ["MC"])
-                if t == 0: act(w(lr), w("IOTA").indirect(w(ll)), AF.Copy, 1.0, ["IOTA", ll], [lr])
-            if k == 3:
-                if t: act(w(lr), w("TRW%d" % (t - 1)).indirect(w("LL%d" % (t - 1))), AF.Copy, 1.0, ["TRW%d.%d" % (t - 1, a) for a in range(16)] + ["LL%d" % (t - 1)], [lr])
-                tt(w("OWS"), w(br), w("I1"), OP.mult, [br, "I1"], ["OWS"])
-            if k == 1 and t: lift("EXL", 0, w(lr), 512, lr)
-        if t: down(w(ll), "EXL", 0, 512, None, ll)
-        else: quant(w("VQ"), w("VQS"), w("VB"), ["VB"], ["VQ"])
-        colsum(0)
-        for b in range(4): act(w("FH", 512 * b, 512 * b + 512), w("P%d" % (2 + b)), AF.Copy, 0.5, ["P%d" % (2 + b)], ["FH%d" % b])
-        act(w("TR%d" % t), w(lr), AF.Copy, 1.0, [lr], ["TR%d" % t])
-        tt(w("RSJ"), w("DS", 15, 512, 16), w("R5"), OP.add, ["DS%d" % c for c in range(8)] + CXK, ["RSJ"])
-        tt(w("PAY"), w(tb).indirect(w(ll)), w("OWS"), OP.mult, ["%s.%d" % (tb, a) for a in range(16)] + [ll, "OWS"], ["PAY"])
-        lift("EXA", 0, w("P6"), 512, "P6")
-        tt(w("RSI"), w("RS"), w("RSJ"), OP.add, ["RS%d" % c for c in range(32)] + ["RSJ"], ["RSI"])
-        down(w("CSL"), "EXA", 0, 512, None, "CSL")
-        tt(w("RK"), w("RSI"), w("CSL"), OP.subtract, ["RSI", "CSL"], ["RK"])
-        cp(w("RKU"), w("RK"), ["RK"], ["RKU"])
-        cp(w("POS").indirect(w("RKU")), w("PAY"), ["RKU", "PAY"], ["POS"])
-        act(w("POSA"), w("POS"), AF.Abs, 1.0, ["POS"], ["POSA"])
-        ts(w("FR"), w("POS", 1, 512, 2), 0.0, None, OP.is_lt, None, ["POS"], ["FR"])
-        ts(w("F5"), w("POS", 1, 512, 2), 0.0, 512.0, OP.is_lt, OP.mult, ["POS"], ["F5"])
-        scan(w("FC"), w("ONEF"), w("FR"), ["ONEF", "FR"], ["FC"])
-        tt(w("VP"), w("FC"), w("F5"), OP.add, ["FC", "F5"], ["VP"])
-        ts(w("TOT"), w("FC", 255, 256), -1.0, -257.0, OP.mult, OP.add, ["FC"], ["TOT"])
-        lift("EXB", 0, w("VP"), 256, "VP")
-        down(w("VL"), "EXB", 0, 256, None, "VL")
-        tt(w("NX1"), w("J16"), w("VL"), OP.subtract, CXK + ["VL"], ["NX1"])
-        ts(w("NX2"), w("VL"), w("TOT"), None, OP.add, None, ["VL", "TOT"], ["NX2"])
-        tt(w("NN"), w("NX1"), w("NX2"), OP.max, ["NX1", "NX2"], ["NN"])
-        cp(w("NU"), w("NN"), ["NN"], ["NU"])
-        cp(w("FO", 0, 256).indirect(w("NU")), w("POSA", 0, 512, 2), ["NU", "POSA"], ["FOk"])
-        cp(w("FO", 256, 512).indirect(w("NU")), w("POSA", 1, 512, 2), ["NU", "POSA"], ["FOq"])
-        for b in range(4): act(w("FB", 512 * b, 512 * b + 512), w("P%d" % (2 + b)), AF.Copy, 1.0, ["P%d" % (2 + b)], ["FB%d" % b])
+        def done(k, end=False):
+            pack_b(k)
+            waiting.append(k)
+            if k == 7: started[0] = True
+            if started[0]:
+                for j in sorted(waiting, reverse=True): colsum(j, j == 7, end and j == min(waiting))
+                waiting.clear()
 
-        def lists(h):
-            o = 128 if h == "L" else 0
-            lift("EXK", o, w("FO", o, o + 128), 128, "FOk")
-            lift("EXK", o + 256, w("FO", o + 256, o + 384), 128, "FOq")
-            down(w(kq, o // 8, o // 8 + 8), "EXK", o, 128, -1.0, "K%s%d" % (h, t))
-            down(w(kq, o // 8 + 8, o // 8 + 16), "EXK", o + 256, 128, -1.0, "Q%s%d" % (h, t))
+        for c in range(C0 - 2, 0, -1):
+            below(c)
+            if c == 8: scan(w("RD"), w("RD0"), row(32, 0, 512), OP.min, OP.add)
+            rowsum(c + 1)
+            if c % 4 == 0 and 4 <= c < 20: done(c // 4)
+            if c == AT7: done(7)
+            if c == AT6: done(6)
+            if c == 12 and t == 0:
+                quant(w("EQ"), w("EQS"), w("EB"))
+            if c == 12:
+                for b in range(4): mm(w("P%d" % b), w("EQ", 128 * b, 128 * b + 128), w("EQS", 128 * b, 128 * b + 128), xc, xs)
+            if c == 6 and t:
+                lift("EXE", w(lr), 512)
+            if c == 5 and t:
+                down(w(ll), "EXE", 512)
+                send(nxt[t], w("LI%d" % t), w(ll), "lia%d" % t, "lil%d" % t)
+        iota(w("EW"), [[0, 512]], 256, 0)
+        done(0)
+        rowsum(1)
+        scan(w("OWS"), w("I1"), w(br), OP.max, OP.mult)
+        done(5, True)
+        tt(w("T1", 0, C0), w("JK", JL - 1, JL * C0, JL), w("RD", 15, 16 * C0, 16), OP.add)
+        tt(w("T1", C0, 32), w("RS", C0, 32), w("RD", 16 * C0 + 15, 512, 16), OP.add)
+        if t == 0: ts(w("JS"), w("J16"), w("UP"), None, OP.mult)
+        tt(w("PAY"), ind(w(tb), w(ll)), w("OWS"), OP.mult)
+        lift("EXA", w("PD"), 512)
+        ts(w("T3"), w("T1"), w("UP"), None, OP.mult)
+        for b in range(4): act(w("FH", 512 * b, 512 * b + 512), w("P%d" % b), AF.Copy, 0.5)
+        tt(w("RK"), top("EXA", 512), w("T3"), OP.subtract)
+        ts(w("RKU"), w("RK"), w("MC"), w("R15"), OP.mult, OP.add)
+        cp(ind(w("POS"), w("RKU")), w("PAY"))
+        act(w("POSA"), w("POS"), AF.Abs, 4.0)
+        ts(w("F5", 1, 257), w("POS", 1, 512, 2), 0.0, 512.0, OP.is_lt, OP.mult)
+        ts(w("FM", 1, 257), w("F5", 1, 257), -511.0 / 512.0, None, OP.mult)
+        scan(w("VP", 0, 257), w("FM", 0, 257), w("F5", 1, 258), OP.add, OP.add)
+        lift("EXB", w("VP", 0, 256), 256)
+        ts(w("TOT"), w("VP", 256, 257), w("NUP"), w("NUQ"), OP.mult, OP.add)
+        tt(w("NB"), w("JS"), top("EXB", 256), OP.subtract)
+        ts(w("NA"), top("EXB", 256), w("TOT"), None, OP.add)
+        scan(w("PKD"), w("PK"), w("POSA"), OP.mult, OP.add)
+        tt(w("NN"), w("NA"), w("NB"), OP.max)
+        ts(w("NU"), w("NN"), w("MC"), 0.25, OP.mult, OP.add)
+        cp(ind(w("FO"), w("NU")), w("PKD", 1, 512, 2))
+        nv = 4 - NS[t]
+        for b in range(nv): act(w("FB", 512 * b, 512 * b + 512), w("P%d" % b), AF.Copy)
+        if t: act(w("TR%d" % t), w(lr), AF.Copy)
+        lift("EXK", w("FO"), 256)
+        down(w("KQV"), "EXK", 256, -513.0)
+        ts(w("KQI", 0, 16), w("KQV"), 9, None, OP.arith_shift_right)
+        ts(w("KQI", 16, 32), w("KQV"), 511, None, OP.bitwise_and)
+        cp(w(kq), w("KQI"))
 
-        def firsts(h):
-            o, i = (16, 512) if h == "L" else (0, 0)
-            for b in range(4):
-                act(w("KB", i + 128 * b, i + 128 * b + 128), w("FH", 512 * b, 512 * b + 512).indirect(w(kq, o, o + 8)), AF.Copy, 1.0, ["FH%d" % b, "K%s%d" % (h, t)], ["KB%s%d" % (h, b)])
+        def first(h, b):
+            o, i = (8, 512) if h == "L" else (0, 0)
+            act(w("KB", i + 128 * b, i + 128 * b + 128), ind(w("FH", 512 * b, 512 * b + 512), w(kq, o, o + 8)), AF.Copy)
 
         def second(h, b):
-            o, i = (24, 512) if h == "L" else (8, 0)
-            tt(w("A%s%d" % (h, t), b, 512, 4), w("FH", 512 * b, 512 * b + 512).indirect(w(kq, o, o + 8)), w("KB", i + 128 * b, i + 128 * b + 128), OP.add, ["FH%d" % b, "Q%s%d" % (h, t), "KB%s%d" % (h, b)], ["A%s%d.%d" % (h, t, b)])
+            o, i = (24, 512) if h == "L" else (16, 0)
+            tt(w("A%s%d" % (h, t), b, 512, 4), ind(w("FH", 512 * b, 512 * b + 512), w(kq, o, o + 8)), w("KB", i + 128 * b, i + 128 * b + 128), OP.add)
 
-        def pack(h):
-            quant(w("A%sQ%d" % (h, t)), w("A%sS%d" % (h, t)), w("A%s%d" % (h, t)), ["A%s%d.%d" % (h, t, b) for b in range(4)], ["A%sQ%d" % (h, t)])
+        def pack(h): quant(w("A%sQ%d" % (h, t)), w("A%sS%d" % (h, t)), w("A%s%d" % (h, t)))
 
-        lists("K")
-        firsts("K")
-        cp(w("NMR"), w(lr).indirect(w(kq, 8, 16)), [lr, "QK%d" % t], ["NMR"])
-        second("K", 0)
-        lift("EXN", 0, w("NMR"), 128, "NMR")
-        second("K", 1)
-        down(w("NL%d" % t), "EXN", 0, 128, None, "NL%d" % t)
-        second("K", 2)
-        second("K", 3)
+        def turn_rows():
+            act(w("LQK%d" % t, 0, 128), ind(w(lr), w(kq, 24, 32)), AF.Copy)
+            act(w("LQK%d" % t, 128, 256), ind(w(lr), w(kq, 8, 16)), AF.Copy)
+
+        for b in range(4): first("K", b)
+        act(w("NMR"), ind(w(lr), w(kq, 16, 24)), AF.Copy)
+        cp(ind(w("EW"), w(kq, 24, 32)), w("IOTA", 128, 256))
+        for b in range(4): second("K", b)
         pack("K")
-        send(nxt, w("NLI%d" % t), w("NL%d" % t), "nma%d" % t, "nml%d" % t, ["NL%d" % t])
-        send(nxt, w("INQ%d" % t).bitcast(dt.uint8), w("AKQ%d" % t).bitcast(dt.uint8), "cda%d" % t, "cdl%d" % t, ["AKQ%d" % t], 2)
-        send(nxt, w("INS%d" % t), w("AKS%d" % t), "cda%d" % t, "cdl%d" % t, ["AKQ%d" % t], 2)
-        lists("L")
-        if last: turn_rows(t)
-        firsts("L")
-        if last: turn_send(t, prv)
+        lift("EXN", w("NMR"), 128)
+        send(nxt[t], cast(w("INQ%d" % t), dt.uint8), cast(w("AKQ%d" % t), dt.uint8), "cda%d" % t, "cdl%d" % t, 2)
+        send(nxt[t], w("INS%d" % t), w("AKS%d" % t), "cda%d" % t, "cdl%d" % t, 2)
+        if last: turn_rows()
+        for b in range(4): first("L", b)
+        down(w("NL%d" % t), "EXN", 128)
+        send(nxt[t], w("NLI%d" % t), w("NL%d" % t), "nma%d" % t, "nml%d" % t)
+        if last:
+            turn(t)
+            turned(t)
         for b in range(4): second("L", b)
         pack("L")
-        lands(prv, "NLI%d" % t, "nma%d" % t)
-        lands(prv, "INQ%d" % t, "cda%d" % t, 2)
+        if not last: turn_rows()
+        lands(prv[t], [w("NLI%d" % t)], "nma%d" % t)
+        lands(prv[t], [w("INQ%d" % t), w("INS%d" % t)], "cda%d" % t)
 
-        def layer(b, P, q, s, key, o, h):
-            mm(w(P, 0, 128), w("WQ", 128 * b, 128 * b + 128), w("WS", 128 * b, 128 * b + 128), w(q), w(s), True, True, ["WQ", "WS", key], [P])
-            act(w("HS", HW * b + o, HW * b + o + 128), w(P, 0, 128), AF.Copy, 0.03125, [P], ["HS%d%s" % (b, h)])
+        def layer(b, q, s, o):
+            P = w("P" + "ABCD"[b], 0, 128)
+            mm(P, w("WQ", 128 * b, 128 * b + 128), w("WS", 128 * b, 128 * b + 128), w(q), w(s))
+            act(w("HS", HW * b + o, HW * b + o + 128), P, AF.Copy, 0.03125)
 
-        for b in range(4): layer(b, "P%d" % (0, 1, 6, 7)[b], "ALQ%d" % t, "ALS%d" % t, "ALQ%d" % t, 128, "L")
-        cp(w("EW").indirect(w(kq, 24, 32)), w("IOTA", 128, 256), ["QL%d" % t, "IOTA"], ["EW"])
-        cp(w("EW").indirect(w("NLI%d" % t)), w("IOTA", 0, 128), ["NLI%d" % t, "IOTA"], ["EW"])
-        lift("EXE", 0, w("EW"), 512, "EW")
-        down(w("EL"), "EXE", 0, 512, None, "EL")
-        for b in range(4): layer(b, "P%d" % (2 + b), "INQ%d" % t, "INS%d" % t, "INQ%d" % t, 0, "K")
-        for b in range(4):
-            tt(w("XN%d" % t, b, 2048, 4), w("HS", HW * b, HW * b + HW).indirect(w("EL")), w("FB", 512 * b, 512 * b + 512), OP.add, ["HS%dK" % b, "HS%dL" % b, "HSZ%d" % b, "EL", "FB%d" % b], ["XN%d.%d" % (t, b)])
-        if not last: turn_rows(t)
+        for b in range(4): layer(b, "ALQ%d" % t, "ALS%d" % t, 128)
+        if not last: turn(t)
+        else: quant(w("VQ"), w("VQS"), w("VB"))
+        cp(ind(w("EW"), w("NLI%d" % t)), w("IOTA", 0, 128))
+        lift("EXE", w("EW"), 512)
+        down(w("EL"), "EXE", 512)
+        for b in range(4): layer(b, "INQ%d" % t, "INS%d" % t, 0)
+        xn = "XN%d" % t
+        for h in (1, 0):
+            o, el = 256 * h, w("EL", 16 * h, 16 * h + 16)
+            for b in range(nv, 4): act(w("GB", 512 * (b - 1) + o, 512 * (b - 1) + o + 256), ind(w("HS", HW * b, HW * b + HW), el), AF.Copy)
+            for b in range(nv): tt(w(xn, 4 * o + b, 4 * o + 1024, 4), ind(w("HS", HW * b, HW * b + HW), el), w("FB", 512 * b + o, 512 * b + o + 256), OP.add)
+            for b in range(nv, 4): tt(w(xn, 4 * o + b, 4 * o + 1024, 4), w("GB", 512 * (b - 1) + o, 512 * (b - 1) + o + 256), w("P%d" % b, o, o + 256), OP.add)
+            if h or last: pack_x(t + 1, h)
+            if last:
+                q, s = xq(t + 1, h)
+                P = w("P" + "AB"[h], 0, 256)
+                mm(P, w("VQ"), w("VQS"), q, s)
+                dma("y", hbm(T.oc[:, 4 * o:4 * o + 1024]), cast(q, dt.uint8), "st", 13)
+                for k in range(4):
+                    dma("y", hbm(T.osc[4 * k:4 * k + 4, o:o + 256]), w("XS", 512 * ROUNDS + o, 512 * ROUNDS + o + 256, rows=slice(32 * k, 32 * k + 4)), "st", 13)
 
     t = ROUNDS - 1
-    lands(T.cores[(rank + 2 ** t) % N], "TRX%d" % t, "tra%d" % t)
-    dma("y", T["TRW%d" % t][0:128:16, :], w("TRX%d" % t), "trx%d" % t, 1, ["TRX%d" % t], ["TRW%d" % t])
-    stores, e = 13, 512 * ROUNDS
-    for h in range(2):
-        o = e + 256 * h
-        quant(w("XQ", o, o + 256), w("XS", o, o + 256), w("XN%d" % t, 1024 * h, 1024 * h + 1024), ["XN%d.%d" % (t, b) for b in range(4)], ["XQe%d" % h])
-        mm(w("P%d" % (6 + h), 0, 256), w("VQ"), w("VQS"), w("XQ", o, o + 256), w("XS", o, o + 256), True, True, ["VQ", "XQe%d" % h], ["P%d" % (6 + h)])
-        dma("y", T.oc[:, 1024 * h:1024 * h + 1024], w("XQ", o, o + 256).bitcast(dt.uint8), "st", stores, ["XQe%d" % h], ["oc%d" % h])
-    act(w("YS", 0, 256), w("P6", 0, 256), AF.Copy, 1.0, ["P6"], ["YSa"])
-    cp(w("YS", 256, 512), w("P7", 0, 256), ["P7"], ["YSb"])
-    dma("s", T.y[:, 0:256], w("YS", 0, 256), "st", stores, ["YSa"], ["ya"])
-    dma("y", T.y[:, 256:512], w("YS", 256, 512), "st", stores, ["YSb"], ["yb"])
-    act(w("LKO"), w("TRW%d" % t).indirect(w("LL%d" % t)), AF.Copy, 1.0, ["TRW%d" % t, "LL%d" % t], ["LKO"])
-    dma("s", T.lk[:, :], T.LKO[0:128:16, :], "st", stores, ["LKO"], ["lk"])
-    for k in range(4):
-        for h in range(2):
-            o = e + 256 * h
-            dma("y", T.osc[4 * k:4 * k + 4, 256 * h:256 * h + 256], T.XS[32 * k:32 * k + 4, o:o + 256], "st", stores, ["XQe%d" % h], ["osc%d%d" % (k, h)])
+    act(w("YS", 256, 512), w("PB", 0, 256), AF.Copy)
+    dma("s", hbm(T.y[:, 256:512]), w("YS", 256, 512), "st", 13)
+    cp(w("YS", 0, 256), w("PA", 0, 256))
+    lands(nxt[t], [w("TRX%d" % t)], "tra%d" % t)
+    dma("s", hbm(T.y[:, 0:256]), w("YS", 0, 256), "st", 13)
+    dma("y", hbm(T.lk[:, :]), w("TRX%d" % t), "st", 13)
     for sem in total:
         if know["g"].get(sem, 0) < total[sem]: g.wait_ge(T.sem[sem], total[sem])

@@ -5,10 +5,12 @@ N, ROUNDS = 4, 2
 HW = 264
 BIG = 2.0 ** 26
 FAR = 1e25
-C0 = 23
+C0 = 24
 JL = 8 * C0
-NS = (3, 2)
-AT7, AT6 = 16, 4
+NS = (2, 2)
+EARLY = (False, True)
+TAIL = ((0, 256),)
+AT = {7: 16, 6: 3, 5: 1}
 TC = [max(128, 64 * (k + 1)) for k in range(8)]
 TO = [sum(TC[:k]) for k in range(9)]
 CODES, F32, BF, F16 = "float8_e4m3fn_x4", "float32", "bfloat16", "float16"
@@ -20,11 +22,15 @@ def buf(names, cols, dtype, where="sbuf"):
     for n in names.split(): SCRATCH[n] = (where, [128, cols], dtype)
 
 
-buf("X0 XN0 XN1 EB FH", 2048, BF)
+buf("X0 XN0 XN1 FH", 2048, BF)
 buf("FB", 1024, BF)
-buf("UB VB ON OB AROW KM RZ RD0 BR0 BR1 TB0 TB1 AK0 AK1 AL0 AL1", 512, BF)
-buf("UQ UR UT VQ OQ AKQ0 AKQ1 ALQ0 ALQ1 INQ0 INQ1", 128, CODES)
-buf("UQS URS UTS VQS OQS AKS0 AKS1 ALS0 ALS1 INS0 INS1", 128, "uint8")
+buf("UB VB OB RD0 BR0 BR1 TB0 TB1 AK0 AK1 AL0 AL1", 512, BF)
+buf("ON AROW KM RZ", 256, BF)
+buf("Z", 520, BF)
+buf("UQ UR UT VQ OQ AKQ0 AKQ1", 128, CODES)
+buf("UQS URS UTS VQS OQS AKS0 AKS1", 128, "uint8")
+buf("SQ0 SQ1", 256, CODES)
+buf("SS0 SS1", 256, "uint8")
 buf("WQ EQ", 512, CODES)
 buf("WS EQS", 512, "uint8")
 buf("XQ", 512 * 3, CODES)
@@ -34,11 +40,13 @@ buf("QS", TO[8], "uint8")
 buf("BT", 4 * TO[8], BF)
 buf("SG", 3 * 512, BF)
 buf("JK", C0 * JL, F16)
-buf("I1 OWS RD", 512, F16)
+buf("I1", 520, F16)
+buf("OWS RD", 512, F16)
 buf("F5 FM VP", 264, F16)
 buf("KB", 1024, BF)
 buf("LINKI", 32, "int32")
-buf("CT", 528, F32)
+buf("CX", 256, F32)
+buf("PK", 128, F32)
 buf("SM", 16, F32)
 buf("INT", 24, "int32")
 buf("UO", 16, "uint16")
@@ -47,7 +55,8 @@ buf("WK", 192, F32)
 buf("EX", 1920, F32)
 buf("II", 48, "int32")
 buf("U16", 80, "uint16")
-buf("IOTA PK MSK H PAY POS POSA PKD EW YS LR0 LR1 TR0 TR1 NR0 NR1", 512, F32)
+buf("IOTA", 520, F32)
+buf("MSK H PAY POS POSA PKD EW YS LR0 LR1 NR0 NR1", 512, F32)
 buf("FO LQK0 LQK1", 256, F32)
 buf("NMR", 128, F32)
 buf("HS", 4 * HW, F32)
@@ -59,9 +68,8 @@ buf("BRD0 BRD1 BRX0 BRX1", 32, BF, "dram")
 buf("PA PB PC PD P0 P1 P2 P3", 512, F32, "psum")
 
 PIECE = {
-    "CX": ("CT", 0, 512), "J16": ("CT", 512, 16),
-    "PM": ("SM", 0, 2), "MC": ("SM", 2, 1), "UP": ("SM", 3, 1), "NUP": ("SM", 4, 1), "NUQ": ("SM", 5, 1), "R15": ("SM", 6, 1),
-    "GM": ("SM", 8, 2), "E4": ("SM", 12, 4),
+    "PM": ("SM", 0, 2), "MC": ("SM", 2, 1), "UP": ("SM", 3, 1), "NUP": ("SM", 4, 1), "NUQ": ("SM", 5, 1), "R15": ("SM", 6, 1), "PU": ("SM", 7, 1),
+    "GM": ("SM", 8, 2), "MK": ("SM", 10, 1), "E4": ("SM", 12, 2),
     "UOI": ("INT", 0, 16), "PI": ("INT", 16, 2), "PJ": ("INT", 18, 2), "PG": ("INT", 20, 2),
     "T1": ("WK", 0, 32), "T3": ("WK", 32, 32), "RK": ("WK", 64, 32), "NA": ("WK", 96, 16), "NB": ("WK", 112, 16), "NN": ("WK", 128, 16),
     "JS": ("WK", 144, 16), "TOT": ("WK", 160, 1),
@@ -118,7 +126,7 @@ def rank_program(g, core, T, topo):
         for n, c in o:
             if SCRATCH[n][0] == "psum": need |= set(i for i, _ in read[n])
             if q != "t": need |= set(wrote[n][c].tolist())
-            need |= set(i for i, d in read[n] if np.intersect1d(c, d).size)
+            need |= set(i for i, d in read[n] if d[c].any())
         need.discard(-1)
         for i in sorted(need, key=lambda i: -tokens[i][2]):
             _, s, val, seen = tokens[i]
@@ -132,8 +140,12 @@ def rank_program(g, core, T, topo):
         tokens.append(token)
         for n, c in o:
             wrote[n][c] = len(tokens) - 1
-            read[n] = [] if SCRATCH[n][0] == "psum" else [(i, np.setdiff1d(d, c)) for i, d in read[n] if np.setdiff1d(d, c).size]
-        for n, c in r: read[n].append((len(tokens) - 1, c))
+            for _, d in read[n]: d[c] = False
+            read[n] = [] if SCRATCH[n][0] == "psum" else [(i, d) for i, d in read[n] if d.any()]
+        for n, c in r:
+            d = np.zeros(SCRATCH[n][1][1], bool)
+            d[c] = True
+            read[n].append((len(tokens) - 1, d))
 
     def op(q, call, ins, outs):
         r, o = sides(ins, outs)
@@ -184,32 +196,31 @@ def rank_program(g, core, T, topo):
     def act(out, in_, func, scale=1.0, bias=None, accum=None):
         if accum is not None: op("s", lambda: S.activation(out[0], in_[0], func, accum_out=accum[0]), [in_], [out, accum])
         elif bias is None and scale == 1.0: op("s", lambda: S.activation(out[0], in_[0], func), [in_], [out])
-        elif bias is None: op("s", lambda: S.activation(out[0], in_[0], func, scale=scale), [in_], [out])
-        else: op("s", lambda: S.activation(out[0], in_[0], func, bias=raw(bias), scale=scale), [in_, bias], [out])
+        elif bias is None: op("s", lambda: S.activation(out[0], in_[0], func, scale=raw(scale)), [in_, scale], [out])
+        else: op("s", lambda: S.activation(out[0], in_[0], func, bias=raw(bias), scale=raw(scale)), [in_, bias, scale], [out])
 
-    def lift(ex, row, n): scan(w(ex, 0, n), w("CX", 0, n), row, OP.mult, OP.add)
-    def top(ex, n): return w(ex, 15, n, 16)
-    def down(out, ex, n, more=None): ts(out, top(ex, n), w("MC"), more, OP.mult, None if more is None else OP.add)
+    def lift(ex, row, a, b): scan(w(ex, a, b), w("CX", 0, b - a), w(row, a, b), OP.mult, OP.add)
+    def top(ex, a, b): return w(ex, a + 15, b, 16)
+    def down(out, ex, a, b, more=None): ts(out, top(ex, a, b), w("MC"), more, OP.mult, None if more is None else OP.add)
 
     rows8 = slice(0, 128, 16)
     nxt = [T.cores[(rank + 2 ** t) % N] for t in range(ROUNDS)]
     prv = [T.cores[(rank - 2 ** t) % N] for t in range(ROUNDS)]
 
-    dma("y", w("X0", 1024, 2048), hbm(T.x[:, 1024:2048]), "ldx1", 1)
     dma("s", w("UB"), hbm(T.u[:, :]), "ldu", 1)
-    dma("s", w("LINKI"), hbm(T.link[:, :]), "ldk", 1)
+    dma("y", w("LINKI"), hbm(T.link[:, :]), "ldk", 1)
+    dma("y", w("X0", 1024, 2048), hbm(T.x[:, 1024:2048]), "ldx1", 1)
     dma("y", w("X0", 0, 1024), hbm(T.x[:, 0:1024]), "ldx0", 1)
-    dma("y", w("VB"), hbm(T.v[:, :]), "ldv", 1, [w("X0")])
-    dma("y", cast(w("WQ"), dt.uint8), hbm(T.wc[:, :]), "ldw", 2)
-    dma("y", w("WS"), hbm(T.ws[:, :]), "ldw", 2)
 
+    def pad(k): return w("BT", 4 * TO[k] + 64 * (4 * k + 1), 4 * TO[k + 1])
+    r16 = slice(0, 16)
     iotai(w("PI"), [[0, 2]], 0, 1)
     iotai(w("UOI"), [[1, 2], [16, 8]], 0, 0)
-    iota(w("AROW"), [[0, 32], [1, 16]], 0, 0)
-    iota(w("I1"), [[1, 512]], 1, 0)
-    iota(w("E4"), [[1, 4]], 1, 4)
-    iota(w("IOTA"), [[1, 512]], 0, 0)
-    for k in range(8): fill(w("BT", 4 * TO[k] + 64 * (4 * k + 1), 4 * TO[k + 1]), 0.0)
+    iota(w("AROW"), [[0, 16], [1, 16]], 0, 0)
+    iota(w("E4"), [[0, 2]], 4, 4)
+    iota(w("IOTA"), [[1, 520]], 0, 0)
+    fill(pad(0), 0.0)
+    fill(w("ON", rows=slice(0, 32)), 1.0)
     ts(w("PJ"), w("PI"), 15, None, OP.bitwise_and)
     ts(w("PG"), w("PI"), 112, None, OP.bitwise_and)
     cp(w("UO"), w("UOI"))
@@ -217,64 +228,62 @@ def rank_program(g, core, T, topo):
     pm = w("PM", 0, 1)
     ts(w("GM"), w("PG"), -4.0, -31.5, OP.mult, OP.add)
     fill(w("JK", JL - 2, JL), 0.0)
-    fill(w("F5"), 0.0)
+    fill(w("F5", 256, 258), 0.0)
     fill(w("FM", 0, 2), 0.0)
+    fill(w("HS", 256, 4 * HW, HW), 0.0)
+    for k in range(7, 0, -1): act(pad(k), w("BT", 64, 256), AF.Copy)
     ts(w("KM"), w("AROW"), pm, -2.0 * FAR, OP.not_equal, OP.mult)
     ts(w("RZ"), w("AROW"), 0.5, 2.0 * FAR, OP.subtract, OP.mult)
-    fill(w("ON", rows=slice(0, 32)), 1.0)
     ts(w("MC"), pm, 15.0, 1.0 - 1.0 / BIG, OP.is_equal, OP.mult)
     ts(w("UP"), pm, 15.0, BIG, OP.not_equal, OP.mult)
     ts(w("R15"), pm, -1.0, 15.25, OP.mult, OP.add)
-    quant(w("UQ"), w("UQS"), w("UB"))
     ts(w("MC"), w("MC"), 1.0 / BIG, None, OP.max)
     ts(w("UP"), w("UP"), 1.0, None, OP.max)
+    quant(w("UQ"), w("UQS"), w("UB"))
+    select(w("CX", rows=r16), w("ON", rows=r16), [[0, 16], [1, 16]], OP.is_gt, 0.0, 0, -1)
+    select(w("CX", rows=r16), w("CX", rows=r16), [[0, 16], [1, 16]], OP.not_equal, BIG, -1, -1)
+    dma("y", w("VB"), hbm(T.v[:, :]), "ldv", 1, [w("X0")])
+    for i in range(1, 8): dma("y", w("CX", rows=slice(16 * i, 16 * i + 16)), w("CX", rows=r16), "ldc", 7)
+    dma("y", cast(w("WQ"), dt.uint8), hbm(T.wc[:, :]), "ldw", 2)
+    dma("y", w("WS"), hbm(T.ws[:, :]), "ldw", 2)
 
     def pick_u(q, o):
         cp(cast(w(q), dt.uint32), ind(cast(w("UQ"), dt.uint32), w("UO", o, o + 8)))
         act(w(q + "S"), ind(w("UQS"), w("UO", o, o + 8)), AF.Copy)
 
-    def unit(b): ts(w("EB", 512 * b, 512 * b + 512), w("I1"), w("E4", b, b + 1), None, OP.is_equal)
     def xq(t, h): return w("XQ", 512 * t + 256 * h, 512 * t + 256 * h + 256), w("XS", 512 * t + 256 * h, 512 * t + 256 * h + 256)
     def pack_x(t, h): quant(*xq(t, h), w("XN%d" % (t - 1) if t else "X0", 1024 * h, 1024 * h + 1024))
+    def unit(b): quant(w("EQ", 128 * b, 128 * b + 128), w("EQS", 128 * b, 128 * b + 128), w("Z", 3 - b, 515 - b))
 
-    pick_u("UR", 0)
-    pack_x(0, 1)
     cp(w("LL0"), w("LINKI"))
     send(nxt[0], w("LI0"), w("LL0"), "lia0", "lil0")
+    pick_u("UR", 0)
+    act(w("SG", 0, 512), w("IOTA", 0, 512), AF.Abs, 1.0, w("GM", 0, 1))
     pick_u("UT", 8)
-    act(w("SG", 0, 512), w("IOTA"), AF.Abs, 1.0, w("GM", 0, 1))
-    act(w("LR0"), ind(w("IOTA"), w("LL0")), AF.Copy)
-    act(w("TR0"), w("LR0"), AF.Copy)
-    ts(w("NUP"), w("UP"), -1.0, None, OP.mult)
-    ts(w("NUQ"), w("UP"), -256.0, None, OP.mult)
-    for b in range(4): fill(w("HS", HW * b + 256, HW * b + HW), 0.0)
-    for b in range(4): unit(b)
-
-    def later_constants():
-        r16 = slice(0, 16)
-        select(w("CX", rows=r16), w("ON", rows=r16), [[0, 32], [1, 16]], OP.is_gt, 0.0, 0, -1)
-        select(w("CX", rows=r16), w("CX", rows=r16), [[0, 32], [1, 16]], OP.not_equal, BIG, -1, -1)
-        iota(w("J16", rows=r16), [[16, 16]], 0, 1)
-        iota(w("RD0"), [[-16, 32], [1024, 16]], 0, 0)
-
-    def copy_constants():
-        for i in range(1, 8): dma("y", w("CT", rows=slice(16 * i, 16 * i + 16)), w("CT", rows=slice(0, 16)), "ldc", 7)
+    ts(w("I1"), w("IOTA"), 1.0, None, OP.add)
+    pack_x(0, 1)
+    ts(w("Z"), w("I1"), w("E4", 0, 1), None, OP.is_equal)
+    ts(w("OB"), w("SG", 0, 512), 32.0, None, OP.is_lt)
+    act(w("NUP"), w("UP"), AF.Copy, -1.0)
+    act(w("NUQ"), w("UP"), AF.Copy, -256.0)
+    act(w("MK"), w("MC"), AF.Copy, 1.0 / 512.0)
+    act(w("PU"), pm, AF.Copy, w("UP"))
+    act(w("JS"), w("IOTA", 0, 256, 16), AF.Identity, w("UP"), w("PU"))
+    unit(0)
+    unit(1)
 
     def spread(n, src, sem):
         for a in range(16): dma("y", w(n, rows=slice(a, 128, 16)), w(src), sem, 16)
 
-    def turn(t):
-        kq, n = "KQ%d" % t, "LQK%d" % t
-        cp(ind(w("TR%d" % t), w(kq, 8, 16)), w(n, 0, 128))
-        cp(ind(w("TR%d" % t), w(kq, 24, 32)), w(n, 128, 256))
+    def turn(t, h):
+        cp(ind(w("LR%d" % t), w("KQ%d" % t, 8 + 16 * h, 16 + 16 * h)), w("LQK%d" % t, 128 * h, 128 * h + 128))
 
     def turned(t):
         lands(prv[t], [w("LI%d" % t)], "lia%d" % t)
-        act(w("NR%d" % t), ind(w("TR%d" % t), w("LI%d" % t)), AF.Copy)
+        act(w("NR%d" % t), ind(w("LR%d" % t), w("LI%d" % t)), AF.Copy)
         dma("y", w("TRD%d" % t), w("NR%d" % t, rows=rows8), "tro%d" % t, 1)
         send(prv[t], w("TRX%d" % t), w("TRD%d" % t), "tra%d" % t, "trl%d" % t)
 
-    later_constants()
     for t in range(ROUNDS):
         last = t == ROUNDS - 1
         xc, xs = w("XQ", 512 * t, 512 * t + 512), w("XS", 512 * t, 512 * t + 512)
@@ -284,12 +293,11 @@ def rank_program(g, core, T, topo):
         mm(w("PA"), w("UR"), w("URS"), xc, xs)
         mm(w("PC"), w("UR"), w("URS"), xc, xs)
         mm(w("PB"), w("UT"), w("UTS"), xc, xs)
-        tt(w("MSK", 256, 512), w("PD", 0, 256), w("KM", 256, 512), OP.add)
-        if t == 0: ts(w("OB"), w("SG", 0, 512), 32.0, None, OP.is_lt)
-        scan(w("H", 256, 512), w("RZ", 256, 512), w("MSK", 256, 512), OP.min, OP.max)
-        tt(w("MSK", 0, 256), w("PA", 0, 256), w("KM", 0, 256), OP.add)
-        if t == 0: quant(w("OQ"), w("OQS"), w("OB"))
-        scan(w("H", 0, 256), w("RZ", 0, 256), w("MSK", 0, 256), OP.min, OP.max)
+        tt(w("MSK", 256, 512), w("PD", 0, 256), w("KM"), OP.add)
+        if t == 0: unit(2)
+        scan(w("H", 256, 512), w("RZ"), w("MSK", 256, 512), OP.min, OP.max)
+        if t == 0: unit(3)
+        tt(w("MSK", 0, 256), w("PA", 0, 256), w("KM"), OP.add)
 
         def row(c, a, b): return w("BT", 4 * (TO[(c - 1) // 4] + a) + (c - 1) % 4, 4 * (TO[(c - 1) // 4] + b), 4)
         def mine(c): return w("H", 16 * c + 15, 16 * c + 16)
@@ -301,17 +309,20 @@ def rank_program(g, core, T, topo):
         def colsum(k, first, end): mm(w("PD", 0, TC[k]), w("OQ"), w("OQS"), w("QT", TO[k], TO[k + 1]), w("QS", TO[k], TO[k + 1]), first, end)
 
         below(C0 - 1)
+        scan(w("H", 0, 256), w("RZ"), w("MSK", 0, 256), OP.min, OP.max)
+        below(C0 - 2)
         ts(w(br), w("PB"), 0.0, 0.5, OP.is_gt, OP.subtract)
-        if t: turned(t - 1)
         dma("y", w("BRD%d" % t), w(br, rows=rows8), "bro%d" % t, 1)
         send(prv[t], w("BRX%d" % t), w("BRD%d" % t), "bra%d" % t, "brl%d" % t)
-        if t == 0: copy_constants()
         if t:
             lands(nxt[t - 1], [w("TRX%d" % (t - 1))], "tra%d" % (t - 1))
             spread(lr, "TRX%d" % (t - 1), "trx%d" % (t - 1))
         lands(nxt[t], [w("BRX%d" % t)], "bra%d" % t)
         spread(tb, "BRX%d" % t, "tbx%d" % t)
-        if t == 0: iota(w("PK"), [[0, 256], [512, 2]], 0, 0)
+        if t == 0:
+            iota(w("RD0"), [[-16, 32], [1024, 16]], 0, 0)
+            iota(w("PK"), [[0, 64], [512, 2]], 0, 0)
+        iota(w("EW"), [[0, 512]], 256, 0)
 
         sign(31)
         for c in range(30, C0 - 1, -1):
@@ -319,68 +330,73 @@ def rank_program(g, core, T, topo):
             beats(c + 1)
         beats(C0)
         tt(row(32, 0, 512), w("PA"), w("H"), OP.is_le)
-        waiting = []
-        started = [False]
+        rowsum(C0 - 1)
+        if t == 0: quant(w("OQ"), w("OQS"), w("OB"))
+        waiting, packed = [], []
 
-        def done(k, end=False):
+        def done(k):
             pack_b(k)
             waiting.append(k)
-            if k == 7: started[0] = True
-            if started[0]:
-                for j in sorted(waiting, reverse=True): colsum(j, j == 7, end and j == min(waiting))
+            packed.append(k)
+            if 7 in packed:
+                for j in sorted(waiting, reverse=True): colsum(j, j == 7, len(packed) == 8 and j == min(waiting))
                 waiting.clear()
 
-        for c in range(C0 - 2, 0, -1):
+        for c in range(C0 - 3, 0, -1):
             below(c)
-            if c == 8: scan(w("RD"), w("RD0"), row(32, 0, 512), OP.min, OP.add)
             rowsum(c + 1)
-            if c % 4 == 0 and 4 <= c < 20: done(c // 4)
-            if c == AT7: done(7)
-            if c == AT6: done(6)
-            if c == 12 and t == 0:
-                quant(w("EQ"), w("EQS"), w("EB"))
+            if c % 4 == 0 and c + 4 < C0: done(c // 4)
+            for k in AT:
+                if AT[k] == c and 4 * k + 4 >= C0: done(k)
             if c == 12:
                 for b in range(4): mm(w("P%d" % b), w("EQ", 128 * b, 128 * b + 128), w("EQS", 128 * b, 128 * b + 128), xc, xs)
-            if c == 6 and t:
-                lift("EXE", w(lr), 512)
-            if c == 5 and t:
-                down(w(ll), "EXE", 512)
+            if c == 7: scan(w("RD"), w("RD0"), row(32, 0, 512), OP.min, OP.add)
+            if c == 6 and t: lift("EXE", lr, 0, 256)
+            if c == 5 and t: lift("EXE", lr, 256, 512)
+            if c == 4 and t:
+                down(w(ll), "EXE", 0, 512)
                 send(nxt[t], w("LI%d" % t), w(ll), "lia%d" % t, "lil%d" % t)
-        iota(w("EW"), [[0, 512]], 256, 0)
-        done(0)
+            if c == 2: scan(w("OWS"), w("I1", 0, 512), w(br), OP.max, OP.mult)
         rowsum(1)
-        scan(w("OWS"), w("I1"), w(br), OP.max, OP.mult)
-        done(5, True)
-        tt(w("T1", 0, C0), w("JK", JL - 1, JL * C0, JL), w("RD", 15, 16 * C0, 16), OP.add)
+        done(0)
         tt(w("T1", C0, 32), w("RS", C0, 32), w("RD", 16 * C0 + 15, 512, 16), OP.add)
-        if t == 0: ts(w("JS"), w("J16"), w("UP"), None, OP.mult)
-        tt(w("PAY"), ind(w(tb), w(ll)), w("OWS"), OP.mult)
-        lift("EXA", w("PD"), 512)
+        tt(w("T1", 0, C0), w("JK", JL - 1, JL * C0, JL), w("RD", 15, 16 * C0, 16), OP.add)
+        tt(w("PAY", 0, 256), ind(w(tb), w(ll, 0, 16)), w("OWS", 0, 256), OP.mult)
         ts(w("T3"), w("T1"), w("UP"), None, OP.mult)
+        lift("EXA", "PD", 0, 256)
+        lift("EXA", "PD", 256, 512)
         for b in range(4): act(w("FH", 512 * b, 512 * b + 512), w("P%d" % b), AF.Copy, 0.5)
-        tt(w("RK"), top("EXA", 512), w("T3"), OP.subtract)
+        tt(w("RK", 0, 16), top("EXA", 0, 256), w("T3", 0, 16), OP.subtract)
+        tt(w("RK", 16, 32), top("EXA", 256, 512), w("T3", 16, 32), OP.subtract)
+        tt(w("PAY", 256, 512), ind(w(tb), w(ll, 16, 32)), w("OWS", 256, 512), OP.mult)
         ts(w("RKU"), w("RK"), w("MC"), w("R15"), OP.mult, OP.add)
+        if t == 0: act(w(lr), ind(w("IOTA", 0, 512), w(ll)), AF.Copy)
         cp(ind(w("POS"), w("RKU")), w("PAY"))
         act(w("POSA"), w("POS"), AF.Abs, 4.0)
-        ts(w("F5", 1, 257), w("POS", 1, 512, 2), 0.0, 512.0, OP.is_lt, OP.mult)
-        ts(w("FM", 1, 257), w("F5", 1, 257), -511.0 / 512.0, None, OP.mult)
-        scan(w("VP", 0, 257), w("FM", 0, 257), w("F5", 1, 258), OP.add, OP.add)
-        lift("EXB", w("VP", 0, 256), 256)
+        ts(w("F5", 0, 256), w("POS", 1, 512, 2), 0.0, 512.0, OP.is_lt, OP.mult)
+        ts(w("FM", 1, 257), w("POS", 1, 512, 2), 0.0, -511.0, OP.is_lt, OP.mult)
+        scan(w("VP", 0, 257), w("FM", 0, 257), w("F5", 0, 257), OP.add, OP.add)
+
+        def pair(i): scan(w("PKD", 128 * i, 128 * i + 128), w("PK"), w("POSA", 128 * i, 128 * i + 128), OP.mult, OP.add)
+
+        pair(0)
+        lift("EXB", "VP", 0, 256)
         ts(w("TOT"), w("VP", 256, 257), w("NUP"), w("NUQ"), OP.mult, OP.add)
-        tt(w("NB"), w("JS"), top("EXB", 256), OP.subtract)
-        ts(w("NA"), top("EXB", 256), w("TOT"), None, OP.add)
-        scan(w("PKD"), w("PK"), w("POSA"), OP.mult, OP.add)
+        pair(1)
+        tt(w("NB"), w("JS"), top("EXB", 0, 256), OP.subtract)
+        ts(w("NA"), top("EXB", 0, 256), w("TOT"), None, OP.add)
+        pair(2)
         tt(w("NN"), w("NA"), w("NB"), OP.max)
+        pair(3)
         ts(w("NU"), w("NN"), w("MC"), 0.25, OP.mult, OP.add)
         cp(ind(w("FO"), w("NU")), w("PKD", 1, 512, 2))
         nv = 4 - NS[t]
         for b in range(nv): act(w("FB", 512 * b, 512 * b + 512), w("P%d" % b), AF.Copy)
-        if t: act(w("TR%d" % t), w(lr), AF.Copy)
-        lift("EXK", w("FO"), 256)
-        down(w("KQV"), "EXK", 256, -513.0)
-        ts(w("KQI", 0, 16), w("KQV"), 9, None, OP.arith_shift_right)
-        ts(w("KQI", 16, 32), w("KQV"), 511, None, OP.bitwise_and)
-        cp(w(kq), w("KQI"))
+        lift("EXK", "FO", 0, 256)
+        down(w("KQV"), "EXK", 0, 256, -513.0)
+        ts(w(kq, 0, 16), top("EXK", 0, 256), w("MK"), -513.0 / 512.0 - 0.499, OP.mult, OP.add)
+        ts(w("KQI", 0, 16), w("KQV"), 511, None, OP.bitwise_and)
+        cp(w(kq, 16, 32), w("KQI", 0, 16))
 
         def first(h, b):
             o, i = (8, 512) if h == "L" else (0, 0)
@@ -397,59 +413,87 @@ def rank_program(g, core, T, topo):
             act(w("LQK%d" % t, 128, 256), ind(w(lr), w(kq, 8, 16)), AF.Copy)
 
         for b in range(4): first("K", b)
-        act(w("NMR"), ind(w(lr), w(kq, 16, 24)), AF.Copy)
-        cp(ind(w("EW"), w(kq, 24, 32)), w("IOTA", 128, 256))
-        for b in range(4): second("K", b)
-        pack("K")
-        lift("EXN", w("NMR"), 128)
-        send(nxt[t], cast(w("INQ%d" % t), dt.uint8), cast(w("AKQ%d" % t), dt.uint8), "cda%d" % t, "cdl%d" % t, 2)
-        send(nxt[t], w("INS%d" % t), w("AKS%d" % t), "cda%d" % t, "cdl%d" % t, 2)
-        if last: turn_rows()
-        for b in range(4): first("L", b)
-        down(w("NL%d" % t), "EXN", 128)
+        cp(w("NMR"), ind(w(lr), w(kq, 16, 24)))
+        second("K", 0)
+        lift("EXN", "NMR", 0, 128)
+        second("K", 1)
+        down(w("NL%d" % t), "EXN", 0, 128)
         send(nxt[t], w("NLI%d" % t), w("NL%d" % t), "nma%d" % t, "nml%d" % t)
-        if last:
-            turn(t)
-            turned(t)
+        second("K", 2)
+        second("K", 3)
+        pack("K")
+        vq, vs = "SQ%d" % t, "SS%d" % t
+        send(nxt[t], cast(w(vq, 0, 128), dt.uint8), cast(w("AKQ%d" % t), dt.uint8), "cda%d" % t, "cdl%d" % t, 2)
+        send(nxt[t], w(vs, 0, 128), w("AKS%d" % t), "cda%d" % t, "cdl%d" % t, 2)
+        cp(ind(w("EW"), w(kq, 24, 32)), w("IOTA", 128, 256))
+        if EARLY[t]:
+            turn_rows()
+            turn(t, 0)
+            turn(t, 1)
+        for b in range(4): first("L", b)
+        if EARLY[t]: turned(t)
+        else: turn_rows()
         for b in range(4): second("L", b)
-        pack("L")
-        if not last: turn_rows()
+        quant(w(vq, 128, 256), w(vs, 128, 256), w("AL%d" % t))
         lands(prv[t], [w("NLI%d" % t)], "nma%d" % t)
-        lands(prv[t], [w("INQ%d" % t), w("INS%d" % t)], "cda%d" % t)
-
-        def layer(b, q, s, o):
-            P = w("P" + "ABCD"[b], 0, 128)
-            mm(P, w("WQ", 128 * b, 128 * b + 128), w("WS", 128 * b, 128 * b + 128), w(q), w(s))
-            act(w("HS", HW * b + o, HW * b + o + 128), P, AF.Copy, 0.03125)
-
-        for b in range(4): layer(b, "ALQ%d" % t, "ALS%d" % t, 128)
-        if not last: turn(t)
-        else: quant(w("VQ"), w("VQS"), w("VB"))
+        lands(prv[t], [w(vq, 0, 128), w(vs, 0, 128)], "cda%d" % t)
+        for b in range(4): mm(w("P" + "ABCD"[b], 0, 256), w("WQ", 128 * b, 128 * b + 128), w("WS", 128 * b, 128 * b + 128), w(vq), w(vs))
+        def window(b): act(w("HS", HW * b, HW * b + 256), w("P" + "ABCD"[b], 0, 256), AF.Copy, 0.03125)
+        for b in range(nv + 1): window(b)
         cp(ind(w("EW"), w("NLI%d" % t)), w("IOTA", 0, 128))
-        lift("EXE", w("EW"), 512)
-        down(w("EL"), "EXE", 512)
-        for b in range(4): layer(b, "INQ%d" % t, "INS%d" % t, 0)
+        if last: quant(w("VQ"), w("VQS"), w("VB"))
+        if not EARLY[t]: turn(t, 0)
+        lift("EXE", "EW", 256, 512)
+        lift("EXE", "EW", 0, 256)
+        down(w("EL", 16, 32), "EXE", 256, 512)
+        down(w("EL", 0, 16), "EXE", 0, 256)
+        if not EARLY[t]: turn(t, 1)
         xn = "XN%d" % t
-        for h in (1, 0):
-            o, el = 256 * h, w("EL", 16 * h, 16 * h + 16)
-            for b in range(nv, 4): act(w("GB", 512 * (b - 1) + o, 512 * (b - 1) + o + 256), ind(w("HS", HW * b, HW * b + HW), el), AF.Copy)
-            for b in range(nv): tt(w(xn, 4 * o + b, 4 * o + 1024, 4), ind(w("HS", HW * b, HW * b + HW), el), w("FB", 512 * b + o, 512 * b + o + 256), OP.add)
-            for b in range(nv, 4): tt(w(xn, 4 * o + b, 4 * o + 1024, 4), w("GB", 512 * (b - 1) + o, 512 * (b - 1) + o + 256), w("P%d" % b, o, o + 256), OP.add)
-            if h or last: pack_x(t + 1, h)
-            if last:
-                q, s = xq(t + 1, h)
-                P = w("P" + "AB"[h], 0, 256)
-                mm(P, w("VQ"), w("VQS"), q, s)
-                dma("y", hbm(T.oc[:, 4 * o:4 * o + 1024]), cast(q, dt.uint8), "st", 13)
-                for k in range(4):
-                    dma("y", hbm(T.osc[4 * k:4 * k + 4, o:o + 256]), w("XS", 512 * ROUNDS + o, 512 * ROUNDS + o + 256, rows=slice(32 * k, 32 * k + 4)), "st", 13)
 
-    t = ROUNDS - 1
-    act(w("YS", 256, 512), w("PB", 0, 256), AF.Copy)
-    dma("s", hbm(T.y[:, 256:512]), w("YS", 256, 512), "st", 13)
-    cp(w("YS", 0, 256), w("PA", 0, 256))
+        def picked(b, a, e): return ind(w("HS", HW * b, HW * b + HW), w("EL", a // 16, e // 16))
+        def pick(b, a, e): act(w("GB", 512 * (b - 1) + a, 512 * (b - 1) + e), picked(b, a, e), AF.Copy)
+        def new_x(b, a, e):
+            out = w(xn, 4 * a + b, 4 * e, 4)
+            if b < nv: tt(out, picked(b, a, e), w("FB", 512 * b + a, 512 * b + e), OP.add)
+            else: tt(out, w("GB", 512 * (b - 1) + a, 512 * (b - 1) + e), w("P%d" % b, a, e), OP.add)
+
+        for b in range(nv, 4):
+            if b > nv: window(b)
+            pick(b, 256, 512)
+        for b in range(nv, 4): pick(b, 0, 256)
+        for b in range(nv): new_x(b, 256, 512)
+        for b in range(nv): new_x(b, 0, 256)
+        for b in range(nv, 4): new_x(b, 256, 512)
+        pack_x(t + 1, 1)
+        if not last:
+            for b in range(nv, 4): new_x(b, 0, 256)
+            if not EARLY[t]: turned(t)
+
+    t, o = ROUNDS - 1, 512 * ROUNDS
+    stores = 2 * len(TAIL) + 11
+
+    def store(a, e, P):
+        q, s = w("XQ", o + a, o + e), w("XS", o + a, o + e)
+        mm(w(P, 0, e - a), w("VQ"), w("VQS"), q, s)
+        dma("y", hbm(T.oc[:, 4 * a:4 * e]), cast(q, dt.uint8), "st", stores)
+
+    def scales(a, e):
+        for k in range(4): dma("y", hbm(T.osc[4 * k:4 * k + 4, a:e]), w("XS", o + a, o + e, rows=slice(32 * k, 32 * k + 4)), "st", stores)
+
+    store(256, 512, "PA")
+    scales(256, 512)
+    act(w("YS", 256, 512), w("PA", 0, 256), AF.Copy)
+    dma("s", hbm(T.y[:, 256:512]), w("YS", 256, 512), "st", stores)
+    for i, (a, e) in enumerate(TAIL):
+        for b in range(nv, 4): new_x(b, a, e)
+        quant(w("XQ", o + a, o + e), w("XS", o + a, o + e), w(xn, 4 * a, 4 * e))
+        store(a, e, "P" + "BC"[i])
+    scales(0, 256)
+    for i, (a, e) in enumerate(TAIL):
+        if i + 1 < len(TAIL): act(w("YS", a, e), w("P" + "BC"[i], 0, e - a), AF.Copy)
+        else: cp(w("YS", a, e), w("P" + "BC"[i], 0, e - a))
+        dma("s", hbm(T.y[:, a:e]), w("YS", a, e), "st", stores)
     lands(nxt[t], [w("TRX%d" % t)], "tra%d" % t)
-    dma("s", hbm(T.y[:, 0:256]), w("YS", 0, 256), "st", 13)
-    dma("y", hbm(T.lk[:, :]), w("TRX%d" % t), "st", 13)
+    dma("y", hbm(T.lk[:, :]), w("TRX%d" % t), "st", stores)
     for sem in total:
         if know["g"].get(sem, 0) < total[sem]: g.wait_ge(T.sem[sem], total[sem])

@@ -5,14 +5,21 @@ N, ROUNDS = 4, 2
 HW = 264
 BIG = 2.0 ** 26
 FAR = 1e25
-C0 = 24
+C0 = 25
 JL = 8 * C0
-NS = (2, 2)
-EARLY = (False, True)
-TAIL = ((0, 256),)
-AT = {7: 16, 6: 3, 5: 1}
-TC = [max(128, 64 * (k + 1)) for k in range(8)]
+SP = (256, 256)
+COPIES = (4, 2)
+LOW = [15, 14, 13]
+TAIL = ((256, 384), (384, 512))
+LAG = 2
+SPAD = (2, 7)
+MID = ([], [])
+PLAN = ["OQ", "in0", 12, 11, "mask", 10, "hold", 9, 8, 7, "in1", "F", 6, 5, "bits", 16, "S", "T5", "T6", "Z", 24, 23, 22, 21, "s", "T0", "T4", 20, 19, 18, 17, 4, 3, "s", "T3", "T1", 2, 1, "S", "RD", "T7", "T2", "OWS", "R"]
+ORDER = [32, C0 - 1, C0 - 2, C0 - 3] + list(range(31, C0 - 1, -1)) + list(range(C0 - 4, 0, -1))
+TILES = [ORDER[4 * k:4 * k + 4] for k in range(8)]
+TC = [max(128, 16 * max(r)) for r in TILES]
 TO = [sum(TC[:k]) for k in range(9)]
+SLOT = {c: (i // 4, i % 4) for i, c in enumerate(ORDER)}
 CODES, F32, BF, F16 = "float8_e4m3fn_x4", "float32", "bfloat16", "float16"
 
 SCRATCH = {}
@@ -22,10 +29,9 @@ def buf(names, cols, dtype, where="sbuf"):
     for n in names.split(): SCRATCH[n] = (where, [128, cols], dtype)
 
 
-buf("X0 XN0 XN1 FH", 2048, BF)
-buf("FB", 1024, BF)
-buf("UB VB OB RD0 BR0 BR1 TB0 TB1 AK0 AK1 AL0 AL1", 512, BF)
-buf("ON AROW KM RZ", 256, BF)
+buf("X0 XN0 XN1 FH FB", 2048, BF)
+buf("UB VB OA OB RD0 BR0 BR1 TB0 TB1 AK0 AK1 AL0 AL1", 512, BF)
+buf("AROW KM RZ", 256, BF)
 buf("Z", 520, BF)
 buf("UQ UR UT VQ OQ AKQ0 AKQ1", 128, CODES)
 buf("UQS URS UTS VQS OQS AKS0 AKS1", 128, "uint8")
@@ -39,13 +45,12 @@ buf("QT", TO[8], CODES)
 buf("QS", TO[8], "uint8")
 buf("BT", 4 * TO[8], BF)
 buf("SG", 3 * 512, BF)
-buf("JK", C0 * JL, F16)
-buf("I1", 520, F16)
-buf("OWS RD", 512, F16)
+buf("JK", 32 * JL, F16)
+buf("I1 OWS RD", 512, F16)
 buf("F5 FM VP", 264, F16)
 buf("KB", 1024, BF)
 buf("LINKI", 32, "int32")
-buf("CX", 256, F32)
+buf("CT", 260, F32)
 buf("PK", 128, F32)
 buf("SM", 16, F32)
 buf("INT", 24, "int32")
@@ -55,21 +60,24 @@ buf("WK", 192, F32)
 buf("EX", 1920, F32)
 buf("II", 48, "int32")
 buf("U16", 80, "uint16")
-buf("IOTA", 520, F32)
+buf("IOTA", 512, F32)
+buf("T2", 32, F32)
 buf("MSK H PAY POS POSA PKD EW YS LR0 LR1 NR0 NR1", 512, F32)
 buf("FO LQK0 LQK1", 256, F32)
 buf("NMR", 128, F32)
 buf("HS", 4 * HW, F32)
 buf("GB", 3 * 512, F32)
-buf("KQ0 KQ1 LL0 LL1 LI0 LI1", 32, "uint16")
+buf("KQ0 KQ1 LL0 LL1 LI0 LI1 NLL", 32, "uint16")
 buf("NL0 NL1 NLI0 NLI1", 8, "uint16")
-buf("TRD0 TRD1 TRX0 TRX1", 32, F32, "dram")
-buf("BRD0 BRD1 BRX0 BRX1", 32, BF, "dram")
+buf("TRD TRX", 32, F32, "dram")
+buf("BRD0 BRX0", 32 * COPIES[0], BF, "dram")
+buf("BRD1 BRX1", 32 * COPIES[1], BF, "dram")
 buf("PA PB PC PD P0 P1 P2 P3", 512, F32, "psum")
 
 PIECE = {
-    "PM": ("SM", 0, 2), "MC": ("SM", 2, 1), "UP": ("SM", 3, 1), "NUP": ("SM", 4, 1), "NUQ": ("SM", 5, 1), "R15": ("SM", 6, 1), "PU": ("SM", 7, 1),
-    "GM": ("SM", 8, 2), "MK": ("SM", 10, 1), "E4": ("SM", 12, 2),
+    "CX": ("CT", 0, 256), "MC": ("CT", 256, 1), "UP": ("CT", 257, 1),
+    "PM": ("SM", 0, 2), "E8": ("SM", 2, 2), "NUP": ("SM", 4, 1), "NUQ": ("SM", 5, 1), "R15": ("SM", 6, 1), "PU": ("SM", 7, 1),
+    "GM": ("SM", 8, 2), "MK": ("SM", 10, 1), "PN": ("SM", 11, 1), "E4": ("SM", 12, 2),
     "UOI": ("INT", 0, 16), "PI": ("INT", 16, 2), "PJ": ("INT", 18, 2), "PG": ("INT", 20, 2),
     "T1": ("WK", 0, 32), "T3": ("WK", 32, 32), "RK": ("WK", 64, 32), "NA": ("WK", 96, 16), "NB": ("WK", 112, 16), "NN": ("WK", 128, 16),
     "JS": ("WK", 144, 16), "TOT": ("WK", 160, 1),
@@ -89,6 +97,7 @@ def rank_program(g, core, T, topo):
     queue = {"v": g.vector, "s": g.scalar, "t": g.tensor, "g": g, "y": g.sync}
     own = {"v": "cv", "s": "cs", "t": "ct", "g": "cg"}
     count = {"cv": 0, "cs": 0, "ct": 0, "cg": 0}
+    mark = {s: [] for s in count}
     total = {}
     know = {q: {} for q in queue}
     tokens = []
@@ -132,6 +141,9 @@ def rank_program(g, core, T, topo):
             _, s, val, seen = tokens[i]
             if s == sem and s not in count: continue
             if know[q].get(s, 0) >= val: continue
+            if s == own.get(q) and count[s] - LAG > val:
+                val = count[s] - LAG
+                seen = tokens[mark[s][val - 1]][3]
             queue[q].wait_ge(T.sem[s], val)
             know[q][s] = val
             for s2 in seen: know[q][s2] = max(know[q].get(s2, 0), seen[s2])
@@ -154,6 +166,7 @@ def rank_program(g, core, T, topo):
         call().then_inc(T.sem[sem], 1)
         count[sem] += 1
         total[sem] = count[sem]
+        mark[sem].append(len(tokens))
         note((q, sem, count[sem], dict(know[q])), r, o)
 
     def dma(q, out, in_, sem, of, after=()):
@@ -208,44 +221,43 @@ def rank_program(g, core, T, topo):
     prv = [T.cores[(rank - 2 ** t) % N] for t in range(ROUNDS)]
 
     dma("s", w("UB"), hbm(T.u[:, :]), "ldu", 1)
-    dma("y", w("LINKI"), hbm(T.link[:, :]), "ldk", 1)
-    dma("y", w("X0", 1024, 2048), hbm(T.x[:, 1024:2048]), "ldx1", 1)
     dma("y", w("X0", 0, 1024), hbm(T.x[:, 0:1024]), "ldx0", 1)
+    dma("y", w("X0", 1024, 2048), hbm(T.x[:, 1024:2048]), "ldx1", 1)
+    dma("y", w("LINKI"), hbm(T.link[:, :]), "ldk", 1)
 
-    def pad(k): return w("BT", 4 * TO[k] + 64 * (4 * k + 1), 4 * TO[k + 1])
+    def pad(k): return w("BT", 4 * TO[k] + 64 * min(TILES[k]), 4 * TO[k + 1])
     r16 = slice(0, 16)
     iotai(w("PI"), [[0, 2]], 0, 1)
     iotai(w("UOI"), [[1, 2], [16, 8]], 0, 0)
+    iota(w("E8"), [[0, 2]], -63, -8)
+    iota(w("IOTA"), [[1, 512]], 0, 0)
     iota(w("AROW"), [[0, 16], [1, 16]], 0, 0)
-    iota(w("E4"), [[0, 2]], 4, 4)
-    iota(w("IOTA"), [[1, 520]], 0, 0)
+    iota(w("E4"), [[0, 2]], -3, -4)
+    fill(w("JK", JL - 1, JL * 32, JL), 0.0)
+    fill(w("Z", 512, 520), 0.0)
+    fill(w("RS"), 0.0)
     fill(pad(0), 0.0)
-    fill(w("ON", rows=slice(0, 32)), 1.0)
+    zero = 4 * TO[0] + 64 * min(TILES[0])
     ts(w("PJ"), w("PI"), 15, None, OP.bitwise_and)
-    ts(w("PG"), w("PI"), 112, None, OP.bitwise_and)
     cp(w("UO"), w("UOI"))
     cp(w("PM"), w("PJ"))
     pm = w("PM", 0, 1)
-    ts(w("GM"), w("PG"), -4.0, -31.5, OP.mult, OP.add)
-    fill(w("JK", JL - 2, JL), 0.0)
-    fill(w("F5", 256, 258), 0.0)
-    fill(w("FM", 0, 2), 0.0)
-    fill(w("HS", 256, 4 * HW, HW), 0.0)
-    for k in range(7, 0, -1): act(pad(k), w("BT", 64, 256), AF.Copy)
-    ts(w("KM"), w("AROW"), pm, -2.0 * FAR, OP.not_equal, OP.mult)
-    ts(w("RZ"), w("AROW"), 0.5, 2.0 * FAR, OP.subtract, OP.mult)
-    ts(w("MC"), pm, 15.0, 1.0 - 1.0 / BIG, OP.is_equal, OP.mult)
-    ts(w("UP"), pm, 15.0, BIG, OP.not_equal, OP.mult)
-    ts(w("R15"), pm, -1.0, 15.25, OP.mult, OP.add)
-    ts(w("MC"), w("MC"), 1.0 / BIG, None, OP.max)
-    ts(w("UP"), w("UP"), 1.0, None, OP.max)
+    for k in range(1, 8):
+        if k in SPAD: act(pad(k), w("BT", zero, zero + 4 * TC[k] - 64 * min(TILES[k])), AF.Copy)
+        else: fill(pad(k), 0.0)
     quant(w("UQ"), w("UQS"), w("UB"))
-    select(w("CX", rows=r16), w("ON", rows=r16), [[0, 16], [1, 16]], OP.is_gt, 0.0, 0, -1)
-    select(w("CX", rows=r16), w("CX", rows=r16), [[0, 16], [1, 16]], OP.not_equal, BIG, -1, -1)
+    iota(w("CT", rows=r16), [[0, 260]], 1, 0)
+    iota(w("RD0"), [[-16, 32], [1024, 16]], 0, 0)
     dma("y", w("VB"), hbm(T.v[:, :]), "ldv", 1, [w("X0")])
-    for i in range(1, 8): dma("y", w("CX", rows=slice(16 * i, 16 * i + 16)), w("CX", rows=r16), "ldc", 7)
     dma("y", cast(w("WQ"), dt.uint8), hbm(T.wc[:, :]), "ldw", 2)
     dma("y", w("WS"), hbm(T.ws[:, :]), "ldw", 2)
+
+    def lift_constants():
+        select(w("CX", rows=r16), w("CX", rows=r16), [[0, 16], [1, 16]], OP.is_gt, 0.0, 0, -1)
+        select(w("MC", rows=r16), w("MC", rows=r16), [[0, 1]], OP.is_equal, 1.0 / BIG, -15, 1)
+        select(w("CX", rows=r16), w("CX", rows=r16), [[0, 16], [1, 16]], OP.not_equal, BIG, -1, -1)
+        select(w("UP", rows=r16), w("UP", rows=r16), [[0, 1]], OP.is_equal, BIG, -15, 1)
+        for i in range(1, 8): dma("y", w("CT", rows=slice(16 * i, 16 * i + 16)), w("CT", rows=r16), "ldc", 7)
 
     def pick_u(q, o):
         cp(cast(w(q), dt.uint32), ind(cast(w("UQ"), dt.uint32), w("UO", o, o + 8)))
@@ -255,148 +267,192 @@ def rank_program(g, core, T, topo):
     def pack_x(t, h): quant(*xq(t, h), w("XN%d" % (t - 1) if t else "X0", 1024 * h, 1024 * h + 1024))
     def unit(b): quant(w("EQ", 128 * b, 128 * b + 128), w("EQS", 128 * b, 128 * b + 128), w("Z", 3 - b, 515 - b))
 
-    cp(w("LL0"), w("LINKI"))
-    send(nxt[0], w("LI0"), w("LL0"), "lia0", "lil0")
-    pick_u("UR", 0)
-    act(w("SG", 0, 512), w("IOTA", 0, 512), AF.Abs, 1.0, w("GM", 0, 1))
-    pick_u("UT", 8)
-    ts(w("I1"), w("IOTA"), 1.0, None, OP.add)
-    pack_x(0, 1)
-    ts(w("Z"), w("I1"), w("E4", 0, 1), None, OP.is_equal)
-    ts(w("OB"), w("SG", 0, 512), 32.0, None, OP.is_lt)
-    act(w("NUP"), w("UP"), AF.Copy, -1.0)
-    act(w("NUQ"), w("UP"), AF.Copy, -256.0)
-    act(w("MK"), w("MC"), AF.Copy, 1.0 / 512.0)
-    act(w("PU"), pm, AF.Copy, w("UP"))
-    act(w("JS"), w("IOTA", 0, 256, 16), AF.Identity, w("UP"), w("PU"))
-    unit(0)
-    unit(1)
+    def half(t, h, step):
+        P, a = w("P" + "AD"[h], 0, 256), 256 * h
+        if step == 0: mm(P, w("UR"), w("URS"), *xq(t, h))
+        if step == 0 and h == 0 and LOW: mm(w("PC", 0, 256), w("UR"), w("URS"), *xq(t, h))
+        if step == 1: tt(w("MSK", a, a + 256), P, w("KM"), OP.add)
+        if step == 2: scan(w("H", a, a + 256), w("RZ"), w("MSK", a, a + 256), OP.min, OP.max)
 
-    def spread(n, src, sem):
-        for a in range(16): dma("y", w(n, rows=slice(a, 128, 16)), w(src), sem, 16)
+    act(w("GM"), w("PM"), AF.Identity, 8.0, w("E8", 0, 1))
+    pick_u("UR", 0)
+    act(w("OA"), w("IOTA", 0, 512), AF.Abs, 2.0, w("GM", 0, 1))
+    pick_u("UT", 8)
+    pack_x(0, 0)
+    half(0, 0, 0)
+    ts(w("KM"), w("AROW"), pm, -2.0 * FAR, OP.not_equal, OP.mult)
+    act(w("RZ"), w("AROW"), AF.Copy, 2.0 * FAR, -FAR)
+    ts(w("OB"), w("OA"), 64.0, None, OP.is_lt)
+    half(0, 0, 1)
+
+
+    def small_constants():
+        act(w("R15"), pm, AF.Copy, -1.0, 15.25)
+        act(w("PU"), pm, AF.Copy, w("UP"))
+        act(w("NUP"), w("UP"), AF.Copy, -1.0)
+        act(w("NUQ"), w("UP"), AF.Copy, -256.0)
+        act(w("MK"), w("MC"), AF.Copy, 1.0 / 512.0)
+        act(w("JS"), w("IOTA", 0, 256, 16), AF.Identity, w("UP"), w("PU"))
 
     def turn(t, h):
         cp(ind(w("LR%d" % t), w("KQ%d" % t, 8 + 16 * h, 16 + 16 * h)), w("LQK%d" % t, 128 * h, 128 * h + 128))
 
     def turned(t):
-        lands(prv[t], [w("LI%d" % t)], "lia%d" % t)
+        lands(T.cores[(rank - 2 ** t + 2 ** t // 2) % N], [w("LI%d" % t)], "lia%d" % t)
         act(w("NR%d" % t), ind(w("LR%d" % t), w("LI%d" % t)), AF.Copy)
-        dma("y", w("TRD%d" % t), w("NR%d" % t, rows=rows8), "tro%d" % t, 1)
-        send(prv[t], w("TRX%d" % t), w("TRD%d" % t), "tra%d" % t, "trl%d" % t)
+        if t == ROUNDS - 1:
+            dma("y", w("TRD"), w("NR%d" % t, rows=rows8), "tro%d" % t, 1)
+            send(prv[t], w("TRX"), w("TRD"), "tra%d" % t, "trl%d" % t)
 
     for t in range(ROUNDS):
         last = t == ROUNDS - 1
         xc, xs = w("XQ", 512 * t, 512 * t + 512), w("XS", 512 * t, 512 * t + 512)
         ll, lr, kq, br, tb = ("%s%d" % (n, t) for n in ("LL", "LR", "KQ", "BR", "TB"))
-        mm(w("PD", 0, 256), w("UR"), w("URS"), *xq(t, 1))
-        pack_x(t, 0)
-        mm(w("PA"), w("UR"), w("URS"), xc, xs)
-        mm(w("PC"), w("UR"), w("URS"), xc, xs)
-        mm(w("PB"), w("UT"), w("UTS"), xc, xs)
-        tt(w("MSK", 256, 512), w("PD", 0, 256), w("KM"), OP.add)
-        if t == 0: unit(2)
-        scan(w("H", 256, 512), w("RZ"), w("MSK", 256, 512), OP.min, OP.max)
-        if t == 0: unit(3)
-        tt(w("MSK", 0, 256), w("PA", 0, 256), w("KM"), OP.add)
+        def scores(P, n): mm(w(P, 0, n), w("UR"), w("URS"), w("XQ", 512 * t, 512 * t + n), w("XS", 512 * t, 512 * t + n))
+        def unpack(b): mm(w("P%d" % b), w("EQ", 128 * b, 128 * b + 128), w("EQS", 128 * b, 128 * b + 128), xc, xs)
 
-        def row(c, a, b): return w("BT", 4 * (TO[(c - 1) // 4] + a) + (c - 1) % 4, 4 * (TO[(c - 1) // 4] + b), 4)
+        pack_x(t, 1)
+        half(t, 1, 0)
+        scores("P1", 496)
+        mm(w("PB"), w("UT"), w("UTS"), xc, xs)
+        scores("P0", 16 * (C0 - 1))
+        if t == 0:
+            half(0, 0, 2)
+            cp(w("LL0"), w("LINKI"))
+            send(nxt[0], w("LI0"), w("LL0"), "lia0", "lil0")
+
+        def row(c, a, b): return w("BT", 4 * (TO[SLOT[c][0]] + a) + SLOT[c][1], 4 * (TO[SLOT[c][0]] + b), 4)
         def mine(c): return w("H", 16 * c + 15, 16 * c + 16)
-        def sign(c): act(w("SG", 512 * (c % 3), 512 * (c % 3) + 16 * c), w("PC", 0, 16 * c), AF.Sign, -1.0, mine(c))
-        def beats(c): act(row(c, 0, 16 * c), w("SG", 512 * (c % 3), 512 * (c % 3) + 16 * c), AF.Relu, accum=w("RS", c, c + 1))
-        def below(c): ts(row(c, 0, 16 * c), w("PA", 0, 16 * c), mine(c), None, OP.is_lt)
+        srows = LOW + MID[t] + list(range(31, C0 - 1, -1))
+        def signs(c): return w("SG", 512 * (srows.index(c) % 3), 512 * (srows.index(c) % 3) + 16 * c)
+        def sign(c): act(signs(c), w("PC" if c <= 16 else "P1", 0, 16 * c), AF.Sign, -1.0, mine(c))
+        def beats(c): act(row(c, 0, 16 * c), signs(c), AF.Relu, accum=w("RS", c, c + 1))
+        def below(c): ts(row(c, 0, 16 * c), w("PA" if c <= 16 else "P0", 0, 16 * c), mine(c), None, OP.is_lt)
+        def inside(h): tt(row(32, 256 * h, 256 * h + 256), w("P" + "AD"[h], 0, 256), w("H", 256 * h, 256 * h + 256), OP.is_le)
         def rowsum(c): scan(w("JK", JL * (c + 1) - 8 * c, JL * (c + 1)), row(c, 0, 8 * c), row(c, 8 * c, 16 * c), OP.add, OP.add)
         def pack_b(k): quant(w("QT", TO[k], TO[k + 1]), w("QS", TO[k], TO[k + 1]), w("BT", 4 * TO[k], 4 * TO[k + 1]))
         def colsum(k, first, end): mm(w("PD", 0, TC[k]), w("OQ"), w("OQS"), w("QT", TO[k], TO[k + 1]), w("QS", TO[k], TO[k + 1]), first, end)
 
-        below(C0 - 1)
-        scan(w("H", 0, 256), w("RZ"), w("MSK", 0, 256), OP.min, OP.max)
-        below(C0 - 2)
-        ts(w(br), w("PB"), 0.0, 0.5, OP.is_gt, OP.subtract)
-        dma("y", w("BRD%d" % t), w(br, rows=rows8), "bro%d" % t, 1)
-        send(prv[t], w("BRX%d" % t), w("BRD%d" % t), "bra%d" % t, "brl%d" % t)
-        if t:
-            lands(nxt[t - 1], [w("TRX%d" % (t - 1))], "tra%d" % (t - 1))
-            spread(lr, "TRX%d" % (t - 1), "trx%d" % (t - 1))
-        lands(nxt[t], [w("BRX%d" % t)], "bra%d" % t)
-        spread(tb, "BRX%d" % t, "tbx%d" % t)
-        if t == 0:
-            iota(w("RD0"), [[-16, 32], [1024, 16]], 0, 0)
-            iota(w("PK"), [[0, 64], [512, 2]], 0, 0)
-        iota(w("EW"), [[0, 512]], 256, 0)
+        def bits():
+            ts(w(br), w("PB"), 0.0, 0.5, OP.is_gt, OP.subtract)
+            k = 16 // COPIES[t]
+            dma("y", w("BRD%d" % t), w(br, rows=slice(0, 128, k)), "bro%d" % t, 1)
+            send(prv[t], w("BRX%d" % t), w("BRD%d" % t), "bra%d" % t, "brl%d" % t)
+            lands(nxt[t], [w("BRX%d" % t)], "bra%d" % t)
+            for a in range(k): dma("y", w(tb, rows=slice(a, 128, k)), w("BRX%d" % t), "tbx%d" % t, k)
+            if t == 0:
+                lift_constants()
+                iota(w("I1"), [[1, 512]], 1, 0)
+                for z in (w("F5", 256, 257), w("FM", 0, 1)): iota(z, [[0, 1]], 0, 0)
+                iota(w("PK"), [[0, 64], [512, 2]], 0, 0)
+                iota(w("HS", 256, 4 * HW, HW), [[0, 4]], 0, 0)
+            for c in MID[t]: iota(w("JK", JL * (c + 1) - 1, JL * (c + 1)), [[0, 1]], 0, 0)
+            iota(w("EW"), [[0, 512]], 256, 0)
 
-        sign(31)
-        for c in range(30, C0 - 1, -1):
-            sign(c)
-            beats(c + 1)
-        beats(C0)
-        tt(row(32, 0, 512), w("PA"), w("H"), OP.is_le)
-        rowsum(C0 - 1)
-        if t == 0: quant(w("OQ"), w("OQS"), w("OB"))
-        waiting, packed = [], []
+        def scalar_rows(rows):
+            for i, c in enumerate(rows):
+                sign(c)
+                if i: beats(rows[i - 1])
+            if rows: beats(rows[-1])
+
+        scalar_rows(LOW)
+
+        def unit_row():
+            act(w("OA"), w("IOTA", 0, 512), AF.Abs, 1.0, w("E4", 0, 1))
+            act(w("Z", 0, 512), w("OA"), AF.Relu, -1.0, 1.0)
+
+        made, packed, waiting = [], [], []
 
         def done(k):
             pack_b(k)
-            waiting.append(k)
             packed.append(k)
-            if 7 in packed:
-                for j in sorted(waiting, reverse=True): colsum(j, j == 7, len(packed) == 8 and j == min(waiting))
+            waiting.append(k)
+            if 0 in packed:
+                for j in sorted(waiting): colsum(j, j == 0, len(packed) == 8 and j == max(waiting))
                 waiting.clear()
 
-        for c in range(C0 - 3, 0, -1):
-            below(c)
-            rowsum(c + 1)
-            if c % 4 == 0 and c + 4 < C0: done(c // 4)
-            for k in AT:
-                if AT[k] == c and 4 * k + 4 >= C0: done(k)
-            if c == 12:
-                for b in range(4): mm(w("P%d" % b), w("EQ", 128 * b, 128 * b + 128), w("EQS", 128 * b, 128 * b + 128), xc, xs)
-            if c == 7: scan(w("RD"), w("RD0"), row(32, 0, 512), OP.min, OP.add)
-            if c == 6 and t: lift("EXE", lr, 0, 256)
-            if c == 5 and t: lift("EXE", lr, 256, 512)
-            if c == 4 and t:
-                down(w(ll), "EXE", 0, 512)
-                send(nxt[t], w("LI%d" % t), w(ll), "lia%d" % t, "lil%d" % t)
-            if c == 2: scan(w("OWS"), w("I1", 0, 512), w(br), OP.max, OP.mult)
-        rowsum(1)
-        done(0)
-        tt(w("T1", C0, 32), w("RS", C0, 32), w("RD", 16 * C0 + 15, 512, 16), OP.add)
-        tt(w("T1", 0, C0), w("JK", JL - 1, JL * C0, JL), w("RD", 15, 16 * C0, 16), OP.add)
+        steps = {
+            "in0": lambda: inside(0), "in1": lambda: inside(1), "mask": lambda: half(t, 1, 1), "bits": bits,
+            "hold": lambda: (half(t, 1, 2), scalar_rows(srows[len(LOW):])),
+            "Z": lambda: unit_row() if t == 0 else None,
+            "R": lambda: tt(w("T2"), w("JK", JL - 1, JL * 32, JL), w("RD", 15, 512, 16), OP.add),
+            "F": lambda: [unpack(b) for b in (2, 3)] if t else None,
+            "OQ": lambda: quant(w("OQ"), w("OQS"), w("OB")) if t == 0 else None,
+            "RD": lambda: scan(w("RD"), w("RD0"), row(32, 0, 512), OP.min, OP.add),
+            "OWS": lambda: scan(w("OWS", 0, 256), w("I1", 0, 256), w(br, 0, 256), OP.max, OP.mult),
+        }
+        for step in PLAN:
+            if step in steps: steps[step]()
+            elif step in ("s", "S"):
+                for c in made[:len(made) - (step == "s")]: rowsum(c)
+                del made[:len(made) - (step == "s")]
+            elif isinstance(step, str): done(int(step[1:]))
+            elif step not in srows:
+                below(step)
+                made.append(step)
+        def unpacked(b):
+            if t == 0: unit(b)
+            if t == 0 or b < 2: unpack(b)
+
+        def halved(b): act(w("FH", 512 * b, 512 * b + 512), w("P%d" % b), AF.Copy, 0.5)
+
+        if t:
+            unpacked(0)
+            unpacked(1)
+        if t == 0: small_constants()
         tt(w("PAY", 0, 256), ind(w(tb), w(ll, 0, 16)), w("OWS", 0, 256), OP.mult)
-        ts(w("T3"), w("T1"), w("UP"), None, OP.mult)
+        tt(w("T1"), w("RS"), w("T2"), OP.add)
+        act(w("T3"), w("T1"), AF.Copy, w("UP"))
         lift("EXA", "PD", 0, 256)
         lift("EXA", "PD", 256, 512)
-        for b in range(4): act(w("FH", 512 * b, 512 * b + 512), w("P%d" % b), AF.Copy, 0.5)
-        tt(w("RK", 0, 16), top("EXA", 0, 256), w("T3", 0, 16), OP.subtract)
-        tt(w("RK", 16, 32), top("EXA", 256, 512), w("T3", 16, 32), OP.subtract)
+        act(w(lr), ind(w("IOTA", 0, 512), w(ll)), AF.Copy)
+        if t == 0: unpacked(0)
+        scan(w("OWS", 256, 512), w("I1", 256, 512), w(br, 256, 512), OP.max, OP.mult)
+        tt(w("RK"), top("EXA", 0, 512), w("T3"), OP.subtract)
         tt(w("PAY", 256, 512), ind(w(tb), w(ll, 16, 32)), w("OWS", 256, 512), OP.mult)
         ts(w("RKU"), w("RK"), w("MC"), w("R15"), OP.mult, OP.add)
-        if t == 0: act(w(lr), ind(w("IOTA", 0, 512), w(ll)), AF.Copy)
+        if t == 0:
+            unpacked(1)
+            unpacked(2)
+        for b in ((2, 3, 0, 1) if t else (0, 1, 2)): halved(b)
         cp(ind(w("POS"), w("RKU")), w("PAY"))
-        act(w("POSA"), w("POS"), AF.Abs, 4.0)
+        act(w("POSA", 0, 192), w("POS", 0, 192), AF.Abs, 4.0)
+        act(w("POSA", 192, 512), w("POS", 192, 512), AF.Abs, 4.0)
+        if t == 0:
+            unpacked(3)
+            halved(3)
         ts(w("F5", 0, 256), w("POS", 1, 512, 2), 0.0, 512.0, OP.is_lt, OP.mult)
         ts(w("FM", 1, 257), w("POS", 1, 512, 2), 0.0, -511.0, OP.is_lt, OP.mult)
+
+        def pair(a, b): scan(w("PKD", a, b), w("PK", 0, b - a), w("POSA", a, b), OP.mult, OP.add)
+
+        pair(0, 96)
         scan(w("VP", 0, 257), w("FM", 0, 257), w("F5", 0, 257), OP.add, OP.add)
-
-        def pair(i): scan(w("PKD", 128 * i, 128 * i + 128), w("PK"), w("POSA", 128 * i, 128 * i + 128), OP.mult, OP.add)
-
-        pair(0)
+        pair(96, 192)
         lift("EXB", "VP", 0, 256)
         ts(w("TOT"), w("VP", 256, 257), w("NUP"), w("NUQ"), OP.mult, OP.add)
-        pair(1)
+        pair(192, 288)
         tt(w("NB"), w("JS"), top("EXB", 0, 256), OP.subtract)
         ts(w("NA"), top("EXB", 0, 256), w("TOT"), None, OP.add)
-        pair(2)
+        pair(288, 400)
         tt(w("NN"), w("NA"), w("NB"), OP.max)
-        pair(3)
+        pair(400, 512)
         ts(w("NU"), w("NN"), w("MC"), 0.25, OP.mult, OP.add)
         cp(ind(w("FO"), w("NU")), w("PKD", 1, 512, 2))
-        nv = 4 - NS[t]
-        for b in range(nv): act(w("FB", 512 * b, 512 * b + 512), w("P%d" % b), AF.Copy)
-        lift("EXK", "FO", 0, 256)
+        sp = SP[t]
+        nv = 4 if last else 3
+        for b in range(nv): act(w("FB", 512 * b, 512 * b + sp), w("P%d" % b, 0, sp), AF.Copy)
+        def firsts(a): ts(w(kq, a, a + 8), top("EXK", 16 * a, 16 * a + 128), w("MK"), -513.0 / 512.0 - 0.499, OP.mult, OP.add)
+
+        lift("EXK", "FO", 0, 128)
+        lift("EXK", "FO", 128, 256)
+        firsts(0)
         down(w("KQV"), "EXK", 0, 256, -513.0)
-        ts(w(kq, 0, 16), top("EXK", 0, 256), w("MK"), -513.0 / 512.0 - 0.499, OP.mult, OP.add)
-        ts(w("KQI", 0, 16), w("KQV"), 511, None, OP.bitwise_and)
-        cp(w(kq, 16, 32), w("KQI", 0, 16))
+        firsts(8)
+        ts(w("KQI", 0, 8), w("KQV", 0, 8), 511, None, OP.bitwise_and)
+        ts(w("KQI", 8, 16), w("KQV", 8, 16), 511, None, OP.bitwise_and)
+        cp(w(kq, 16, 24), w("KQI", 0, 8))
+        cp(w(kq, 24, 32), w("KQI", 8, 16))
 
         def first(h, b):
             o, i = (8, 512) if h == "L" else (0, 0)
@@ -413,87 +469,96 @@ def rank_program(g, core, T, topo):
             act(w("LQK%d" % t, 128, 256), ind(w(lr), w(kq, 8, 16)), AF.Copy)
 
         for b in range(4): first("K", b)
-        cp(w("NMR"), ind(w(lr), w(kq, 16, 24)))
-        second("K", 0)
+        act(w("NMR"), ind(w(lr), w(kq, 16, 24)), AF.Copy)
+        for b in range(4): second("K", b)
         lift("EXN", "NMR", 0, 128)
-        second("K", 1)
-        down(w("NL%d" % t), "EXN", 0, 128)
-        send(nxt[t], w("NLI%d" % t), w("NL%d" % t), "nma%d" % t, "nml%d" % t)
-        second("K", 2)
-        second("K", 3)
         pack("K")
+        down(w("NL%d" % t), "EXN", 0, 128)
         vq, vs = "SQ%d" % t, "SS%d" % t
+        send(nxt[t], w("NLI%d" % t), w("NL%d" % t), "nma%d" % t, "nml%d" % t)
         send(nxt[t], cast(w(vq, 0, 128), dt.uint8), cast(w("AKQ%d" % t), dt.uint8), "cda%d" % t, "cdl%d" % t, 2)
         send(nxt[t], w(vs, 0, 128), w("AKS%d" % t), "cda%d" % t, "cdl%d" % t, 2)
         cp(ind(w("EW"), w(kq, 24, 32)), w("IOTA", 128, 256))
-        if EARLY[t]:
-            turn_rows()
-            turn(t, 0)
-            turn(t, 1)
+        turn_rows()
         for b in range(4): first("L", b)
-        if EARLY[t]: turned(t)
-        else: turn_rows()
-        for b in range(4): second("L", b)
-        quant(w(vq, 128, 256), w(vs, 128, 256), w("AL%d" % t))
+        turn(t, 0)
+        second("L", 0)
+        turn(t, 1)
+        turned(t)
+        for b in range(1, 4): second("L", b)
+
+        def layer(a):
+            for b in range(4):
+                mm(w("P" + "ABCD"[b], 0, 128), w("WQ", 128 * b, 128 * b + 128), w("WS", 128 * b, 128 * b + 128), w(vq, a, a + 128), w(vs, a, a + 128))
+                act(w("HS", HW * b + a, HW * b + a + 128), w("P" + "ABCD"[b], 0, 128), AF.Copy, 0.03125)
+
         lands(prv[t], [w("NLI%d" % t)], "nma%d" % t)
         lands(prv[t], [w(vq, 0, 128), w(vs, 0, 128)], "cda%d" % t)
-        for b in range(4): mm(w("P" + "ABCD"[b], 0, 256), w("WQ", 128 * b, 128 * b + 128), w("WS", 128 * b, 128 * b + 128), w(vq), w(vs))
-        def window(b): act(w("HS", HW * b, HW * b + 256), w("P" + "ABCD"[b], 0, 256), AF.Copy, 0.03125)
-        for b in range(nv + 1): window(b)
+        layer(0)
         cp(ind(w("EW"), w("NLI%d" % t)), w("IOTA", 0, 128))
-        if last: quant(w("VQ"), w("VQS"), w("VB"))
-        if not EARLY[t]: turn(t, 0)
-        lift("EXE", "EW", 256, 512)
+        quant(w(vq, 128, 256), w(vs, 128, 256), w("AL%d" % t))
+        layer(128)
         lift("EXE", "EW", 0, 256)
-        down(w("EL", 16, 32), "EXE", 256, 512)
-        down(w("EL", 0, 16), "EXE", 0, 256)
-        if not EARLY[t]: turn(t, 1)
+        lift("EXE", "EW", 256, 512)
+        if last:
+            quant(w("VQ"), w("VQS"), w("VB"))
+            down(w("EL"), "EXE", 0, 512)
+        else:
+            lift("EXA", "NR%d" % t, 0, 192)
+            down(w("EL"), "EXE", 0, 512)
+            lift("EXA", "NR%d" % t, 192, 384)
         xn = "XN%d" % t
 
         def picked(b, a, e): return ind(w("HS", HW * b, HW * b + HW), w("EL", a // 16, e // 16))
-        def pick(b, a, e): act(w("GB", 512 * (b - 1) + a, 512 * (b - 1) + e), picked(b, a, e), AF.Copy)
-        def new_x(b, a, e):
-            out = w(xn, 4 * a + b, 4 * e, 4)
-            if b < nv: tt(out, picked(b, a, e), w("FB", 512 * b + a, 512 * b + e), OP.add)
-            else: tt(out, w("GB", 512 * (b - 1) + a, 512 * (b - 1) + e), w("P%d" % b, a, e), OP.add)
+        if nv < 4: act(w("GB", 1024, 1024 + sp), picked(3, 0, sp), AF.Copy)
+        for b in range(4): act(w("GB", 256 * b, 256 * b + 512 - sp), picked(b, sp, 512), AF.Copy)
+        for b in range(nv): tt(w(xn, b, 4 * sp, 4), picked(b, 0, sp), w("FB", 512 * b, 512 * b + sp), OP.add)
+        if nv < 4: tt(w(xn, 3, 4 * sp, 4), w("GB", 1024, 1024 + sp), w("P3", 0, sp), OP.add)
 
-        for b in range(nv, 4):
-            if b > nv: window(b)
-            pick(b, 256, 512)
-        for b in range(nv, 4): pick(b, 0, 256)
-        for b in range(nv): new_x(b, 256, 512)
-        for b in range(nv): new_x(b, 0, 256)
-        for b in range(nv, 4): new_x(b, 256, 512)
-        pack_x(t + 1, 1)
+        def upper(b, a=sp, e=512): tt(w(xn, 4 * a + b, 4 * e, 4), w("GB", 256 * b + a - sp, 256 * b + e - sp), w("P%d" % b, a, e), OP.add)
+
         if not last:
-            for b in range(nv, 4): new_x(b, 0, 256)
-            if not EARLY[t]: turned(t)
+            lift("EXA", "NR%d" % t, 384, 512)
+            pack_x(t + 1, 0)
+            half(t + 1, 0, 0)
+            upper(0)
+            upper(1)
+            half(t + 1, 0, 1)
+            upper(2)
+            half(t + 1, 0, 2)
+            upper(3)
+            down(w("NLL"), "EXA", 0, 512)
+            send(prv[t], w("LL%d" % (t + 1)), w("NLL"), "tra%d" % t, "trl%d" % t)
+            send(T.cores[(rank - 2 ** t + 2 ** (t + 1)) % N], w("LI%d" % (t + 1)), w("NLL"), "lia%d" % (t + 1), "lil%d" % (t + 1))
+            lands(nxt[t], [w("LL%d" % (t + 1))], "tra%d" % t)
 
-    t, o = ROUNDS - 1, 512 * ROUNDS
-    stores = 2 * len(TAIL) + 11
+    t, o, stores = ROUNDS - 1, 512 * ROUNDS, 9
+    pieces = [(0, sp)] + list(TAIL)
 
-    def store(a, e, P):
+    def store(i):
+        a, e = pieces[i]
         q, s = w("XQ", o + a, o + e), w("XS", o + a, o + e)
-        mm(w(P, 0, e - a), w("VQ"), w("VQS"), q, s)
-        dma("y", hbm(T.oc[:, 4 * a:4 * e]), cast(q, dt.uint8), "st", stores)
+        quant(q, s, w(xn, 4 * a, 4 * e))
+        mm(w("P" + "ABC"[i], 0, e - a), w("VQ"), w("VQS"), q, s)
+        if i: a = sp
+        if e in (sp, 512): dma("y", hbm(T.oc[:, 4 * a:4 * e]), cast(w("XQ", o + a, o + e), dt.uint8), "st", stores)
 
-    def scales(a, e):
-        for k in range(4): dma("y", hbm(T.osc[4 * k:4 * k + 4, a:e]), w("XS", o + a, o + e, rows=slice(32 * k, 32 * k + 4)), "st", stores)
+    def result(i):
+        a, e = pieces[i]
+        if i + 1 < len(pieces): act(w("YS", a, e), w("P" + "ABC"[i], 0, e - a), AF.Copy)
+        else: cp(w("YS", a, e), w("P" + "ABC"[i], 0, e - a))
+        if i: a = sp
+        if e in (sp, 512): dma("s", hbm(T.y[:, a:e]), w("YS", a, e), "st", stores)
 
-    store(256, 512, "PA")
-    scales(256, 512)
-    act(w("YS", 256, 512), w("PA", 0, 256), AF.Copy)
-    dma("s", hbm(T.y[:, 256:512]), w("YS", 256, 512), "st", stores)
-    for i, (a, e) in enumerate(TAIL):
-        for b in range(nv, 4): new_x(b, a, e)
-        quant(w("XQ", o + a, o + e), w("XS", o + a, o + e), w(xn, 4 * a, 4 * e))
-        store(a, e, "P" + "BC"[i])
-    scales(0, 256)
-    for i, (a, e) in enumerate(TAIL):
-        if i + 1 < len(TAIL): act(w("YS", a, e), w("P" + "BC"[i], 0, e - a), AF.Copy)
-        else: cp(w("YS", a, e), w("P" + "BC"[i], 0, e - a))
-        dma("s", hbm(T.y[:, a:e]), w("YS", a, e), "st", stores)
-    lands(nxt[t], [w("TRX%d" % t)], "tra%d" % t)
-    dma("y", hbm(T.lk[:, :]), w("TRX%d" % t), "st", stores)
+    upper(0)
+    store(0)
+    lands(nxt[t], [w("TRX")], "tra%d" % t)
+    dma("y", hbm(T.lk[:, :]), w("TRX"), "st", stores)
+    upper(1)
+    upper(2)
+    for a, e in TAIL: upper(3, a, e)
+    for i in range(len(TAIL)): store(i + 1)
+    for k in range(4): dma("y", hbm(T.osc[4 * k:4 * k + 4, :]), w("XS", o, o + 512, rows=slice(32 * k, 32 * k + 4)), "st", stores)
+    for i in range(len(pieces)): result(i)
     for sem in total:
         if know["g"].get(sem, 0) < total[sem]: g.wait_ge(T.sem[sem], total[sem])

@@ -3,23 +3,23 @@ from concourse.mybir import dt, AluOpType as OP, ActivationFunctionType as AF
 
 N, ROUNDS = 4, 2
 HW = 264
-BIG = 2.0 ** 26
+BIG = 2.0 ** 32
+B4 = 2.0 ** 20
 FAR = 1e25
 C0 = 25
-JL = 8 * C0
-SP = (256, 256)
+D, WV = (C0 - 1) // 2, 16 * C0
+NPICK = (4, 4)
 COPIES = (4, 2)
-LOW = [15, 14, 13]
 TAIL = ((256, 384), (384, 512))
+VPAD = 10
+CUTS = (0, 108, 216, 296, 404, 512)
 LAG = 2
-SPAD = (2, 7)
-MID = ([], [])
-PLAN = ["OQ", "in0", 12, 11, "mask", 10, "hold", 9, 8, 7, "in1", "F", 6, 5, "bits", 16, "S", "T5", "T6", "Z", 24, 23, 22, 21, "s", "T0", "T4", 20, 19, 18, 17, 4, 3, "s", "T3", "T1", 2, 1, "S", "RD", "T7", "T2", "OWS", "R"]
-ORDER = [32, C0 - 1, C0 - 2, C0 - 3] + list(range(31, C0 - 1, -1)) + list(range(C0 - 4, 0, -1))
-TILES = [ORDER[4 * k:4 * k + 4] for k in range(8)]
-TC = [max(128, 16 * max(r)) for r in TILES]
-TO = [sum(TC[:k]) for k in range(9)]
-SLOT = {c: (i // 4, i % 4) for i, c in enumerate(ORDER)}
+ROWS = list(range(31, C0 - 1, -1))
+DS = WV // 4 + 4
+AT = {**{d: DS * d - WV // 4 for d in range(1, D + 1)}, **{c: DS * D + 128 * i for i, c in enumerate([32] + ROWS)}}
+TILES = [[d - 1, d] for d in range(D, 0, -2)]
+NV = len(TILES)
+TILES += [[32, 31], [30, 29], [28, 27], [26], [25]]
 CODES, F32, BF, F16 = "float8_e4m3fn_x4", "float32", "bfloat16", "float16"
 
 SCRATCH = {}
@@ -30,39 +30,43 @@ def buf(names, cols, dtype, where="sbuf"):
 
 
 buf("X0 XN0 XN1 FH FB", 2048, BF)
-buf("UB VB OA OB RD0 BR0 BR1 TB0 TB1 AK0 AK1 AL0 AL1", 512, BF)
-buf("AROW KM RZ", 256, BF)
+buf("UB VB OA OB OC BR0 BR1 TB0 TB1 EA EW AK0 AK1 AL0 AL1", 512, BF)
+buf("AROW KM RZ CY", 256, BF)
+buf("CT", 384, BF)
+buf("RM", WV // 4, BF)
+buf("RD0", 512 - WV, BF)
 buf("Z", 520, BF)
-buf("UQ UR UT VQ OQ AKQ0 AKQ1", 128, CODES)
-buf("UQS URS UTS VQS OQS AKS0 AKS1", 128, "uint8")
+buf("ZB", 960, BF)
+buf("UQ UR UT VQ OQ AQ AKQ0 AKQ1", 128, CODES)
+buf("UQS URS UTS VQS OQS AQS AKS0 AKS1", 128, "uint8")
 buf("SQ0 SQ1", 256, CODES)
 buf("SS0 SS1", 256, "uint8")
 buf("WQ EQ", 512, CODES)
 buf("WS EQS", 512, "uint8")
 buf("XQ", 512 * 3, CODES)
 buf("XS", 512 * 3, "uint8")
-buf("QT", TO[8], CODES)
-buf("QS", TO[8], "uint8")
-buf("BT", 4 * TO[8], BF)
+buf("QT", AT[C0] + 256, CODES)
+buf("QS", AT[C0] + 256, "uint8")
+buf("BT", 4 * AT[C0] + 512, BF)
 buf("SG", 3 * 512, BF)
-buf("JK", 32 * JL, F16)
-buf("I1 OWS RD", 512, F16)
-buf("F5 FM VP", 264, F16)
+buf("I1 PAY", 512, F16)
+buf("RD", 512 - WV, F16)
+buf("F5 FM VP EXB", 264, F16)
+buf("EXE", 512, BF)
 buf("KB", 1024, BF)
 buf("LINKI", 32, "int32")
-buf("CT", 260, F32)
 buf("PK", 128, F32)
-buf("SM", 16, F32)
-buf("INT", 24, "int32")
-buf("UO", 16, "uint16")
-buf("RS", 32, F32)
+buf("SM", 24, F32)
+buf("INT", 56, "int32")
+buf("UO", 48, "uint16")
+buf("RS NT NX", 32, F32)
 buf("WK", 192, F32)
-buf("EX", 1920, F32)
+buf("EX", 896, F32)
 buf("II", 48, "int32")
 buf("U16", 80, "uint16")
 buf("IOTA", 512, F32)
-buf("T2", 32, F32)
-buf("MSK H PAY POS POSA PKD EW YS LR0 LR1 NR0 NR1", 512, F32)
+buf("MSK H POS PKD YS LR0 LR1 NR0 NR1", 512, F32)
+buf("HF", WV, F32)
 buf("FO LQK0 LQK1", 256, F32)
 buf("NMR", 128, F32)
 buf("HS", 4 * HW, F32)
@@ -75,19 +79,33 @@ buf("BRD1 BRX1", 32 * COPIES[1], BF, "dram")
 buf("PA PB PC PD P0 P1 P2 P3", 512, F32, "psum")
 
 PIECE = {
-    "CX": ("CT", 0, 256), "MC": ("CT", 256, 1), "UP": ("CT", 257, 1),
     "PM": ("SM", 0, 2), "E8": ("SM", 2, 2), "NUP": ("SM", 4, 1), "NUQ": ("SM", 5, 1), "R15": ("SM", 6, 1), "PU": ("SM", 7, 1),
-    "GM": ("SM", 8, 2), "MK": ("SM", 10, 1), "PN": ("SM", 11, 1), "E4": ("SM", 12, 2),
-    "UOI": ("INT", 0, 16), "PI": ("INT", 16, 2), "PJ": ("INT", 18, 2), "PG": ("INT", 20, 2),
+    "MC": ("SM", 10, 1), "U4": ("SM", 11, 1), "M2": ("SM", 12, 1), "U2": ("SM", 13, 1), "NL": ("SM", 14, 1), "IL": ("SM", 15, 1),
+    "N4": ("SM", 16, 1), "I4": ("SM", 17, 1), "M4": ("SM", 18, 1), "S4": ("SM", 19, 1), "NU4": ("SM", 20, 1), "MK": ("SM", 21, 1),
+    "CX": ("CT", 0, 256), "C4": ("CT", 256, 128),
+    "EXS": ("EX", 0, 128), "EXV": ("EX", 128, 128), "EXR": ("EX", 256, 128),
+    "UOI": ("INT", 0, 16), "HOI": ("INT", 16, 32), "PI": ("INT", 48, 2), "PJ": ("INT", 50, 2),
     "T1": ("WK", 0, 32), "T3": ("WK", 32, 32), "RK": ("WK", 64, 32), "NA": ("WK", 96, 16), "NB": ("WK", 112, 16), "NN": ("WK", 128, 16),
     "JS": ("WK", 144, 16), "TOT": ("WK", 160, 1),
-    "EXA": ("EX", 0, 512), "EXB": ("EX", 512, 256), "EXK": ("EX", 768, 256), "EXN": ("EX", 1024, 128), "EXE": ("EX", 1152, 512),
+    "EXK": ("EX", 512, 256), "EXN": ("EX", 768, 128),
     "KQV": ("II", 0, 16), "KQI": ("II", 16, 32),
     "RKU": ("U16", 0, 32), "NU": ("U16", 32, 16), "EL": ("U16", 48, 32),
 }
-SEMAPHORES = ["cv", "cs", "ct", "cg", "ldx0", "ldx1", "ldu", "ldk", "ldv", "ldw", "ldc", "st"]
+SEMAPHORES = ["cv", "cs", "ct", "cg", "ldx0", "ldx1", "ldu", "ldk", "ldv", "ldw", "ldc", "ldz", "ldo", "nrx", "st"]
 for _t in range(ROUNDS):
     SEMAPHORES += [s + "%d" % _t for s in ("bro", "bra", "brl", "tbx", "nma", "nml", "cda", "cdl", "tro", "tra", "trl", "trx", "lia", "lil")]
+
+def both(k): return [(d, h) for d in reversed(TILES[k]) for h in (0, 1)]
+
+
+def then(k, *more): return both(k)[:1] + ["T%d" % (k - 1)] + both(k)[1:] + list(more)
+
+
+VPLAN = (["ones", "in1", "mask", (12, 2), "hold", (11, 2), "in0", (10, 2), (9, 2), "bits", (1, 3), (2, 3), (3, 3), "AQ", "F", "OQ"] + both(0) + ["turn"] + then(1, "links") + then(2, "T6") + then(3) + then(4, "T7")
+         + then(5) + ["RDU", "T8", "T5", "T9", "T10", "high", "EA0", "small", "CV", "RDL", "PAY0", "EXS", "low", "EA1", "RK", "PAY1", "RKU", "spare0", "POS", "spare1"])
+SPLAN = ["ahead", "full"] + ROWS + ["LR"]
+AFTER = [["rows", "k", "turn", "turned", "q", "own", "layer", "came"]] * 2
+EARLY = 2
 
 
 def rank_program(g, core, T, topo):
@@ -199,7 +217,7 @@ def rank_program(g, core, T, topo):
     def tt(out, in0, in1, o): op("v", lambda: V.tensor_tensor(out[0], in0[0], in1[0], o), [in0, in1], [out])
     def cp(out, in_): op("v", lambda: V.tensor_copy(out[0], in_[0]), [in_], [out])
     def fill(out, c): op("v", lambda: V.memset(out[0], c), [], [out])
-    def scan(out, d0, d1, op0, op1): op("v", lambda: V.tensor_tensor_scan(out[0], d0[0], d1[0], 0.0, op0, op1), [d0, d1], [out])
+    def scan(out, d0, d1, op0, op1, first=0.0): op("v", lambda: V.tensor_tensor_scan(out[0], d0[0], d1[0], first, op0, op1), [d0, d1], [out])
     def quant(q, s, in_): op("v", lambda: V.quantize_mx(q[0], s[0], in_[0]), [in_], [q, s])
     def mm(out, a, asc, b, bsc, start=True, stop=True): op("t", lambda: g.tensor.matmul_mx(out[0], a[0], asc[0], b[0], bsc[0], start, stop), [a, asc, b, bsc], [out])
     def iota(out, pattern, base, cm): op("g", lambda: G.iota(out[0], pattern, base, cm, allow_small_or_imprecise_dtypes=True), [], [out])
@@ -212,7 +230,7 @@ def rank_program(g, core, T, topo):
         elif bias is None: op("s", lambda: S.activation(out[0], in_[0], func, scale=raw(scale)), [in_, scale], [out])
         else: op("s", lambda: S.activation(out[0], in_[0], func, bias=raw(bias), scale=raw(scale)), [in_, bias, scale], [out])
 
-    def lift(ex, row, a, b): scan(w(ex, a, b), w("CX", 0, b - a), w(row, a, b), OP.mult, OP.add)
+    def lift(ex, row, a, b, by="CX"): scan(w(ex, a, b), w(by, 0, b - a), w(row, a, b), OP.mult, OP.add if by == "CX" else OP.max)
     def top(ex, a, b): return w(ex, a + 15, b, 16)
     def down(out, ex, a, b, more=None): ts(out, top(ex, a, b), w("MC"), more, OP.mult, None if more is None else OP.add)
 
@@ -221,42 +239,35 @@ def rank_program(g, core, T, topo):
     prv = [T.cores[(rank - 2 ** t) % N] for t in range(ROUNDS)]
 
     dma("s", w("UB"), hbm(T.u[:, :]), "ldu", 1)
-    dma("y", w("X0", 0, 1024), hbm(T.x[:, 0:1024]), "ldx0", 1)
     dma("y", w("X0", 1024, 2048), hbm(T.x[:, 1024:2048]), "ldx1", 1)
-    dma("y", w("LINKI"), hbm(T.link[:, :]), "ldk", 1)
+    dma("s", w("LINKI"), hbm(T.link[:, :]), "ldk", 1)
+    dma("y", w("X0", 0, 1024), hbm(T.x[:, 0:1024]), "ldx0", 1)
 
-    def pad(k): return w("BT", 4 * TO[k] + 64 * min(TILES[k]), 4 * TO[k + 1])
     r16 = slice(0, 16)
+    fill(w("ZB"), 0.0)
     iotai(w("PI"), [[0, 2]], 0, 1)
     iotai(w("UOI"), [[1, 2], [16, 8]], 0, 0)
-    iota(w("E8"), [[0, 2]], -63, -8)
-    iota(w("IOTA"), [[1, 512]], 0, 0)
+    iotai(w("HOI"), [[16, 32]], 15, 0)
+    select(w("Z"), w("ZB", 0, 520), [[1, 520]], OP.not_equal, 1.0, -3, -4)
     iota(w("AROW"), [[0, 16], [1, 16]], 0, 0)
-    iota(w("E4"), [[0, 2]], -3, -4)
-    fill(w("JK", JL - 1, JL * 32, JL), 0.0)
-    fill(w("Z", 512, 520), 0.0)
-    fill(w("RS"), 0.0)
-    fill(pad(0), 0.0)
-    zero = 4 * TO[0] + 64 * min(TILES[0])
+    iota(w("E8"), [[0, 2]], -3, -8)
+    iota(w("IOTA"), [[1, 512]], 0, 0)
     ts(w("PJ"), w("PI"), 15, None, OP.bitwise_and)
-    cp(w("UO"), w("UOI"))
+    cp(w("UO"), w("INT", 0, 48))
     cp(w("PM"), w("PJ"))
     pm = w("PM", 0, 1)
-    for k in range(1, 8):
-        if k in SPAD: act(pad(k), w("BT", zero, zero + 4 * TC[k] - 64 * min(TILES[k])), AF.Copy)
-        else: fill(pad(k), 0.0)
+    quant(w("QT", AT[32], AT[32] + 128), w("QS", AT[32], AT[32] + 128), w("ZB", 0, 512))
+    pads = [(4 * AT[c] + 16 * c, 512 - 16 * c) for c in reversed(ROWS)] + [(4 * AT[d] - 16, 16) for d in range(1, D + 1)]
+    for a, n in pads[:VPAD]: fill(w("BT", a, a + n), 0.0)
     quant(w("UQ"), w("UQS"), w("UB"))
-    iota(w("CT", rows=r16), [[0, 260]], 1, 0)
-    iota(w("RD0"), [[-16, 32], [1024, 16]], 0, 0)
-    dma("y", w("VB"), hbm(T.v[:, :]), "ldv", 1, [w("X0")])
-    dma("y", cast(w("WQ"), dt.uint8), hbm(T.wc[:, :]), "ldw", 2)
-    dma("y", w("WS"), hbm(T.ws[:, :]), "ldw", 2)
+    select(w("ZB", 448, 512), w("ZB", 448, 512), [[0, 4], [-1, 4], [1, 4]], OP.not_equal, 1.0, 0, 0)
+    for i in range(8): dma("y", w("OC", rows=slice(16 * i, 16 * i + 16)), w("ZB", 448 - 64 * i, 960 - 64 * i, rows=slice(16 * i, 16 * i + 16)), "ldo", 8)
 
     def lift_constants():
+        select(w("C4", rows=r16), w("C4", rows=r16), [[0, 32], [4, 4]], OP.is_gt, B4, -4, -1)
         select(w("CX", rows=r16), w("CX", rows=r16), [[0, 16], [1, 16]], OP.is_gt, 0.0, 0, -1)
-        select(w("MC", rows=r16), w("MC", rows=r16), [[0, 1]], OP.is_equal, 1.0 / BIG, -15, 1)
+        select(w("C4", rows=r16), w("C4", rows=r16), [[0, 32], [4, 4]], OP.is_gt, 0.0, 0, -1)
         select(w("CX", rows=r16), w("CX", rows=r16), [[0, 16], [1, 16]], OP.not_equal, BIG, -1, -1)
-        select(w("UP", rows=r16), w("UP", rows=r16), [[0, 1]], OP.is_equal, BIG, -15, 1)
         for i in range(1, 8): dma("y", w("CT", rows=slice(16 * i, 16 * i + 16)), w("CT", rows=r16), "ldc", 7)
 
     def pick_u(q, o):
@@ -265,37 +276,54 @@ def rank_program(g, core, T, topo):
 
     def xq(t, h): return w("XQ", 512 * t + 256 * h, 512 * t + 256 * h + 256), w("XS", 512 * t + 256 * h, 512 * t + 256 * h + 256)
     def pack_x(t, h): quant(*xq(t, h), w("XN%d" % (t - 1) if t else "X0", 1024 * h, 1024 * h + 1024))
-    def unit(b): quant(w("EQ", 128 * b, 128 * b + 128), w("EQS", 128 * b, 128 * b + 128), w("Z", 3 - b, 515 - b))
+    def eq(b): return w("EQ", 128 * b, 128 * b + 128), w("EQS", 128 * b, 128 * b + 128)
+    def unit(b): quant(*eq(b), w("Z", 3 - b, 515 - b))
 
     def half(t, h, step):
-        P, a = w("P" + "AD"[h], 0, 256), 256 * h
-        if step == 0: mm(P, w("UR"), w("URS"), *xq(t, h))
-        if step == 0 and h == 0 and LOW: mm(w("PC", 0, 256), w("UR"), w("URS"), *xq(t, h))
-        if step == 1: tt(w("MSK", a, a + 256), P, w("KM"), OP.add)
+        a = 256 * h
+        if step == 0:
+            mm(w("P" + "3A"[h], 0, 256), w("UR"), w("URS"), *xq(t, h))
+            if h == 0: mm(w("PB", 0, 496), w("UR"), w("URS"), w("XQ", 512 * t, 512 * t + 496), w("XS", 512 * t, 512 * t + 496))
+            mm(w("P" + "DC"[h], 0, 256), w("UT"), w("UTS"), *xq(t, h))
+        if step == 1: tt(w("MSK", a, a + 256), w("P" + "3A"[h], 0, 256), w("KM"), OP.add)
         if step == 2: scan(w("H", a, a + 256), w("RZ"), w("MSK", a, a + 256), OP.min, OP.max)
+        if step == 3: ts(w("BR%d" % t, a, a + 256), w("P" + "DC"[h], 0, 256), 0.0, None, OP.is_gt)
+        if step == 4: act(w("HF", a, min(a + 256, WV)), ind(w("H", a, a + 256), w("UO", 16, 16 + min(16, C0 - 16 * h))), AF.Copy)
 
-    act(w("GM"), w("PM"), AF.Identity, 8.0, w("E8", 0, 1))
+    act(w("NL"), pm, AF.Sign, -1.0, 15.0)
+    act(w("R15"), pm, AF.Copy, -1.0, 16 * D + 15.25)
+    act(w("PU"), pm, AF.Copy, 1.0, 1024.0)
+    act(w("IL"), w("NL"), AF.Copy, -1.0, 1.0)
+    act(w("U2"), w("NL"), AF.Copy, 1.0, 1.0)
+    act(w("S4"), pm, AF.Sign, -1.0, 11.5)
+    act(w("M2"), w("NL"), AF.Copy, -0.5, 1.0)
+    act(w("N4"), w("S4"), AF.Copy, 0.5, 0.5)
+    act(w("I4"), w("S4"), AF.Copy, -0.5, 0.5)
+    act(w("NUP"), w("NL"), AF.Copy, -1.0, -1.0)
+    act(w("NUQ"), w("NL"), AF.Copy, -256.0, -256.0)
+    act(w("MC"), w("IL"), AF.Copy, 1.0, 1.0 / BIG)
+    act(w("PU"), w("PU"), AF.Copy, w("U2"))
+    act(w("MK"), w("IL"), AF.Copy, 1024.0, 1024.0 / BIG)
+    act(w("U4"), w("N4"), AF.Copy, B4 - 1.0, 1.0)
+    act(w("NU4"), w("N4"), AF.Copy, 1.0 - B4, -1.0)
+    act(w("M4"), w("I4"), AF.Copy, 1.0 - 1.0 / B4, 1.0 / B4)
     pick_u("UR", 0)
-    act(w("OA"), w("IOTA", 0, 512), AF.Abs, 2.0, w("GM", 0, 1))
+    unit(0)
+    unit(1)
     pick_u("UT", 8)
-    pack_x(0, 0)
-    half(0, 0, 0)
-    ts(w("KM"), w("AROW"), pm, -2.0 * FAR, OP.not_equal, OP.mult)
     act(w("RZ"), w("AROW"), AF.Copy, 2.0 * FAR, -FAR)
-    ts(w("OB"), w("OA"), 64.0, None, OP.is_lt)
-    half(0, 0, 1)
-
-
-    def small_constants():
-        act(w("R15"), pm, AF.Copy, -1.0, 15.25)
-        act(w("PU"), pm, AF.Copy, w("UP"))
-        act(w("NUP"), w("UP"), AF.Copy, -1.0)
-        act(w("NUQ"), w("UP"), AF.Copy, -256.0)
-        act(w("MK"), w("MC"), AF.Copy, 1.0 / 512.0)
-        act(w("JS"), w("IOTA", 0, 256, 16), AF.Identity, w("UP"), w("PU"))
-
-    def turn(t, h):
-        cp(ind(w("LR%d" % t), w("KQ%d" % t, 8 + 16 * h, 16 + 16 * h)), w("LQK%d" % t, 128 * h, 128 * h + 128))
+    for a, n in pads[VPAD:]: act(w("BT", a, a + n), w("ZB", 0, n), AF.Copy)
+    unit(2)
+    pack_x(0, 1)
+    half(0, 1, 0)
+    ts(w("KM"), w("AROW"), pm, -2.0 * FAR, OP.not_equal, OP.mult)
+    cp(w("LL0"), w("LINKI"))
+    send(nxt[0], w("LI0"), w("LL0"), "lia0", "lil0")
+    unit(3)
+    half(0, 1, 1)
+    iota(w("CT", rows=r16), [[0, 384]], 1, 0)
+    act(w("OA"), w("IOTA", 0, 512), AF.Abs, 2.0, w("E8", 0, 1))
+    act(w("JS"), w("IOTA", 0, 256, 16), AF.Identity, w("U2"), w("PU"))
 
     def turned(t):
         lands(T.cores[(rank - 2 ** t + 2 ** t // 2) % N], [w("LI%d" % t)], "lia%d" % t)
@@ -303,38 +331,52 @@ def rank_program(g, core, T, topo):
         if t == ROUNDS - 1:
             dma("y", w("TRD"), w("NR%d" % t, rows=rows8), "tro%d" % t, 1)
             send(prv[t], w("TRX"), w("TRD"), "tra%d" % t, "trl%d" % t)
+        else:
+            for h in range(2): dma("y", w("NT", 16 * h, 16 * h + 16), w("NR%d" % t, rows=slice(16 * h, 128, 32)), "nrx", 2)
 
     for t in range(ROUNDS):
         last = t == ROUNDS - 1
         xc, xs = w("XQ", 512 * t, 512 * t + 512), w("XS", 512 * t, 512 * t + 512)
         ll, lr, kq, br, tb = ("%s%d" % (n, t) for n in ("LL", "LR", "KQ", "BR", "TB"))
         def scores(P, n): mm(w(P, 0, n), w("UR"), w("URS"), w("XQ", 512 * t, 512 * t + n), w("XS", 512 * t, 512 * t + n))
-        def unpack(b): mm(w("P%d" % b), w("EQ", 128 * b, 128 * b + 128), w("EQS", 128 * b, 128 * b + 128), xc, xs)
+        def unpack(b): mm(w("P%d" % b), *eq(b), xc, xs)
+        def halved(b): act(w("FH", 512 * b, 512 * b + 512), w("P%d" % b), AF.Copy, 0.5)
 
-        pack_x(t, 1)
-        half(t, 1, 0)
-        scores("P1", 496)
-        mm(w("PB"), w("UT"), w("UTS"), xc, xs)
-        scores("P0", 16 * (C0 - 1))
-        if t == 0:
-            half(0, 0, 2)
-            cp(w("LL0"), w("LINKI"))
-            send(nxt[0], w("LI0"), w("LL0"), "lia0", "lil0")
+        if t == 0: half(t, 1, 3)
+        else:
+            act(w("EA", 256, 512), w("PC", 0, 256), AF.Sign)
+            act(w(br, 256, 512), w("EA", 256, 512), AF.Relu)
+        pack_x(t, 0)
+        half(t, 0, 0)
+        scores("PC", WV)
+        half(t, 1, 2)
+        half(t, 1, 4)
 
-        def row(c, a, b): return w("BT", 4 * (TO[SLOT[c][0]] + a) + SLOT[c][1], 4 * (TO[SLOT[c][0]] + b), 4)
+        def links():
+            if t == 0: return
+            cp(w("NLL"), w("NX"))
+            send(prv[t - 1], w(ll), w("NLL"), "tra%d" % (t - 1), "trl%d" % (t - 1))
+            send(T.cores[(rank - 2 ** (t - 1) + 2 ** t) % N], w("LI%d" % t), w("NLL"), "lia%d" % t, "lil%d" % t)
+            lands(nxt[t - 1], [w(ll)], "tra%d" % (t - 1))
+
+        def slot(c, a, b): return w("BT", 4 * AT[c] + a, 4 * AT[c] + b)
+        def codes(a, n): return w("QT", a + 128 * (a >= AT[32]), a + 128 * (a >= AT[32]) + n), w("QS", a + 128 * (a >= AT[32]), a + 128 * (a >= AT[32]) + n)
         def mine(c): return w("H", 16 * c + 15, 16 * c + 16)
-        srows = LOW + MID[t] + list(range(31, C0 - 1, -1))
-        def signs(c): return w("SG", 512 * (srows.index(c) % 3), 512 * (srows.index(c) % 3) + 16 * c)
-        def sign(c): act(signs(c), w("PC" if c <= 16 else "P1", 0, 16 * c), AF.Sign, -1.0, mine(c))
-        def beats(c): act(row(c, 0, 16 * c), signs(c), AF.Relu, accum=w("RS", c, c + 1))
-        def below(c): ts(row(c, 0, 16 * c), w("PA" if c <= 16 else "P0", 0, 16 * c), mine(c), None, OP.is_lt)
-        def inside(h): tt(row(32, 256 * h, 256 * h + 256), w("P" + "AD"[h], 0, 256), w("H", 256 * h, 256 * h + 256), OP.is_le)
-        def rowsum(c): scan(w("JK", JL * (c + 1) - 8 * c, JL * (c + 1)), row(c, 0, 8 * c), row(c, 8 * c, 16 * c), OP.add, OP.add)
-        def pack_b(k): quant(w("QT", TO[k], TO[k + 1]), w("QS", TO[k], TO[k + 1]), w("BT", 4 * TO[k], 4 * TO[k + 1]))
-        def colsum(k, first, end): mm(w("PD", 0, TC[k]), w("OQ"), w("OQS"), w("QT", TO[k], TO[k + 1]), w("QS", TO[k], TO[k + 1]), first, end)
+        def signs(c): return w("SG", 512 * (c % 3), 512 * (c % 3) + 16 * c)
+        def sign(c): act(signs(c), w("PB", 0, 16 * c), AF.Sign, -1.0, mine(c))
+        def beats(c): act(slot(c, 0, 16 * c), signs(c), AF.Relu, accum=w("RS", c, c + 1))
+        def inside(h): tt(slot(32, 256 * h, 256 * h + 256), w("P" + "3A"[h], 0, 256), w("H", 256 * h, 256 * h + 256), OP.is_le)
+
+        def apart(d, h):
+            e = WV - 16 * d
+            a = 256 - 16 * d if (d, 2) in VPLAN else 256 if (d, 3) in VPLAN else e
+            if h == 0: tt(slot(d, 0, a), w("PC", 0, a), w("HF", 16 * d, 16 * d + a), OP.is_lt)
+            if h == 1: tt(slot(d, e, WV), w("PC", e, WV), w("HF", 0, 16 * d), OP.is_le)
+            if h == 2: tt(slot(d, a, e), w("P3", a, e), w("HF", 256, WV), OP.is_lt)
+            if h == 3: tt(slot(d, a, e), w("PA", 0, e - a), w("HF", 256 + 16 * d, WV), OP.is_lt)
 
         def bits():
-            ts(w(br), w("PB"), 0.0, 0.5, OP.is_gt, OP.subtract)
+            half(t, 0, 3)
             k = 16 // COPIES[t]
             dma("y", w("BRD%d" % t), w(br, rows=slice(0, 128, k)), "bro%d" % t, 1)
             send(prv[t], w("BRX%d" % t), w("BRD%d" % t), "bra%d" % t, "brl%d" % t)
@@ -342,197 +384,185 @@ def rank_program(g, core, T, topo):
             for a in range(k): dma("y", w(tb, rows=slice(a, 128, k)), w("BRX%d" % t), "tbx%d" % t, k)
             if t == 0:
                 lift_constants()
-                iota(w("I1"), [[1, 512]], 1, 0)
+                dma("y", cast(w("WQ"), dt.uint8), hbm(T.wc[:, :]), "ldw", 2)
+                dma("y", w("WS"), hbm(T.ws[:, :]), "ldw", 2)
+                dma("y", w("VB"), hbm(T.v[:, :]), "ldv", 1)
+                iota(w("RD0"), [[-16, 32 - C0], [1024, 16]], 16 * D - WV, 0)
+                iota(w("RM"), [[0, C0], [1, 4]], 0, 0)
+                select(w("RM"), w("RM"), [[0, C0], [-1, 4]], OP.is_ge, 1.0, 0, 0)
+                iota(w("I1"), [[1, 512]], 0, 0)
                 for z in (w("F5", 256, 257), w("FM", 0, 1)): iota(z, [[0, 1]], 0, 0)
-                iota(w("PK"), [[0, 64], [512, 2]], 0, 0)
+                iota(w("PK"), [[0, 64], [2048, 2]], 0, 0)
                 iota(w("HS", 256, 4 * HW, HW), [[0, 4]], 0, 0)
-            for c in MID[t]: iota(w("JK", JL * (c + 1) - 1, JL * (c + 1)), [[0, 1]], 0, 0)
             iota(w("EW"), [[0, 512]], 256, 0)
 
-        def scalar_rows(rows):
-            for i, c in enumerate(rows):
-                sign(c)
-                if i: beats(rows[i - 1])
-            if rows: beats(rows[-1])
-
-        scalar_rows(LOW)
-
-        def unit_row():
-            act(w("OA"), w("IOTA", 0, 512), AF.Abs, 1.0, w("E4", 0, 1))
-            act(w("Z", 0, 512), w("OA"), AF.Relu, -1.0, 1.0)
-
-        made, packed, waiting = [], [], []
+        signed = []
 
         def done(k):
-            pack_b(k)
-            packed.append(k)
-            waiting.append(k)
-            if 0 in packed:
-                for j in sorted(waiting): colsum(j, j == 0, len(packed) == 8 and j == max(waiting))
-                waiting.clear()
+            a = AT[TILES[k][0]] - 4 * (k < NV)
+            n = len(TILES[k]) * (DS if k < NV else 128)
+            quant(*codes(a, n), w("BT", 4 * a, 4 * (a + n)))
+            won = [AT[d] + WV // 4 - 4 * d for d in TILES[k]] + [0] * (k == NV - 1) if k < NV else [AT[32]] * (k == NV)
+            for c in TILES[k]: mm(w("P3" if k < NV else "PD", 0, 128), w("OQ"), w("OQS"), *codes(AT[c], 128), c in (TILES[0][0], 32), c in (TILES[NV - 1][-1], C0))
+            for a in won: mm(w("PA", 0, 128), w("AQ"), w("AQS"), *codes(a, 128), k == 0 and a == won[0], k == NV - 1 and a == won[-1])
+
+        def ahead(n):
+            for r in ROWS[len(signed):n]:
+                sign(r)
+                signed.append(r)
+
+        def srow(c):
+            ahead(ROWS.index(c) + 2)
+            beats(c)
+
+        def low():
+            tt(w("T1", 0, C0), w("EXV", 3, WV // 4, 4), w("EXR", 3, WV // 4, 4), OP.subtract)
+
+        def high():
+            tt(w("T3", C0, 32), w("RS", C0, 32), w("RD", 15, 512 - WV, 16), OP.add)
+            act(w("T1", C0, 32), w("T3", C0, 32), AF.Copy, w("NU4"))
+
+        def differ(a): tt(w("EA", a, a + 256), ind(w(tb), w(ll, a // 16, a // 16 + 16)), w(br, a, a + 256), OP.not_equal)
+        def pay(a, b): scan(w("PAY", a, b), w("I1", a, b), w("EA", a, b), OP.max, OP.subtract)
 
         steps = {
-            "in0": lambda: inside(0), "in1": lambda: inside(1), "mask": lambda: half(t, 1, 1), "bits": bits,
-            "hold": lambda: (half(t, 1, 2), scalar_rows(srows[len(LOW):])),
-            "Z": lambda: unit_row() if t == 0 else None,
-            "R": lambda: tt(w("T2"), w("JK", JL - 1, JL * 32, JL), w("RD", 15, 512, 16), OP.add),
-            "F": lambda: [unpack(b) for b in (2, 3)] if t else None,
-            "OQ": lambda: quant(w("OQ"), w("OQS"), w("OB")) if t == 0 else None,
-            "RD": lambda: scan(w("RD"), w("RD0"), row(32, 0, 512), OP.min, OP.add),
-            "OWS": lambda: scan(w("OWS", 0, 256), w("I1", 0, 256), w(br, 0, 256), OP.max, OP.mult),
+            "in0": lambda: inside(0), "in1": lambda: inside(1), "ahead": lambda: ahead(1), "low": low, "high": high,
+            "mask": lambda: half(t, 0, 1), "hold": lambda: half(t, 0, 2), "full": lambda: half(t, 0, 4), "bits": bits, "links": links,
+            "turn": lambda: op("v", lambda: V.transpose(w("NX")[0], w("NT")[0]), [w("NT")], [w("NX")]) if t else None,
+            "ones": lambda: ts(w("OB"), w("OA"), 4.0, w("U4"), OP.is_lt, OP.mult) if t == 0 else None,
+            "F": lambda: [unpack(b) for b in range(EARLY)],
+            "AQ": lambda: quant(w("AQ"), w("AQS"), w("OB")) if t == 0 else None,
+            "OQ": lambda: quant(w("OQ"), w("OQS"), w("OC")) if t == 0 else None,
+            "RDU": lambda: scan(w("RD"), w("RD0"), slot(32, WV, 512), OP.min, OP.add),
+            "RDL": lambda: scan(w("EXR", 0, WV // 4), w("RM"), w("PA", 0, WV // 4), OP.mult, OP.add),
+            "CV": lambda: scan(w("EXV", 0, WV // 4), w("C4", 0, WV // 4), w("P3", 0, WV // 4), OP.mult, OP.add),
+            "EA0": lambda: differ(0), "EA1": lambda: differ(256), "PAY0": lambda: pay(0, 256), "PAY1": lambda: pay(256, 512),
+            "small": lambda: ts(w("I1"), w("I1"), 1.0 / 1024, None, OP.mult) if t == 0 else None,
+            "LR": lambda: act(w(lr), ind(w("IOTA", 0, 512), w(ll)), AF.Copy),
+            "EXS": lambda: (scan(w("EXS"), w("C4"), w("PD", 0, 128), OP.mult, OP.add), [unpack(b) for b in range(EARLY, 4)]),
+            "RK": lambda: tt(w("RK"), w("EXS", 3, 128, 4), w("T1"), OP.add),
+            "RKU": lambda: ts(w("RKU"), w("RK"), w("M4"), w("R15"), OP.mult, OP.add),
+            "POS": lambda: cp(ind(w("POS"), w("RKU")), w("PAY")),
+            "spare0": lambda: quant(w("VQ"), w("VQS"), w("VB")) if last else None,
+            "spare1": lambda: ts(w("CY"), w("CX"), 2.0, None, OP.min) if t == 0 else None,
         }
-        for step in PLAN:
-            if step in steps: steps[step]()
-            elif step in ("s", "S"):
-                for c in made[:len(made) - (step == "s")]: rowsum(c)
-                del made[:len(made) - (step == "s")]
-            elif isinstance(step, str): done(int(step[1:]))
-            elif step not in srows:
-                below(step)
-                made.append(step)
-        def unpacked(b):
-            if t == 0: unit(b)
-            if t == 0 or b < 2: unpack(b)
+        needs = {"full": ["hold"], "LR": ["links"], "EXS": ["LR"]}
+        needs.update({"T%d" % k: [c for c in r if c < 32] for k, r in enumerate(TILES) if k >= NV})
+        needs.update({(d, h): ["full"] for d in range(1, D + 1) for h in (0, 1)})
+        issued = []
 
-        def halved(b): act(w("FH", 512 * b, 512 * b + 512), w("P%d" % b), AF.Copy, 0.5)
+        def issue(plan, upto):
+            for step in plan[:plan.index(upto) + 1]:
+                if step in issued: continue
+                for other in needs.get(step, ()): issue(VPLAN if other in VPLAN else SPLAN, other)
+                issued.append(step)
+                if step in steps: steps[step]()
+                elif isinstance(step, str): done(int(step[1:]))
+                elif isinstance(step, tuple): apart(*step)
+                else: srow(step)
 
-        if t:
-            unpacked(0)
-            unpacked(1)
-        if t == 0: small_constants()
-        tt(w("PAY", 0, 256), ind(w(tb), w(ll, 0, 16)), w("OWS", 0, 256), OP.mult)
-        tt(w("T1"), w("RS"), w("T2"), OP.add)
-        act(w("T3"), w("T1"), AF.Copy, w("UP"))
-        lift("EXA", "PD", 0, 256)
-        lift("EXA", "PD", 256, 512)
-        act(w(lr), ind(w("IOTA", 0, 512), w(ll)), AF.Copy)
-        if t == 0: unpacked(0)
-        scan(w("OWS", 256, 512), w("I1", 256, 512), w(br, 256, 512), OP.max, OP.mult)
-        tt(w("RK"), top("EXA", 0, 512), w("T3"), OP.subtract)
-        tt(w("PAY", 256, 512), ind(w(tb), w(ll, 16, 32)), w("OWS", 256, 512), OP.mult)
-        ts(w("RKU"), w("RK"), w("MC"), w("R15"), OP.mult, OP.add)
-        if t == 0:
-            unpacked(1)
-            unpacked(2)
-        for b in ((2, 3, 0, 1) if t else (0, 1, 2)): halved(b)
-        cp(ind(w("POS"), w("RKU")), w("PAY"))
-        act(w("POSA", 0, 192), w("POS", 0, 192), AF.Abs, 4.0)
-        act(w("POSA", 192, 512), w("POS", 192, 512), AF.Abs, 4.0)
-        if t == 0:
-            unpacked(3)
-            halved(3)
+        issue(VPLAN, VPLAN[-1])
+        for b in range(4): halved(b)
         ts(w("F5", 0, 256), w("POS", 1, 512, 2), 0.0, 512.0, OP.is_lt, OP.mult)
         ts(w("FM", 1, 257), w("POS", 1, 512, 2), 0.0, -511.0, OP.is_lt, OP.mult)
 
-        def pair(a, b): scan(w("PKD", a, b), w("PK", 0, b - a), w("POSA", a, b), OP.mult, OP.add)
+        def pair(i): scan(w("PKD", CUTS[i], CUTS[i + 1]), w("PK", 0, CUTS[i + 1] - CUTS[i]), w("POS", CUTS[i], CUTS[i + 1]), OP.mult, OP.add)
 
-        pair(0, 96)
-        scan(w("VP", 0, 257), w("FM", 0, 257), w("F5", 0, 257), OP.add, OP.add)
-        pair(96, 192)
-        lift("EXB", "VP", 0, 256)
+        pair(0)
+        scan(w("VP", 0, 257), w("FM", 0, 257), w("F5", 0, 257), OP.add, OP.add, 1024.0)
+        pair(1)
+        lift("EXB", "VP", 0, 256, "CY")
         ts(w("TOT"), w("VP", 256, 257), w("NUP"), w("NUQ"), OP.mult, OP.add)
-        pair(192, 288)
-        tt(w("NB"), w("JS"), top("EXB", 0, 256), OP.subtract)
+        pair(2)
         ts(w("NA"), top("EXB", 0, 256), w("TOT"), None, OP.add)
-        pair(288, 400)
+        tt(w("NB"), w("JS"), top("EXB", 0, 256), OP.subtract)
+        pair(3)
         tt(w("NN"), w("NA"), w("NB"), OP.max)
-        pair(400, 512)
-        ts(w("NU"), w("NN"), w("MC"), 0.25, OP.mult, OP.add)
+        pair(4)
+        ts(w("NU"), w("NN"), w("M2"), 0.25, OP.mult, OP.add)
         cp(ind(w("FO"), w("NU")), w("PKD", 1, 512, 2))
-        sp = SP[t]
-        nv = 4 if last else 3
-        for b in range(nv): act(w("FB", 512 * b, 512 * b + sp), w("P%d" % b, 0, sp), AF.Copy)
-        def firsts(a): ts(w(kq, a, a + 8), top("EXK", 16 * a, 16 * a + 128), w("MK"), -513.0 / 512.0 - 0.499, OP.mult, OP.add)
+        va = 0 if last else 256
+        sa, nv = 256 - va, NPICK[t]
+        for b in range(nv): act(w("FB", 256 * b, 256 * b + 256), w("P%d" % b, va, va + 256), AF.Copy)
+        def ks(h): ts(w("KQI", 16 * h, 16 * h + 8), w("KQV", 8 * h, 8 * h + 8), 11, 511, OP.logical_shift_right, OP.bitwise_and)
+        def qs(h): ts(w("KQI", 16 * h + 8, 16 * h + 16), w("KQV", 8 * h, 8 * h + 8), 511, None, OP.bitwise_and)
 
-        lift("EXK", "FO", 0, 128)
-        lift("EXK", "FO", 128, 256)
-        firsts(0)
-        down(w("KQV"), "EXK", 0, 256, -513.0)
-        firsts(8)
-        ts(w("KQI", 0, 8), w("KQV", 0, 8), 511, None, OP.bitwise_and)
-        ts(w("KQI", 8, 16), w("KQV", 8, 16), 511, None, OP.bitwise_and)
-        cp(w(kq, 16, 24), w("KQI", 0, 8))
-        cp(w(kq, 24, 32), w("KQI", 8, 16))
+        for h in range(2): lift("EXK", "FO", 128 * h, 128 * h + 128)
+        for h in range(2): ts(w("KQV", 8 * h, 8 * h + 8), top("EXK", 128 * h, 128 * h + 128), w("MK"), 1024.0 * 2049, OP.mult, OP.add)
+        ks(0)
+        qs(0)
+        ks(1)
+        cp(w(kq, 0, 16), w("KQI", 0, 16))
+        qs(1)
 
         def first(h, b):
-            o, i = (8, 512) if h == "L" else (0, 0)
+            o, i = (16, 512) if h == "L" else (0, 0)
             act(w("KB", i + 128 * b, i + 128 * b + 128), ind(w("FH", 512 * b, 512 * b + 512), w(kq, o, o + 8)), AF.Copy)
 
         def second(h, b):
-            o, i = (24, 512) if h == "L" else (16, 0)
+            o, i = (24, 512) if h == "L" else (8, 0)
             tt(w("A%s%d" % (h, t), b, 512, 4), ind(w("FH", 512 * b, 512 * b + 512), w(kq, o, o + 8)), w("KB", i + 128 * b, i + 128 * b + 128), OP.add)
 
         def pack(h): quant(w("A%sQ%d" % (h, t)), w("A%sS%d" % (h, t)), w("A%s%d" % (h, t)))
 
         def turn_rows():
             act(w("LQK%d" % t, 0, 128), ind(w(lr), w(kq, 24, 32)), AF.Copy)
-            act(w("LQK%d" % t, 128, 256), ind(w(lr), w(kq, 8, 16)), AF.Copy)
+            act(w("LQK%d" % t, 128, 256), ind(w(lr), w(kq, 16, 24)), AF.Copy)
 
-        for b in range(4): first("K", b)
-        act(w("NMR"), ind(w(lr), w(kq, 16, 24)), AF.Copy)
-        for b in range(4): second("K", b)
+        act(w("NMR"), ind(w(lr), w(kq, 8, 16)), AF.Copy)
+        for b in range(1, 4): first("K", b)
+        cp(w(kq, 16, 32), w("KQI", 16, 32))
+        cp(w("KB", 0, 128), ind(w("FH", 0, 512), w(kq, 0, 8)))
         lift("EXN", "NMR", 0, 128)
-        pack("K")
+        second("K", 0)
         down(w("NL%d" % t), "EXN", 0, 128)
-        vq, vs = "SQ%d" % t, "SS%d" % t
         send(nxt[t], w("NLI%d" % t), w("NL%d" % t), "nma%d" % t, "nml%d" % t)
+        for b in (1, 2, 3): second("K", b)
+        pack("K")
+        vq, vs = "SQ%d" % t, "SS%d" % t
         send(nxt[t], cast(w(vq, 0, 128), dt.uint8), cast(w("AKQ%d" % t), dt.uint8), "cda%d" % t, "cdl%d" % t, 2)
         send(nxt[t], w(vs, 0, 128), w("AKS%d" % t), "cda%d" % t, "cdl%d" % t, 2)
-        cp(ind(w("EW"), w(kq, 24, 32)), w("IOTA", 128, 256))
-        turn_rows()
-        for b in range(4): first("L", b)
-        turn(t, 0)
-        second("L", 0)
-        turn(t, 1)
-        turned(t)
-        for b in range(1, 4): second("L", b)
-
-        def layer(a):
-            for b in range(4):
-                mm(w("P" + "ABCD"[b], 0, 128), w("WQ", 128 * b, 128 * b + 128), w("WS", 128 * b, 128 * b + 128), w(vq, a, a + 128), w(vs, a, a + 128))
-                act(w("HS", HW * b + a, HW * b + a + 128), w("P" + "ABCD"[b], 0, 128), AF.Copy, 0.03125)
-
         lands(prv[t], [w("NLI%d" % t)], "nma%d" % t)
         lands(prv[t], [w(vq, 0, 128), w(vs, 0, 128)], "cda%d" % t)
-        layer(0)
-        cp(ind(w("EW"), w("NLI%d" % t)), w("IOTA", 0, 128))
-        quant(w(vq, 128, 256), w(vs, 128, 256), w("AL%d" % t))
-        layer(128)
-        lift("EXE", "EW", 0, 256)
-        lift("EXE", "EW", 256, 512)
-        if last:
-            quant(w("VQ"), w("VQS"), w("VB"))
-            down(w("EL"), "EXE", 0, 512)
-        else:
-            lift("EXA", "NR%d" % t, 0, 192)
-            down(w("EL"), "EXE", 0, 512)
-            lift("EXA", "NR%d" % t, 192, 384)
+
+        def layer():
+            quant(w(vq, 128, 256), w(vs, 128, 256), w("AL%d" % t))
+            for b in range(4):
+                mm(w("P" + "ABCD"[b], 0, 256), w("WQ", 128 * b, 128 * b + 128), w("WS", 128 * b, 128 * b + 128), w(vq), w(vs))
+                act(w("HS", HW * b, HW * b + 256), w("P" + "ABCD"[b], 0, 256), AF.Copy, 0.03125)
+
+        def turn(a, e): cp(ind(w(lr), w(kq, 16 + a, 16 + e)), w("LQK%d" % t, 16 * a, 16 * e))
+
+        after = {
+            "rows": turn_rows, "k": lambda: [first("L", b) for b in range(4)], "q": lambda: [second("L", b) for b in range(4)], "layer": layer,
+            "turn": lambda: turn(0, 16), "turn0": lambda: turn(0, 8), "turn1": lambda: turn(8, 16), "turned": lambda: turned(t),
+            "own": lambda: cp(ind(w("EW"), w(kq, 24, 32)), w("IOTA", 128, 256)), "came": lambda: cp(ind(w("EW"), w("NLI%d" % t)), w("IOTA", 0, 128)),
+        }
+        for step in AFTER[t]: after[step]()
+        lift("EXE", "EW", va, va + 256)
+        lift("EXE", "EW", sa, sa + 256)
+        down(w("EL", va // 16, va // 16 + 16), "EXE", va, va + 256)
+        down(w("EL", sa // 16, sa // 16 + 16), "EXE", sa, sa + 256)
         xn = "XN%d" % t
 
-        def picked(b, a, e): return ind(w("HS", HW * b, HW * b + HW), w("EL", a // 16, e // 16))
-        if nv < 4: act(w("GB", 1024, 1024 + sp), picked(3, 0, sp), AF.Copy)
-        for b in range(4): act(w("GB", 256 * b, 256 * b + 512 - sp), picked(b, sp, 512), AF.Copy)
-        for b in range(nv): tt(w(xn, b, 4 * sp, 4), picked(b, 0, sp), w("FB", 512 * b, 512 * b + sp), OP.add)
-        if nv < 4: tt(w(xn, 3, 4 * sp, 4), w("GB", 1024, 1024 + sp), w("P3", 0, sp), OP.add)
+        def picked(b, a): return ind(w("HS", HW * b, HW * b + HW), w("EL", a // 16, a // 16 + 16))
+        for b in range(nv, 4): act(w("GB", 256 * b + 512, 256 * b + 768), picked(b, va), AF.Copy)
+        for b in range(4): act(w("GB", 256 * b, 256 * b + 256), picked(b, sa), AF.Copy)
+        for b in range(nv): tt(w(xn, 4 * va + b, 4 * va + 1024, 4), picked(b, va), w("FB", 256 * b, 256 * b + 256), OP.add)
+        for b in range(nv, 4): tt(w(xn, 4 * va + b, 4 * va + 1024, 4), w("GB", 256 * b + 512, 256 * b + 768), w("P%d" % b, va, va + 256), OP.add)
 
-        def upper(b, a=sp, e=512): tt(w(xn, 4 * a + b, 4 * e, 4), w("GB", 256 * b + a - sp, 256 * b + e - sp), w("P%d" % b, a, e), OP.add)
+        def upper(b, a=sa, e=sa + 256): tt(w(xn, 4 * a + b, 4 * e, 4), w("GB", 256 * b + a - sa, 256 * b + e - sa), w("P%d" % b, a, e), OP.add)
 
         if not last:
-            lift("EXA", "NR%d" % t, 384, 512)
-            pack_x(t + 1, 0)
-            half(t + 1, 0, 0)
             upper(0)
+            pack_x(t + 1, 1)
+            half(t + 1, 1, 0)
             upper(1)
-            half(t + 1, 0, 1)
             upper(2)
-            half(t + 1, 0, 2)
             upper(3)
-            down(w("NLL"), "EXA", 0, 512)
-            send(prv[t], w("LL%d" % (t + 1)), w("NLL"), "tra%d" % t, "trl%d" % t)
-            send(T.cores[(rank - 2 ** t + 2 ** (t + 1)) % N], w("LI%d" % (t + 1)), w("NLL"), "lia%d" % (t + 1), "lil%d" % (t + 1))
-            lands(nxt[t], [w("LL%d" % (t + 1))], "tra%d" % t)
+            half(t + 1, 1, 1)
 
-    t, o, stores = ROUNDS - 1, 512 * ROUNDS, 9
+    t, o, stores, sp = ROUNDS - 1, 512 * ROUNDS, 9, 256
     pieces = [(0, sp)] + list(TAIL)
 
     def store(i):

@@ -6,20 +6,24 @@ HW = 264
 BIG = 2.0 ** 32
 B4 = 2.0 ** 20
 FAR = 1e25
-C0 = 25
-D, WV = (C0 - 1) // 2, 16 * C0
-NPICK = (4, 4)
+C0 = 26
+D, WV, EVEN = C0 // 2, 16 * C0, 1 - C0 % 2
+VW = 256
+BETWEEN = (1, 2, 3, 0)
+HFIRST = False
 COPIES = (4, 2)
 TAIL = ((256, 384), (384, 512))
-VPAD = 10
-CUTS = (0, 108, 216, 296, 404, 512)
+VPAD, SPAD = 7, 6
+WHOLE = 1.5 * 2.0 ** 33
+CUTS = (0, 90, 180, 270, 334, 424, 512)
 LAG = 2
 ROWS = list(range(31, C0 - 1, -1))
 DS = WV // 4 + 4
-AT = {**{d: DS * d - WV // 4 for d in range(1, D + 1)}, **{c: DS * D + 128 * i for i, c in enumerate([32] + ROWS)}}
-TILES = [[d - 1, d] for d in range(D, 0, -2)]
+AT = {**{d: DS * d - WV // 4 for d in range(1, D + 1)}, **{c: DS * D - EVEN * WV // 8 + 128 * i for i, c in enumerate([32] + ROWS)}}
+TILES = [list(range(D - 1 - D % 2, D + 1))] + [[d - 1, d] for d in range(D - 2 - D % 2, 1, -2)]
 NV = len(TILES)
-TILES += [[32, 31], [30, 29], [28, 27], [26], [25]]
+TILES += [[32, 31]] + [ROWS[i:i + 2] for i in range(1, len(ROWS) - 2, 2)] + [ROWS[-2:-1]] * (1 - EVEN) + [ROWS[-1:]]
+SV = ["T%d" % k for k in range(NV, len(TILES))]
 CODES, F32, BF, F16 = "float8_e4m3fn_x4", "float32", "bfloat16", "float16"
 
 SCRATCH = {}
@@ -30,9 +34,9 @@ def buf(names, cols, dtype, where="sbuf"):
 
 
 buf("X0 XN0 XN1 FH FB", 2048, BF)
-buf("UB VB OA OB OC BR0 BR1 TB0 TB1 EA EW AK0 AK1 AL0 AL1", 512, BF)
-buf("AROW KM RZ CY", 256, BF)
-buf("CT", 384, BF)
+buf("UB VB OA OB OC BR0 BR1 TB0 TB1 EA EW DR AK0 AK1 AL0 AL1", 512, BF)
+buf("AROW KM RZ CY SL", 256, BF)
+buf("CT", VW + 128, BF)
 buf("RM", WV // 4, BF)
 buf("RD0", 512 - WV, BF)
 buf("Z", 520, BF)
@@ -49,7 +53,7 @@ buf("QT", AT[C0] + 256, CODES)
 buf("QS", AT[C0] + 256, "uint8")
 buf("BT", 4 * AT[C0] + 512, BF)
 buf("SG", 3 * 512, BF)
-buf("I1 PAY", 512, F16)
+buf("I1 OW PAY", 512, F16)
 buf("RD", 512 - WV, F16)
 buf("F5 FM VP EXB", 264, F16)
 buf("EXE", 512, BF)
@@ -64,7 +68,7 @@ buf("WK", 192, F32)
 buf("EX", 896, F32)
 buf("II", 48, "int32")
 buf("U16", 80, "uint16")
-buf("IOTA", 512, F32)
+buf("IOTA", 520, F32)
 buf("MSK H POS PKD YS LR0 LR1 NR0 NR1", 512, F32)
 buf("HF", WV, F32)
 buf("FO LQK0 LQK1", 256, F32)
@@ -79,10 +83,10 @@ buf("BRD1 BRX1", 32 * COPIES[1], BF, "dram")
 buf("PA PB PC PD P0 P1 P2 P3", 512, F32, "psum")
 
 PIECE = {
-    "PM": ("SM", 0, 2), "E8": ("SM", 2, 2), "NUP": ("SM", 4, 1), "NUQ": ("SM", 5, 1), "R15": ("SM", 6, 1), "PU": ("SM", 7, 1),
-    "MC": ("SM", 10, 1), "U4": ("SM", 11, 1), "M2": ("SM", 12, 1), "U2": ("SM", 13, 1), "NL": ("SM", 14, 1), "IL": ("SM", 15, 1),
+    "PM": ("SM", 0, 2), "E8": ("SM", 2, 2), "E4": ("SM", 8, 2), "NUP": ("SM", 4, 1), "NUQ": ("SM", 5, 1), "R15": ("SM", 6, 1), "PU": ("SM", 7, 1),
+    "MC": ("SM", 10, 1), "U4": ("SM", 11, 1), "M2": ("SM", 12, 1), "U2": ("SM", 13, 1), "U1": ("SM", 14, 1), "IL": ("SM", 15, 1),
     "N4": ("SM", 16, 1), "I4": ("SM", 17, 1), "M4": ("SM", 18, 1), "S4": ("SM", 19, 1), "NU4": ("SM", 20, 1), "MK": ("SM", 21, 1),
-    "CX": ("CT", 0, 256), "C4": ("CT", 256, 128),
+    "CX": ("CT", 0, VW), "C4": ("CT", VW, 128),
     "EXS": ("EX", 0, 128), "EXV": ("EX", 128, 128), "EXR": ("EX", 256, 128),
     "UOI": ("INT", 0, 16), "HOI": ("INT", 16, 32), "PI": ("INT", 48, 2), "PJ": ("INT", 50, 2),
     "T1": ("WK", 0, 32), "T3": ("WK", 32, 32), "RK": ("WK", 64, 32), "NA": ("WK", 96, 16), "NB": ("WK", 112, 16), "NN": ("WK", 128, 16),
@@ -95,16 +99,18 @@ SEMAPHORES = ["cv", "cs", "ct", "cg", "ldx0", "ldx1", "ldu", "ldk", "ldv", "ldw"
 for _t in range(ROUNDS):
     SEMAPHORES += [s + "%d" % _t for s in ("bro", "bra", "brl", "tbx", "nma", "nml", "cda", "cdl", "tro", "tra", "trl", "trx", "lia", "lil")]
 
-def both(k): return [(d, h) for d in reversed(TILES[k]) for h in (0, 1)]
+def both(k): return [(d, h) for d in reversed(TILES[k]) for h in (0, 1) if (d, h) != (D, EVEN)  or not EVEN]
 
 
 def then(k, *more): return both(k)[:1] + ["T%d" % (k - 1)] + both(k)[1:] + list(more)
 
 
-VPLAN = (["ones", "in1", "mask", (12, 2), "hold", (11, 2), "in0", (10, 2), (9, 2), "bits", (1, 3), (2, 3), (3, 3), "AQ", "F", "OQ"] + both(0) + ["turn"] + then(1, "links") + then(2, "T6") + then(3) + then(4, "T7")
-         + then(5) + ["RDU", "T8", "T5", "T9", "T10", "high", "EA0", "small", "CV", "RDL", "PAY0", "EXS", "low", "EA1", "RK", "PAY1", "RKU", "spare0", "POS", "spare1"])
-SPLAN = ["ahead", "full"] + ROWS + ["LR"]
-AFTER = [["rows", "k", "turn", "turned", "q", "own", "layer", "came"]] * 2
+VPLAN = (["ones", "turn", "in1", "mask", (D, 2), "links", "U2", "hold", (D - 1, 2), "PU", "in0", "bits", (D - 2, 2)] + [(d, 2) for d in range(D - 3, C0 - 17, -1)] + [(1, 3), (2, 3), (3, 3), "AQ", "F", "OQ"] + both(0)
+         + then(1) + then(2, "T6") + then(3) + then(4) + then(5, "T7")
+         + ["T5", "T8", "RDU", "small", "T9", "high", "OW", "u0", "u1", "CV", "lifted", "RDL", "EXS", "R15", "low", "PAY0", "RK", "PAY1", "u2", "RKU", "spare0", "POS", "spare1"])
+SPLAN = ["ahead", "full"] + ROWS + ["twin0", "twin1", "LR"]
+AFTER = [["rows", "k", "turn", "turned", "q", "layer", "came"]] * 2
+SLOTS = ((0, 256),)
 EARLY = 2
 
 
@@ -248,26 +254,38 @@ def rank_program(g, core, T, topo):
     iotai(w("PI"), [[0, 2]], 0, 1)
     iotai(w("UOI"), [[1, 2], [16, 8]], 0, 0)
     iotai(w("HOI"), [[16, 32]], 15, 0)
-    select(w("Z"), w("ZB", 0, 520), [[1, 520]], OP.not_equal, 1.0, -3, -4)
     iota(w("AROW"), [[0, 16], [1, 16]], 0, 0)
     iota(w("E8"), [[0, 2]], -3, -8)
-    iota(w("IOTA"), [[1, 512]], 0, 0)
+    iota(w("IOTA"), [[1, 520]], 0, 0)
+    iota(w("E4"), [[0, 2]], -3, -4)
+    pads = [(4 * AT[c] + 16 * c, 512 - 16 * c) for c in reversed(ROWS)] + [(4 * AT[d] - 16, 16) for d in range(1, D + 1)]
     ts(w("PJ"), w("PI"), 15, None, OP.bitwise_and)
+    for a, n in pads[-3:]: fill(w("BT", a, a + n), 0.0)
     cp(w("UO"), w("INT", 0, 48))
     cp(w("PM"), w("PJ"))
     pm = w("PM", 0, 1)
     quant(w("QT", AT[32], AT[32] + 128), w("QS", AT[32], AT[32] + 128), w("ZB", 0, 512))
-    pads = [(4 * AT[c] + 16 * c, 512 - 16 * c) for c in reversed(ROWS)] + [(4 * AT[d] - 16, 16) for d in range(1, D + 1)]
-    for a, n in pads[:VPAD]: fill(w("BT", a, a + n), 0.0)
+    for a, n in pads[VPAD:VPAD + SPAD]: act(w("BT", a, a + n), w("ZB", 0, n), AF.Copy)
+    column = {
+        "U1": lambda: ts(w("U1"), pm, 15.0, 1.0, OP.is_lt, OP.add), "U2": lambda: ts(w("U2"), w("U1"), 1.0 / 512, None, OP.mult),
+        "PU": lambda: ts(w("PU"), pm, 1024.0, w("U2"), OP.add, OP.mult), "NUP": lambda: ts(w("NUP"), pm, 15.0, 2.0, OP.is_equal, OP.subtract),
+        "M2": lambda: ts(w("M2"), pm, 15.0, 0.5, OP.is_equal, OP.max), "M4": lambda: ts(w("M4"), pm, 12.0, 1.0 / B4, OP.is_ge, OP.max),
+        "MC": lambda: ts(w("MC"), pm, 15.0, 1.0 / BIG, OP.is_equal, OP.max),
+        "R15": lambda: ts(w("R15"), pm, -1.0, 16 * (D - EVEN) + 15.25, OP.mult, OP.add),
+    }
+    ts(w("N4"), pm, 12.0, B4, OP.is_lt, OP.mult)
+    for a, n in pads[:4]: fill(w("BT", a, a + n), 0.0)
+    ts(w("KM"), w("AROW"), pm, -2.0 * FAR, OP.not_equal, OP.mult)
+    ts(w("U4"), w("N4"), 1.0, None, OP.max)
     quant(w("UQ"), w("UQS"), w("UB"))
     select(w("ZB", 448, 512), w("ZB", 448, 512), [[0, 4], [-1, 4], [1, 4]], OP.not_equal, 1.0, 0, 0)
     for i in range(8): dma("y", w("OC", rows=slice(16 * i, 16 * i + 16)), w("ZB", 448 - 64 * i, 960 - 64 * i, rows=slice(16 * i, 16 * i + 16)), "ldo", 8)
 
     def lift_constants():
-        select(w("C4", rows=r16), w("C4", rows=r16), [[0, 32], [4, 4]], OP.is_gt, B4, -4, -1)
-        select(w("CX", rows=r16), w("CX", rows=r16), [[0, 16], [1, 16]], OP.is_gt, 0.0, 0, -1)
-        select(w("C4", rows=r16), w("C4", rows=r16), [[0, 32], [4, 4]], OP.is_gt, 0.0, 0, -1)
-        select(w("CX", rows=r16), w("CX", rows=r16), [[0, 16], [1, 16]], OP.not_equal, BIG, -1, -1)
+        select(w("C4", rows=r16), w("ZB", 0, 128, rows=r16), [[0, 32], [-4, 4]], OP.is_ge, B4, 0, 1)
+        select(w("CX", rows=r16), w("ZB", 0, VW, rows=r16), [[0, VW // 16], [-1, 16]], OP.is_ge, 1.0, 0, 1)
+        select(w("C4", rows=r16), w("C4", rows=r16), [[0, 32], [-4, 4]], OP.is_ge, 1.0, 4, 1)
+        select(w("CX", rows=r16), w("CX", rows=r16), [[0, VW // 16], [1, 16]], OP.not_equal, BIG, -1, -1)
         for i in range(1, 8): dma("y", w("CT", rows=slice(16 * i, 16 * i + 16)), w("CT", rows=r16), "ldc", 7)
 
     def pick_u(q, o):
@@ -287,43 +305,24 @@ def rank_program(g, core, T, topo):
             mm(w("P" + "DC"[h], 0, 256), w("UT"), w("UTS"), *xq(t, h))
         if step == 1: tt(w("MSK", a, a + 256), w("P" + "3A"[h], 0, 256), w("KM"), OP.add)
         if step == 2: scan(w("H", a, a + 256), w("RZ"), w("MSK", a, a + 256), OP.min, OP.max)
-        if step == 3: ts(w("BR%d" % t, a, a + 256), w("P" + "DC"[h], 0, 256), 0.0, None, OP.is_gt)
+        if step == 3: ts(w("BR%d" % t, a, a + 256), w("P" + "DC"[h], 0, 256), 0.0, 1024.0, OP.is_gt, OP.mult)
         if step == 4: act(w("HF", a, min(a + 256, WV)), ind(w("H", a, a + 256), w("UO", 16, 16 + min(16, C0 - 16 * h))), AF.Copy)
 
-    act(w("NL"), pm, AF.Sign, -1.0, 15.0)
-    act(w("R15"), pm, AF.Copy, -1.0, 16 * D + 15.25)
-    act(w("PU"), pm, AF.Copy, 1.0, 1024.0)
-    act(w("IL"), w("NL"), AF.Copy, -1.0, 1.0)
-    act(w("U2"), w("NL"), AF.Copy, 1.0, 1.0)
-    act(w("S4"), pm, AF.Sign, -1.0, 11.5)
-    act(w("M2"), w("NL"), AF.Copy, -0.5, 1.0)
-    act(w("N4"), w("S4"), AF.Copy, 0.5, 0.5)
-    act(w("I4"), w("S4"), AF.Copy, -0.5, 0.5)
-    act(w("NUP"), w("NL"), AF.Copy, -1.0, -1.0)
-    act(w("NUQ"), w("NL"), AF.Copy, -256.0, -256.0)
-    act(w("MC"), w("IL"), AF.Copy, 1.0, 1.0 / BIG)
-    act(w("PU"), w("PU"), AF.Copy, w("U2"))
-    act(w("MK"), w("IL"), AF.Copy, 1024.0, 1024.0 / BIG)
-    act(w("U4"), w("N4"), AF.Copy, B4 - 1.0, 1.0)
-    act(w("NU4"), w("N4"), AF.Copy, 1.0 - B4, -1.0)
-    act(w("M4"), w("I4"), AF.Copy, 1.0 - 1.0 / B4, 1.0 / B4)
+    for n in ("U1", "M4"): column[n]()
     pick_u("UR", 0)
-    unit(0)
-    unit(1)
-    pick_u("UT", 8)
-    act(w("RZ"), w("AROW"), AF.Copy, 2.0 * FAR, -FAR)
-    for a, n in pads[VPAD:]: act(w("BT", a, a + n), w("ZB", 0, n), AF.Copy)
-    unit(2)
+    for a, n in pads[VPAD + SPAD:-3]: fill(w("BT", a, a + n), 0.0)
     pack_x(0, 1)
-    half(0, 1, 0)
-    ts(w("KM"), w("AROW"), pm, -2.0 * FAR, OP.not_equal, OP.mult)
+    mm(w("PA", 0, 256), w("UR"), w("URS"), *xq(0, 1))
+    pick_u("UT", 8)
+    mm(w("PC", 0, 256), w("UT"), w("UTS"), *xq(0, 1))
+    act(w("RZ"), w("AROW"), AF.Copy, 2.0 * FAR, -FAR)
     cp(w("LL0"), w("LINKI"))
     send(nxt[0], w("LI0"), w("LL0"), "lia0", "lil0")
-    unit(3)
+    for a, n in pads[4:VPAD]: fill(w("BT", a, a + n), 0.0)
     half(0, 1, 1)
-    iota(w("CT", rows=r16), [[0, 384]], 1, 0)
+    act(w("SG", 0, 520), w("IOTA"), AF.Abs, 1.0, w("E4", 0, 1))
     act(w("OA"), w("IOTA", 0, 512), AF.Abs, 2.0, w("E8", 0, 1))
-    act(w("JS"), w("IOTA", 0, 256, 16), AF.Identity, w("U2"), w("PU"))
+    act(w("Z"), w("SG", 0, 520), AF.Relu, -1.0, 1.0)
 
     def turned(t):
         lands(T.cores[(rank - 2 ** t + 2 ** t // 2) % N], [w("LI%d" % t)], "lia%d" % t)
@@ -345,12 +344,16 @@ def rank_program(g, core, T, topo):
         if t == 0: half(t, 1, 3)
         else:
             act(w("EA", 256, 512), w("PC", 0, 256), AF.Sign)
-            act(w(br, 256, 512), w("EA", 256, 512), AF.Relu)
+            act(w(br, 256, 512), w("EA", 256, 512), AF.Relu, 1024.0)
+        if HFIRST:
+            half(t, 1, 2)
+            half(t, 1, 4)
         pack_x(t, 0)
         half(t, 0, 0)
         scores("PC", WV)
-        half(t, 1, 2)
-        half(t, 1, 4)
+        if not HFIRST:
+            half(t, 1, 2)
+            half(t, 1, 4)
 
         def links():
             if t == 0: return
@@ -387,22 +390,24 @@ def rank_program(g, core, T, topo):
                 dma("y", cast(w("WQ"), dt.uint8), hbm(T.wc[:, :]), "ldw", 2)
                 dma("y", w("WS"), hbm(T.ws[:, :]), "ldw", 2)
                 dma("y", w("VB"), hbm(T.v[:, :]), "ldv", 1)
-                iota(w("RD0"), [[-16, 32 - C0], [1024, 16]], 16 * D - WV, 0)
-                iota(w("RM"), [[0, C0], [1, 4]], 0, 0)
-                select(w("RM"), w("RM"), [[0, C0], [-1, 4]], OP.is_ge, 1.0, 0, 0)
-                iota(w("I1"), [[1, 512]], 0, 0)
+                iota(w("RD0"), [[-16, 32 - C0], [1024, 16]], 16 * (D - EVEN) - WV, 0)
+                iota(w("RM", 0, 4 * D), [[0, D], [1024, 4]], 0, 0)
+                iota(w("RM", 4 * D, 4 * C0), [[0, C0 - D], [1024, 4]], -16 * EVEN, 0)
+                iota(w("I1"), [[1, 512]], 1024, 0)
                 for z in (w("F5", 256, 257), w("FM", 0, 1)): iota(z, [[0, 1]], 0, 0)
-                iota(w("PK"), [[0, 64], [2048, 2]], 0, 0)
+                iota(w("PK"), [[0, 64], [4096, 2]], 0, 0)
                 iota(w("HS", 256, 4 * HW, HW), [[0, 4]], 0, 0)
-            iota(w("EW"), [[0, 512]], 256, 0)
+                iota(w("SL", 0, 128), [[0, 128]], 256, 0)
+                iota(w("SL", 128, 256), [[1, 128]], 128, 0)
+                iota(w("DR", 0, 512, 2), [[0, 256]], 256, 0)
 
         signed = []
 
         def done(k):
             a = AT[TILES[k][0]] - 4 * (k < NV)
-            n = len(TILES[k]) * (DS if k < NV else 128)
+            n = len(TILES[k]) * (DS if k < NV else 128) - EVEN * (k == 0) * WV // 8
             quant(*codes(a, n), w("BT", 4 * a, 4 * (a + n)))
-            won = [AT[d] + WV // 4 - 4 * d for d in TILES[k]] + [0] * (k == NV - 1) if k < NV else [AT[32]] * (k == NV)
+            won = [AT[d] + WV // 4 - 4 * d for d in TILES[k] if d < D + 1 - EVEN] + [0] * (k == NV - 1) if k < NV else [AT[32]] * (k == NV)
             for c in TILES[k]: mm(w("P3" if k < NV else "PD", 0, 128), w("OQ"), w("OQS"), *codes(AT[c], 128), c in (TILES[0][0], 32), c in (TILES[NV - 1][-1], C0))
             for a in won: mm(w("PA", 0, 128), w("AQ"), w("AQS"), *codes(a, 128), k == 0 and a == won[0], k == NV - 1 and a == won[-1])
 
@@ -416,37 +421,39 @@ def rank_program(g, core, T, topo):
             beats(c)
 
         def low():
-            tt(w("T1", 0, C0), w("EXV", 3, WV // 4, 4), w("EXR", 3, WV // 4, 4), OP.subtract)
+            tt(w("T1", 0, C0), w("EXR", 3, WV // 4, 4), w("EXV", 3, WV // 4, 4), OP.subtract)
 
         def high():
             tt(w("T3", C0, 32), w("RS", C0, 32), w("RD", 15, 512 - WV, 16), OP.add)
-            act(w("T1", C0, 32), w("T3", C0, 32), AF.Copy, w("NU4"))
 
-        def differ(a): tt(w("EA", a, a + 256), ind(w(tb), w(ll, a // 16, a // 16 + 16)), w(br, a, a + 256), OP.not_equal)
-        def pay(a, b): scan(w("PAY", a, b), w("I1", a, b), w("EA", a, b), OP.max, OP.subtract)
+        def twin(a): act(w("EA", a, a + 256), ind(w(tb), w(ll, a // 16, a // 16 + 16)), AF.Copy, -1.0, 2048.0)
+        def pay(a, b): scan(w("PAY", a, b), w("OW", a, b), w("EA", a, b), OP.max, OP.subtract)
 
         steps = {
             "in0": lambda: inside(0), "in1": lambda: inside(1), "ahead": lambda: ahead(1), "low": low, "high": high,
             "mask": lambda: half(t, 0, 1), "hold": lambda: half(t, 0, 2), "full": lambda: half(t, 0, 4), "bits": bits, "links": links,
             "turn": lambda: op("v", lambda: V.transpose(w("NX")[0], w("NT")[0]), [w("NT")], [w("NX")]) if t else None,
             "ones": lambda: ts(w("OB"), w("OA"), 4.0, w("U4"), OP.is_lt, OP.mult) if t == 0 else None,
-            "F": lambda: [unpack(b) for b in range(EARLY)],
+            "F": lambda: [unpack(b) for b in range(EARLY if t else 0)],
             "AQ": lambda: quant(w("AQ"), w("AQS"), w("OB")) if t == 0 else None,
             "OQ": lambda: quant(w("OQ"), w("OQS"), w("OC")) if t == 0 else None,
             "RDU": lambda: scan(w("RD"), w("RD0"), slot(32, WV, 512), OP.min, OP.add),
-            "RDL": lambda: scan(w("EXR", 0, WV // 4), w("RM"), w("PA", 0, WV // 4), OP.mult, OP.add),
+            "RDL": lambda: scan(w("EXR", 0, WV // 4), w("RM"), w("PA", 0, WV // 4), OP.min, OP.add),
             "CV": lambda: scan(w("EXV", 0, WV // 4), w("C4", 0, WV // 4), w("P3", 0, WV // 4), OP.mult, OP.add),
-            "EA0": lambda: differ(0), "EA1": lambda: differ(256), "PAY0": lambda: pay(0, 256), "PAY1": lambda: pay(256, 512),
-            "small": lambda: ts(w("I1"), w("I1"), 1.0 / 1024, None, OP.mult) if t == 0 else None,
+            "twin0": lambda: twin(0), "twin1": lambda: twin(256), "PAY0": lambda: pay(0, 256), "PAY1": lambda: pay(256, 512),
+            "OW": lambda: scan(w("OW"), w("I1"), w(br), OP.max, OP.subtract),
+            "u0": lambda: unit(0) if t == 0 else None, "u1": lambda: unit(1) if t == 0 else None, "u2": lambda: (unit(2), unpack(2)) if t == 0 else None,
+            "lifted": lambda: ts(w("T1", C0, 32), w("T3", C0, 32), w("U4"), None, OP.mult),
+            "small": lambda: ts(w("RM"), w("RM"), w("U4"), None, OP.mult) if t == 0 else None,
             "LR": lambda: act(w(lr), ind(w("IOTA", 0, 512), w(ll)), AF.Copy),
-            "EXS": lambda: (scan(w("EXS"), w("C4"), w("PD", 0, 128), OP.mult, OP.add), [unpack(b) for b in range(EARLY, 4)]),
-            "RK": lambda: tt(w("RK"), w("EXS", 3, 128, 4), w("T1"), OP.add),
+            "EXS": lambda: (scan(w("EXS"), w("C4"), w("PD", 0, 128), OP.mult, OP.add), [unpack(b) for b in (range(EARLY, 4) if t else (0, 1))]),
+            "RK": lambda: tt(w("RK"), w("EXS", 3, 128, 4), w("T1"), OP.subtract),
             "RKU": lambda: ts(w("RKU"), w("RK"), w("M4"), w("R15"), OP.mult, OP.add),
             "POS": lambda: cp(ind(w("POS"), w("RKU")), w("PAY")),
-            "spare0": lambda: quant(w("VQ"), w("VQS"), w("VB")) if last else None,
-            "spare1": lambda: ts(w("CY"), w("CX"), 2.0, None, OP.min) if t == 0 else None,
+            "spare0": lambda: quant(w("VQ"), w("VQS"), w("VB")) if last else (unit(3), unpack(3)),
+            "spare1": lambda: ts(w("CY"), w("CX", 0, 256), 2.0, None, OP.min) if t == 0 else None,
         }
-        needs = {"full": ["hold"], "LR": ["links"], "EXS": ["LR"]}
+        needs = {"full": ["hold"], "twin0": ["links"], "PAY0": ["twin0"], "PAY1": ["LR"]}
         needs.update({"T%d" % k: [c for c in r if c < 32] for k, r in enumerate(TILES) if k >= NV})
         needs.update({(d, h): ["full"] for d in range(1, D + 1) for h in (0, 1)})
         issued = []
@@ -457,38 +464,48 @@ def rank_program(g, core, T, topo):
                 for other in needs.get(step, ()): issue(VPLAN if other in VPLAN else SPLAN, other)
                 issued.append(step)
                 if step in steps: steps[step]()
+                elif step in column: column[step]() if t == 0 else None
                 elif isinstance(step, str): done(int(step[1:]))
                 elif isinstance(step, tuple): apart(*step)
                 else: srow(step)
 
         issue(VPLAN, VPLAN[-1])
+        if t == 0: act(w("JS"), w("IOTA", 0, 256, 16), AF.Identity, w("U2"), w("PU"))
         for b in range(4): halved(b)
-        ts(w("F5", 0, 256), w("POS", 1, 512, 2), 0.0, 512.0, OP.is_lt, OP.mult)
-        ts(w("FM", 1, 257), w("POS", 1, 512, 2), 0.0, -511.0, OP.is_lt, OP.mult)
+        ts(w("F5", 0, 256), w("POS", 1, 512, 2), WHOLE, WHOLE - 1024.0, OP.add, OP.not_equal)
 
         def pair(i): scan(w("PKD", CUTS[i], CUTS[i + 1]), w("PK", 0, CUTS[i + 1] - CUTS[i]), w("POS", CUTS[i], CUTS[i + 1]), OP.mult, OP.add)
 
+        def spare(*names):
+            for n in names if t == 0 else (): column[n]()
+
         pair(0)
-        scan(w("VP", 0, 257), w("FM", 0, 257), w("F5", 0, 257), OP.add, OP.add, 1024.0)
+        spare("NUP")
+        ts(w("FM", 1, 257), w("F5", 0, 256), -511.0 / 512, None, OP.mult)
         pair(1)
-        lift("EXB", "VP", 0, 256, "CY")
-        ts(w("TOT"), w("VP", 256, 257), w("NUP"), w("NUQ"), OP.mult, OP.add)
+        spare("M2")
+        scan(w("VP", 0, 257), w("FM", 0, 257), w("F5", 0, 257), OP.add, OP.add, 2.0)
         pair(2)
-        ts(w("NA"), top("EXB", 0, 256), w("TOT"), None, OP.add)
-        tt(w("NB"), w("JS"), top("EXB", 0, 256), OP.subtract)
+        spare("MC")
+        lift("EXB", "VP", 0, 256, "CY")
+        ts(w("TOT"), w("VP", 256, 257), 0.5, w("NUP"), OP.add, OP.mult)
         pair(3)
-        tt(w("NN"), w("NA"), w("NB"), OP.max)
+        tt(w("NB"), w("JS"), top("EXB", 0, 256), OP.subtract)
+        ts(w("NA"), top("EXB", 0, 256), w("TOT"), None, OP.add)
         pair(4)
-        ts(w("NU"), w("NN"), w("M2"), 0.25, OP.mult, OP.add)
+        tt(w("NN"), w("NA"), w("NB"), OP.max)
+        pair(5)
+        ts(w("NU"), w("NN"), w("M2"), 512.0, OP.mult, OP.mult)
         cp(ind(w("FO"), w("NU")), w("PKD", 1, 512, 2))
-        va = 0 if last else 256
-        sa, nv = 256 - va, NPICK[t]
-        for b in range(nv): act(w("FB", 256 * b, 256 * b + 256), w("P%d" % b, va, va + 256), AF.Copy)
-        def ks(h): ts(w("KQI", 16 * h, 16 * h + 8), w("KQV", 8 * h, 8 * h + 8), 11, 511, OP.logical_shift_right, OP.bitwise_and)
+        (va, ve), (sa, se) = ((0, VW), (VW, 512)) if last else ((512 - VW, 512), (0, 512 - VW))
+        for b in range(4): act(w("FB", VW * b, VW * b + VW), w("P%d" % b, va, ve), AF.Copy)
+        act(w("DR", 1, 512, 2), ind(w("SL"), w("NU")), AF.Copy)
+        act(w("EW"), ind(w("DR"), w("RKU")), AF.Copy)
+        def ks(h): ts(w("KQI", 16 * h, 16 * h + 8), w("KQV", 8 * h, 8 * h + 8), 12, 511, OP.logical_shift_right, OP.bitwise_and)
         def qs(h): ts(w("KQI", 16 * h + 8, 16 * h + 16), w("KQV", 8 * h, 8 * h + 8), 511, None, OP.bitwise_and)
 
         for h in range(2): lift("EXK", "FO", 128 * h, 128 * h + 128)
-        for h in range(2): ts(w("KQV", 8 * h, 8 * h + 8), top("EXK", 128 * h, 128 * h + 128), w("MK"), 1024.0 * 2049, OP.mult, OP.add)
+        for h in range(2): ts(w("KQV", 8 * h, 8 * h + 8), top("EXK", 128 * h, 128 * h + 128), w("MC"), 2048.0 * 4097, OP.mult, OP.add)
         ks(0)
         qs(0)
         ks(1)
@@ -509,61 +526,56 @@ def rank_program(g, core, T, topo):
             act(w("LQK%d" % t, 0, 128), ind(w(lr), w(kq, 24, 32)), AF.Copy)
             act(w("LQK%d" % t, 128, 256), ind(w(lr), w(kq, 16, 24)), AF.Copy)
 
+        for b in (1, 2, 3): first("K", b)
         act(w("NMR"), ind(w(lr), w(kq, 8, 16)), AF.Copy)
-        for b in range(1, 4): first("K", b)
-        cp(w(kq, 16, 32), w("KQI", 16, 32))
         cp(w("KB", 0, 128), ind(w("FH", 0, 512), w(kq, 0, 8)))
+        cp(w(kq, 16, 32), w("KQI", 16, 32))
+        for b in (1, 0, 2, 3): second("K", b)
         lift("EXN", "NMR", 0, 128)
-        second("K", 0)
-        down(w("NL%d" % t), "EXN", 0, 128)
-        send(nxt[t], w("NLI%d" % t), w("NL%d" % t), "nma%d" % t, "nml%d" % t)
-        for b in (1, 2, 3): second("K", b)
         pack("K")
+        down(w("NL%d" % t), "EXN", 0, 128)
         vq, vs = "SQ%d" % t, "SS%d" % t
         send(nxt[t], cast(w(vq, 0, 128), dt.uint8), cast(w("AKQ%d" % t), dt.uint8), "cda%d" % t, "cdl%d" % t, 2)
         send(nxt[t], w(vs, 0, 128), w("AKS%d" % t), "cda%d" % t, "cdl%d" % t, 2)
+        send(nxt[t], w("NLI%d" % t), w("NL%d" % t), "nma%d" % t, "nml%d" % t)
         lands(prv[t], [w("NLI%d" % t)], "nma%d" % t)
         lands(prv[t], [w(vq, 0, 128), w(vs, 0, 128)], "cda%d" % t)
 
         def layer():
             quant(w(vq, 128, 256), w(vs, 128, 256), w("AL%d" % t))
-            for b in range(4):
-                mm(w("P" + "ABCD"[b], 0, 256), w("WQ", 128 * b, 128 * b + 128), w("WS", 128 * b, 128 * b + 128), w(vq), w(vs))
-                act(w("HS", HW * b, HW * b + 256), w("P" + "ABCD"[b], 0, 256), AF.Copy, 0.03125)
+            for a, e in SLOTS:
+                for b in range(4):
+                    mm(w("P" + "ABCD"[b], 0, e - a), w("WQ", 128 * b, 128 * b + 128), w("WS", 128 * b, 128 * b + 128), w(vq, a, e), w(vs, a, e))
+                    act(w("HS", HW * b + a, HW * b + e), w("P" + "ABCD"[b], 0, e - a), AF.Copy, 0.03125)
 
         def turn(a, e): cp(ind(w(lr), w(kq, 16 + a, 16 + e)), w("LQK%d" % t, 16 * a, 16 * e))
 
         after = {
             "rows": turn_rows, "k": lambda: [first("L", b) for b in range(4)], "q": lambda: [second("L", b) for b in range(4)], "layer": layer,
             "turn": lambda: turn(0, 16), "turn0": lambda: turn(0, 8), "turn1": lambda: turn(8, 16), "turned": lambda: turned(t),
-            "own": lambda: cp(ind(w("EW"), w(kq, 24, 32)), w("IOTA", 128, 256)), "came": lambda: cp(ind(w("EW"), w("NLI%d" % t)), w("IOTA", 0, 128)),
+            "came": lambda: cp(ind(w("EW"), w("NLI%d" % t)), w("IOTA", 0, 128)),
         }
         for step in AFTER[t]: after[step]()
-        lift("EXE", "EW", va, va + 256)
-        lift("EXE", "EW", sa, sa + 256)
-        down(w("EL", va // 16, va // 16 + 16), "EXE", va, va + 256)
-        down(w("EL", sa // 16, sa // 16 + 16), "EXE", sa, sa + 256)
+        for a, e in ((va, ve), (sa, se)): lift("EXE", "EW", a, e)
+        for a, e in ((va, ve), (sa, se)): down(w("EL", a // 16, e // 16), "EXE", a, e)
         xn = "XN%d" % t
 
-        def picked(b, a): return ind(w("HS", HW * b, HW * b + HW), w("EL", a // 16, a // 16 + 16))
-        for b in range(nv, 4): act(w("GB", 256 * b + 512, 256 * b + 768), picked(b, va), AF.Copy)
-        for b in range(4): act(w("GB", 256 * b, 256 * b + 256), picked(b, sa), AF.Copy)
-        for b in range(nv): tt(w(xn, 4 * va + b, 4 * va + 1024, 4), picked(b, va), w("FB", 256 * b, 256 * b + 256), OP.add)
-        for b in range(nv, 4): tt(w(xn, 4 * va + b, 4 * va + 1024, 4), w("GB", 256 * b + 512, 256 * b + 768), w("P%d" % b, va, va + 256), OP.add)
+        def picked(b, a, e): return ind(w("HS", HW * b, HW * b + HW), w("EL", a // 16, e // 16))
+        for b in range(4): act(w("GB", 256 * b, 256 * b + se - sa), picked(b, sa, se), AF.Copy)
+        if "turned" not in AFTER[t]: turned(t)
+        for b in range(4): tt(w(xn, 4 * va + b, 4 * ve, 4), picked(b, va, ve), w("FB", VW * b, VW * b + VW), OP.add)
 
-        def upper(b, a=sa, e=sa + 256): tt(w(xn, 4 * a + b, 4 * e, 4), w("GB", 256 * b + a - sa, 256 * b + e - sa), w("P%d" % b, a, e), OP.add)
+        def upper(b, a=sa, e=se): tt(w(xn, 4 * a + b, 4 * e, 4), w("GB", 256 * b + a - sa, 256 * b + e - sa), w("P%d" % b, a, e), OP.add)
 
         if not last:
             upper(0)
             pack_x(t + 1, 1)
             half(t + 1, 1, 0)
-            upper(1)
-            upper(2)
-            upper(3)
-            half(t + 1, 1, 1)
+            for step in BETWEEN: upper(step) if step else half(t + 1, 1, 1)
 
-    t, o, stores, sp = ROUNDS - 1, 512 * ROUNDS, 9, 256
-    pieces = [(0, sp)] + list(TAIL)
+    t, o = ROUNDS - 1, 512 * ROUNDS
+    pieces = [(0, 256)] + list(TAIL)
+    stores, sp = 9, 256
 
     def store(i):
         a, e = pieces[i]
@@ -586,7 +598,7 @@ def rank_program(g, core, T, topo):
     dma("y", hbm(T.lk[:, :]), w("TRX"), "st", stores)
     upper(1)
     upper(2)
-    for a, e in TAIL: upper(3, a, e)
+    for a, e in TAIL: upper(3, max(a, VW), e)
     for i in range(len(TAIL)): store(i + 1)
     for k in range(4): dma("y", hbm(T.osc[4 * k:4 * k + 4, :]), w("XS", o, o + 512, rows=slice(32 * k, 32 * k + 4)), "st", stores)
     for i in range(len(pieces)): result(i)

import numpy as np
from concourse.mybir import dt, AluOpType as OP, ActivationFunctionType as AF

N, ROUNDS = 4, 2
HW = 264
BIG = 2.0 ** 32
B4 = 2.0 ** 20
FAR = 1e25
C0 = 26
D, WV, EVEN = C0 // 2, 16 * C0, 1 - C0 % 2
VW = 256
BETWEEN = (1, 2, 3, 0)
HFIRST = False
COPIES = (4, 2)
TAIL = ((256, 384), (384, 512))
VPAD, SPAD = 7, 6
WHOLE = 1.5 * 2.0 ** 33
CUTS = (0, 90, 180, 270, 334, 424, 512)
LAG = 2
ROWS = list(range(31, C0 - 1, -1))
DS = WV // 4 + 4
AT = {**{d: DS * d - WV // 4 for d in range(1, D + 1)}, **{c: DS * D - EVEN * WV // 8 + 128 * i for i, c in enumerate([32] + ROWS)}}
TILES = [list(range(D - 1 - D % 2, D + 1))] + [[d - 1, d] for d in range(D - 2 - D % 2, 1, -2)]
NV = len(TILES)
TILES += [[32, 31]] + [ROWS[i:i + 2] for i in range(1, len(ROWS) - 2, 2)] + [ROWS[-2:-1]] * (1 - EVEN) + [ROWS[-1:]]
SV = ["T%d" % k for k in range(NV, len(TILES))]
CODES, F32, BF, F16 = "float8_e4m3fn_x4", "float32", "bfloat16", "float16"

SCRATCH = {}


def buf(names, cols, dtype, where="sbuf"):
    for n in names.split(): SCRATCH[n] = (where, [128, cols], dtype)


buf("X0 XN0 XN1 FH FB", 2048, BF)
buf("UB VB OA OB OC BR0 BR1 TB0 TB1 EA EW DR AK0 AK1 AL0 AL1", 512, BF)
buf("AROW KM RZ CY SL", 256, BF)
buf("CT", VW + 128, BF)
buf("RM", WV // 4, BF)
buf("RD0", 512 - WV, BF)
buf("Z", 520, BF)
buf("ZB", 960, BF)
buf("UQ UR UT VQ OQ AQ AKQ0 AKQ1", 128, CODES)
buf("UQS URS UTS VQS OQS AQS AKS0 AKS1", 128, "uint8")
buf("SQ0 SQ1", 256, CODES)
buf("SS0 SS1", 256, "uint8")
buf("WQ EQ", 512, CODES)
buf("WS EQS", 512, "uint8")
buf("XQ", 512 * 3, CODES)
buf("XS", 512 * 3, "uint8")
buf("QT", AT[C0] + 256, CODES)
buf("QS", AT[C0] + 256, "uint8")
buf("BT", 4 * AT[C0] + 512, BF)
buf("SG", 3 * 512, BF)
buf("I1 OW PAY", 512, F16)
buf("RD", 512 - WV, F16)
buf("F5 FM VP EXB", 264, F16)
buf("EXE", 512, BF)
buf("KB", 1024, BF)
buf("LINKI", 32, "int32")
buf("PK", 128, F32)
buf("SM", 24, F32)
buf("INT", 56, "int32")
buf("UO", 48, "uint16")
buf("RS NT NX", 32, F32)
buf("WK", 192, F32)
buf("EX", 896, F32)
buf("II", 48, "int32")
buf("U16", 80, "uint16")
buf("IOTA", 520, F32)
buf("MSK H POS PKD YS LR0 LR1 NR0 NR1", 512, F32)
buf("HF", WV, F32)
buf("FO LQK0 LQK1", 256, F32)
buf("NMR", 128, F32)
buf("HS", 4 * HW, F32)
buf("GB", 3 * 512, F32)
buf("KQ0 KQ1 LL0 LL1 LI0 LI1 NLL", 32, "uint16")
buf("NL0 NL1 NLI0 NLI1", 8, "uint16")
buf("TRD TRX", 32, F32, "dram")
buf("BRD0 BRX0", 32 * COPIES[0], BF, "dram")
buf("BRD1 BRX1", 32 * COPIES[1], BF, "dram")
buf("PA PB PC PD P0 P1 P2 P3", 512, F32, "psum")

PIECE = {
    "PM": ("SM", 0, 2), "E8": ("SM", 2, 2), "E4": ("SM", 8, 2), "NUP": ("SM", 4, 1), "NUQ": ("SM", 5, 1), "R15": ("SM", 6, 1), "PU": ("SM", 7, 1),
    "MC": ("SM", 10, 1), "U4": ("SM", 11, 1), "M2": ("SM", 12, 1), "U2": ("SM", 13, 1), "U1": ("SM", 14, 1), "IL": ("SM", 15, 1),
    "N4": ("SM", 16, 1), "I4": ("SM", 17, 1), "M4": ("SM", 18, 1), "S4": ("SM", 19, 1), "NU4": ("SM", 20, 1), "MK": ("SM", 21, 1),
    "CX": ("CT", 0, VW), "C4": ("CT", VW, 128),
    "EXS": ("EX", 0, 128), "EXV": ("EX", 128, 128), "EXR": ("EX", 256, 128),
    "UOI": ("INT", 0, 16), "HOI": ("INT", 16, 32), "PI": ("INT", 48, 2), "PJ": ("INT", 50, 2),
    "T1": ("WK", 0, 32), "T3": ("WK", 32, 32), "RK": ("WK", 64, 32), "NA": ("WK", 96, 16), "NB": ("WK", 112, 16), "NN": ("WK", 128, 16),
    "JS": ("WK", 144, 16), "TOT": ("WK", 160, 1),
    "EXK": ("EX", 512, 256), "EXN": ("EX", 768, 128),
    "KQV": ("II", 0, 16), "KQI": ("II", 16, 32),
    "RKU": ("U16", 0, 32), "NU": ("U16", 32, 16), "EL": ("U16", 48, 32),
}
SEMAPHORES = ["cv", "cs", "ct", "cg", "ldx0", "ldx1", "ldu", "ldk", "ldv", "ldw", "ldc", "ldz", "ldo", "nrx", "st"]
for _t in range(ROUNDS):
    SEMAPHORES += [s + "%d" % _t for s in ("bro", "bra", "brl", "tbx", "nma", "nml", "cda", "cdl", "tro", "tra", "trl", "trx", "lia", "lil")]

def both(k): return [(d, h) for d in reversed(TILES[k]) for h in (0, 1) if (d, h) != (D, EVEN)  or not EVEN]


def then(k, *more): return both(k)[:1] + ["T%d" % (k - 1)] + both(k)[1:] + list(more)


VPLAN = (["ones", "turn", "in1", "mask", (D, 2), "links", "U2", "hold", (D - 1, 2), "PU", "in0", "bits", (D - 2, 2)] + [(d, 2) for d in range(D - 3, C0 - 17, -1)] + [(1, 3), (2, 3), (3, 3), "AQ", "F", "OQ"] + both(0)
         + then(1) + then(2, "T6") + then(3) + then(4) + then(5, "T7")
         + ["T5", "T8", "RDU", "small", "T9", "high", "OW", "u0", "u1", "CV", "lifted", "RDL", "EXS", "R15", "low", "PAY0", "RK", "PAY1", "u2", "RKU", "spare0", "POS", "spare1"])
SPLAN = ["ahead", "full"] + ROWS + ["twin0", "twin1", "LR"]
AFTER = [["rows", "k", "turn", "turned", "q", "layer", "came"]] * 2
SLOTS = ((0, 256),)
EARLY = 2


def rank_program(g, core, T, topo):
    rank = T.rank_of(core)
    if rank is None:
        return
    queue = {"v": g.vector, "s": g.scalar, "t": g.tensor, "g": g, "y": g.sync}
    own = {"v": "cv", "s": "cs", "t": "ct", "g": "cg"}
    count = {"cv": 0, "cs": 0, "ct": 0, "cg": 0}
    mark = {s: [] for s in count}
    total = {}
    know = {q: {} for q in queue}
    tokens = []
    wrote = {n: np.full(SCRATCH[n][1][1], -1) for n in SCRATCH}
    read = {n: [] for n in SCRATCH}

    def w(n, a=0, b=None, step=1, rows=None):
        if n in PIECE: name, off, width = PIECE[n]
        else: name, off, width = n, 0, SCRATCH[n][1][1]
        if b is None: b = width
        cols = slice(off + a, off + b) if step == 1 else slice(off + a, off + b, step)
        return (T[name][slice(None) if rows is None else rows, cols], [(name, np.arange(off + a, off + b, step))], [])

    def ind(win, off): return (win[0].indirect(off[0]), win[1], off[1])
    def cast(v, d): return (v[0].bitcast(d), v[1], v[2])
    def hbm(ap): return (ap, [], [])
    def raw(x): return x[0] if isinstance(x, tuple) else x

    def sides(ins, outs):
        r, o = [], []
        for x in ins:
            if isinstance(x, tuple): r += x[1] + x[2]
        for x in outs:
            if isinstance(x, tuple):
                o += x[1]
                r += x[2]
        return r, o

    def settle(q, r, o, sem):
        need = set()
        for n, c in r:
            need |= set(wrote[n][c].tolist())
            if SCRATCH[n][0] == "psum":
                need |= set(wrote[n].tolist()) | set(i for i, _ in read[n] if tokens[i][0] != q)
        for n, c in o:
            if SCRATCH[n][0] == "psum": need |= set(i for i, _ in read[n])
            if q != "t": need |= set(wrote[n][c].tolist())
            need |= set(i for i, d in read[n] if d[c].any())
        need.discard(-1)
        for i in sorted(need, key=lambda i: -tokens[i][2]):
            _, s, val, seen = tokens[i]
            if s == sem and s not in count: continue
            if know[q].get(s, 0) >= val: continue
            if s == own.get(q) and count[s] - LAG > val:
                val = count[s] - LAG
                seen = tokens[mark[s][val - 1]][3]
            queue[q].wait_ge(T.sem[s], val)
            know[q][s] = val
            for s2 in seen: know[q][s2] = max(know[q].get(s2, 0), seen[s2])

    def note(token, r, o):
        tokens.append(token)
        for n, c in o:
            wrote[n][c] = len(tokens) - 1
            for _, d in read[n]: d[c] = False
            read[n] = [] if SCRATCH[n][0] == "psum" else [(i, d) for i, d in read[n] if d.any()]
        for n, c in r:
            d = np.zeros(SCRATCH[n][1][1], bool)
            d[c] = True
            read[n].append((len(tokens) - 1, d))

    def op(q, call, ins, outs):
        r, o = sides(ins, outs)
        settle(q, r, o, None)
        sem = own[q]
        call().then_inc(T.sem[sem], 1)
        count[sem] += 1
        total[sem] = count[sem]
        mark[sem].append(len(tokens))
        note((q, sem, count[sem], dict(know[q])), r, o)

    def dma(q, out, in_, sem, of, after=()):
        r, o = sides([in_] + list(after), [out])
        settle(q, r, o, sem)
        queue[q].dma_start(out[0], in_[0]).then_inc(T.sem[sem], 16)
        total[sem] = 16 * of
        note((q, sem, 16 * of, dict(know[q])), sides([in_], [])[0], o)

    def send(dst, out, in_, rsem, lsem, of=1):
        r, _ = sides([in_], [])
        settle("g", r, [], None)
        rid, pid = topo.addr(dst)[:2]
        n = len(topo.engines(core, dst))
        g.remote_dma(out[0], in_[0], T.sem[rsem], T.sem[lsem], pid, rid, topo.mask(core, dst))
        total[lsem] = n * of
        note(("g", lsem, n * of, dict(know["g"])), r, [])

    def lands(src, views, rsem):
        n = len(topo.engines(src, core)) * len(views)
        total[rsem] = n
        note(("far", rsem, n, {}), [], sides([], views)[1])

    V, S, G = g.vector, g.scalar, g

    def ts(out, in0, a, b, op0, op1=None):
        if op1 is None: op("v", lambda: V.tensor_scalar(out[0], in0[0], raw(a), None, op0), [in0, a], [out])
        else: op("v", lambda: V.tensor_scalar(out[0], in0[0], raw(a), raw(b), op0, op1), [in0, a, b], [out])

    def tt(out, in0, in1, o): op("v", lambda: V.tensor_tensor(out[0], in0[0], in1[0], o), [in0, in1], [out])
    def cp(out, in_): op("v", lambda: V.tensor_copy(out[0], in_[0]), [in_], [out])
    def fill(out, c): op("v", lambda: V.memset(out[0], c), [], [out])
    def scan(out, d0, d1, op0, op1, first=0.0): op("v", lambda: V.tensor_tensor_scan(out[0], d0[0], d1[0], first, op0, op1), [d0, d1], [out])
    def quant(q, s, in_): op("v", lambda: V.quantize_mx(q[0], s[0], in_[0]), [in_], [q, s])
    def mm(out, a, asc, b, bsc, start=True, stop=True): op("t", lambda: g.tensor.matmul_mx(out[0], a[0], asc[0], b[0], bsc[0], start, stop), [a, asc, b, bsc], [out])
    def iota(out, pattern, base, cm): op("g", lambda: G.iota(out[0], pattern, base, cm, allow_small_or_imprecise_dtypes=True), [], [out])
    def iotai(out, pattern, base, cm): op("g", lambda: G.iota(out[0], pattern, base, cm), [], [out])
    def select(out, in_, pattern, cmp, c, base, cm): op("g", lambda: G.affine_select(out[0], in_[0], pattern, cmp, c, base, cm), [in_], [out])

    def act(out, in_, func, scale=1.0, bias=None, accum=None):
        if accum is not None: op("s", lambda: S.activation(out[0], in_[0], func, accum_out=accum[0]), [in_], [out, accum])
        elif bias is None and scale == 1.0: op("s", lambda: S.activation(out[0], in_[0], func), [in_], [out])
        elif bias is None: op("s", lambda: S.activation(out[0], in_[0], func, scale=raw(scale)), [in_, scale], [out])
        else: op("s", lambda: S.activation(out[0], in_[0], func, bias=raw(bias), scale=raw(scale)), [in_, bias, scale], [out])

    def lift(ex, row, a, b, by="CX"): scan(w(ex, a, b), w(by, 0, b - a), w(row, a, b), OP.mult, OP.add if by == "CX" else OP.max)
    def top(ex, a, b): return w(ex, a + 15, b, 16)
    def down(out, ex, a, b, more=None): ts(out, top(ex, a, b), w("MC"), more, OP.mult, None if more is None else OP.add)

    rows8 = slice(0, 128, 16)
    nxt = [T.cores[(rank + 2 ** t) % N] for t in range(ROUNDS)]
    prv = [T.cores[(rank - 2 ** t) % N] for t in range(ROUNDS)]

    dma("s", w("UB"), hbm(T.u[:, :]), "ldu", 1)
    dma("y", w("X0", 1024, 2048), hbm(T.x[:, 1024:2048]), "ldx1", 1)
    dma("s", w("LINKI"), hbm(T.link[:, :]), "ldk", 1)
    dma("y", w("X0", 0, 1024), hbm(T.x[:, 0:1024]), "ldx0", 1)

    r16 = slice(0, 16)
    fill(w("ZB"), 0.0)
    iotai(w("PI"), [[0, 2]], 0, 1)
    iotai(w("UOI"), [[1, 2], [16, 8]], 0, 0)
    iotai(w("HOI"), [[16, 32]], 15, 0)
    iota(w("AROW"), [[0, 16], [1, 16]], 0, 0)
    iota(w("E8"), [[0, 2]], -3, -8)
    iota(w("IOTA"), [[1, 520]], 0, 0)
    iota(w("E4"), [[0, 2]], -3, -4)
    pads = [(4 * AT[c] + 16 * c, 512 - 16 * c) for c in reversed(ROWS)] + [(4 * AT[d] - 16, 16) for d in range(1, D + 1)]
    ts(w("PJ"), w("PI"), 15, None, OP.bitwise_and)
    for a, n in pads[-3:]: fill(w("BT", a, a + n), 0.0)
    cp(w("UO"), w("INT", 0, 48))
    cp(w("PM"), w("PJ"))
    pm = w("PM", 0, 1)
    quant(w("QT", AT[32], AT[32] + 128), w("QS", AT[32], AT[32] + 128), w("ZB", 0, 512))
    for a, n in pads[VPAD:VPAD + SPAD]: act(w("BT", a, a + n), w("ZB", 0, n), AF.Copy)
    column = {
        "U1": lambda: ts(w("U1"), pm, 15.0, 1.0, OP.is_lt, OP.add), "U2": lambda: ts(w("U2"), w("U1"), 1.0 / 512, None, OP.mult),
        "PU": lambda: ts(w("PU"), pm, 1024.0, w("U2"), OP.add, OP.mult), "NUP": lambda: ts(w("NUP"), pm, 15.0, 2.0, OP.is_equal, OP.subtract),
        "M2": lambda: ts(w("M2"), pm, 15.0, 0.5, OP.is_equal, OP.max), "M4": lambda: ts(w("M4"), pm, 12.0, 1.0 / B4, OP.is_ge, OP.max),
        "MC": lambda: ts(w("MC"), pm, 15.0, 1.0 / BIG, OP.is_equal, OP.max),
        "R15": lambda: ts(w("R15"), pm, -1.0, 16 * (D - EVEN) + 15.25, OP.mult, OP.add),
    }
    ts(w("N4"), pm, 12.0, B4, OP.is_lt, OP.mult)
    for a, n in pads[:4]: fill(w("BT", a, a + n), 0.0)
    ts(w("KM"), w("AROW"), pm, -2.0 * FAR, OP.not_equal, OP.mult)
    ts(w("U4"), w("N4"), 1.0, None, OP.max)
    quant(w("UQ"), w("UQS"), w("UB"))
    select(w("ZB", 448, 512), w("ZB", 448, 512), [[0, 4], [-1, 4], [1, 4]], OP.not_equal, 1.0, 0, 0)
    for i in range(8): dma("y", w("OC", rows=slice(16 * i, 16 * i + 16)), w("ZB", 448 - 64 * i, 960 - 64 * i, rows=slice(16 * i, 16 * i + 16)), "ldo", 8)

    def lift_constants():
        select(w("C4", rows=r16), w("ZB", 0, 128, rows=r16), [[0, 32], [-4, 4]], OP.is_ge, B4, 0, 1)
        select(w("CX", rows=r16), w("ZB", 0, VW, rows=r16), [[0, VW // 16], [-1, 16]], OP.is_ge, 1.0, 0, 1)
        select(w("C4", rows=r16), w("C4", rows=r16), [[0, 32], [-4, 4]], OP.is_ge, 1.0, 4, 1)
        select(w("CX", rows=r16), w("CX", rows=r16), [[0, VW // 16], [1, 16]], OP.not_equal, BIG, -1, -1)
        for i in range(1, 8): dma("y", w("CT", rows=slice(16 * i, 16 * i + 16)), w("CT", rows=r16), "ldc", 7)

    def pick_u(q, o):
        cp(cast(w(q), dt.uint32), ind(cast(w("UQ"), dt.uint32), w("UO", o, o + 8)))
        act(w(q + "S"), ind(w("UQS"), w("UO", o, o + 8)), AF.Copy)

    def xq(t, h): return w("XQ", 512 * t + 256 * h, 512 * t + 256 * h + 256), w("XS", 512 * t + 256 * h, 512 * t + 256 * h + 256)
    def pack_x(t, h): quant(*xq(t, h), w("XN%d" % (t - 1) if t else "X0", 1024 * h, 1024 * h + 1024))
    def eq(b): return w("EQ", 128 * b, 128 * b + 128), w("EQS", 128 * b, 128 * b + 128)
    def unit(b): quant(*eq(b), w("Z", 3 - b, 515 - b))

    def half(t, h, step):
        a = 256 * h
        if step == 0:
            mm(w("P" + "3A"[h], 0, 256), w("UR"), w("URS"), *xq(t, h))
            if h == 0: mm(w("PB", 0, 496), w("UR"), w("URS"), w("XQ", 512 * t, 512 * t + 496), w("XS", 512 * t, 512 * t + 496))
            mm(w("P" + "DC"[h], 0, 256), w("UT"), w("UTS"), *xq(t, h))
        if step == 1: tt(w("MSK", a, a + 256), w("P" + "3A"[h], 0, 256), w("KM"), OP.add)
        if step == 2: scan(w("H", a, a + 256), w("RZ"), w("MSK", a, a + 256), OP.min, OP.max)
        if step == 3: ts(w("BR%d" % t, a, a + 256), w("P" + "DC"[h], 0, 256), 0.0, 1024.0, OP.is_gt, OP.mult)
        if step == 4: act(w("HF", a, min(a + 256, WV)), ind(w("H", a, a + 256), w("UO", 16, 16 + min(16, C0 - 16 * h))), AF.Copy)

    for n in ("U1", "M4"): column[n]()
    pick_u("UR", 0)
    for a, n in pads[VPAD + SPAD:-3]: fill(w("BT", a, a + n), 0.0)
    pack_x(0, 1)
    mm(w("PA", 0, 256), w("UR"), w("URS"), *xq(0, 1))
    pick_u("UT", 8)
    mm(w("PC", 0, 256), w("UT"), w("UTS"), *xq(0, 1))
    act(w("RZ"), w("AROW"), AF.Copy, 2.0 * FAR, -FAR)
    cp(w("LL0"), w("LINKI"))
    send(nxt[0], w("LI0"), w("LL0"), "lia0", "lil0")
    for a, n in pads[4:VPAD]: fill(w("BT", a, a + n), 0.0)
    half(0, 1, 1)
    act(w("SG", 0, 520), w("IOTA"), AF.Abs, 1.0, w("E4", 0, 1))
    act(w("OA"), w("IOTA", 0, 512), AF.Abs, 2.0, w("E8", 0, 1))
    act(w("Z"), w("SG", 0, 520), AF.Relu, -1.0, 1.0)

    def turned(t):
        lands(T.cores[(rank - 2 ** t + 2 ** t // 2) % N], [w("LI%d" % t)], "lia%d" % t)
        act(w("NR%d" % t), ind(w("LR%d" % t), w("LI%d" % t)), AF.Copy)
        if t == ROUNDS - 1:
            dma("y", w("TRD"), w("NR%d" % t, rows=rows8), "tro%d" % t, 1)
            send(prv[t], w("TRX"), w("TRD"), "tra%d" % t, "trl%d" % t)
        else:
            for h in range(2): dma("y", w("NT", 16 * h, 16 * h + 16), w("NR%d" % t, rows=slice(16 * h, 128, 32)), "nrx", 2)

    for t in range(ROUNDS):
        last = t == ROUNDS - 1
        xc, xs = w("XQ", 512 * t, 512 * t + 512), w("XS", 512 * t, 512 * t + 512)
        ll, lr, kq, br, tb = ("%s%d" % (n, t) for n in ("LL", "LR", "KQ", "BR", "TB"))
        def scores(P, n): mm(w(P, 0, n), w("UR"), w("URS"), w("XQ", 512 * t, 512 * t + n), w("XS", 512 * t, 512 * t + n))
        def unpack(b): mm(w("P%d" % b), *eq(b), xc, xs)
        def halved(b): act(w("FH", 512 * b, 512 * b + 512), w("P%d" % b), AF.Copy, 0.5)

        if t == 0: half(t, 1, 3)
        else:
            act(w("EA", 256, 512), w("PC", 0, 256), AF.Sign)
            act(w(br, 256, 512), w("EA", 256, 512), AF.Relu, 1024.0)
        if HFIRST:
            half(t, 1, 2)
            half(t, 1, 4)
        pack_x(t, 0)
        half(t, 0, 0)
        scores("PC", WV)
        if not HFIRST:
            half(t, 1, 2)
            half(t, 1, 4)

        def links():
            if t == 0: return
            cp(w("NLL"), w("NX"))
            send(prv[t - 1], w(ll), w("NLL"), "tra%d" % (t - 1), "trl%d" % (t - 1))
            send(T.cores[(rank - 2 ** (t - 1) + 2 ** t) % N], w("LI%d" % t), w("NLL"), "lia%d" % t, "lil%d" % t)
            lands(nxt[t - 1], [w(ll)], "tra%d" % (t - 1))

        def slot(c, a, b): return w("BT", 4 * AT[c] + a, 4 * AT[c] + b)
        def codes(a, n): return w("QT", a + 128 * (a >= AT[32]), a + 128 * (a >= AT[32]) + n), w("QS", a + 128 * (a >= AT[32]), a + 128 * (a >= AT[32]) + n)
        def mine(c): return w("H", 16 * c + 15, 16 * c + 16)
        def signs(c): return w("SG", 512 * (c % 3), 512 * (c % 3) + 16 * c)
        def sign(c): act(signs(c), w("PB", 0, 16 * c), AF.Sign, -1.0, mine(c))
        def beats(c): act(slot(c, 0, 16 * c), signs(c), AF.Relu, accum=w("RS", c, c + 1))
        def inside(h): tt(slot(32, 256 * h, 256 * h + 256), w("P" + "3A"[h], 0, 256), w("H", 256 * h, 256 * h + 256), OP.is_le)

        def apart(d, h):
            e = WV - 16 * d
            a = 256 - 16 * d if (d, 2) in VPLAN else 256 if (d, 3) in VPLAN else e
            if h == 0: tt(slot(d, 0, a), w("PC", 0, a), w("HF", 16 * d, 16 * d + a), OP.is_lt)
            if h == 1: tt(slot(d, e, WV), w("PC", e, WV), w("HF", 0, 16 * d), OP.is_le)
            if h == 2: tt(slot(d, a, e), w("P3", a, e), w("HF", 256, WV), OP.is_lt)
            if h == 3: tt(slot(d, a, e), w("PA", 0, e - a), w("HF", 256 + 16 * d, WV), OP.is_lt)

        def bits():
            half(t, 0, 3)
            k = 16 // COPIES[t]
            dma("y", w("BRD%d" % t), w(br, rows=slice(0, 128, k)), "bro%d" % t, 1)
            send(prv[t], w("BRX%d" % t), w("BRD%d" % t), "bra%d" % t, "brl%d" % t)
            lands(nxt[t], [w("BRX%d" % t)], "bra%d" % t)
            for a in range(k): dma("y", w(tb, rows=slice(a, 128, k)), w("BRX%d" % t), "tbx%d" % t, k)
            if t == 0:
                lift_constants()
                dma("y", cast(w("WQ"), dt.uint8), hbm(T.wc[:, :]), "ldw", 2)
                dma("y", w("WS"), hbm(T.ws[:, :]), "ldw", 2)
                dma("y", w("VB"), hbm(T.v[:, :]), "ldv", 1)
                iota(w("RD0"), [[-16, 32 - C0], [1024, 16]], 16 * (D - EVEN) - WV, 0)
                iota(w("RM", 0, 4 * D), [[0, D], [1024, 4]], 0, 0)
                iota(w("RM", 4 * D, 4 * C0), [[0, C0 - D], [1024, 4]], -16 * EVEN, 0)
                iota(w("I1"), [[1, 512]], 1024, 0)
                for z in (w("F5", 256, 257), w("FM", 0, 1)): iota(z, [[0, 1]], 0, 0)
                iota(w("PK"), [[0, 64], [4096, 2]], 0, 0)
                iota(w("HS", 256, 4 * HW, HW), [[0, 4]], 0, 0)
                iota(w("SL", 0, 128), [[0, 128]], 256, 0)
                iota(w("SL", 128, 256), [[1, 128]], 128, 0)
                iota(w("DR", 0, 512, 2), [[0, 256]], 256, 0)

        signed = []

        def done(k):
            a = AT[TILES[k][0]] - 4 * (k < NV)
            n = len(TILES[k]) * (DS if k < NV else 128) - EVEN * (k == 0) * WV // 8
            quant(*codes(a, n), w("BT", 4 * a, 4 * (a + n)))
            won = [AT[d] + WV // 4 - 4 * d for d in TILES[k] if d < D + 1 - EVEN] + [0] * (k == NV - 1) if k < NV else [AT[32]] * (k == NV)
            for c in TILES[k]: mm(w("P3" if k < NV else "PD", 0, 128), w("OQ"), w("OQS"), *codes(AT[c], 128), c in (TILES[0][0], 32), c in (TILES[NV - 1][-1], C0))
            for a in won: mm(w("PA", 0, 128), w("AQ"), w("AQS"), *codes(a, 128), k == 0 and a == won[0], k == NV - 1 and a == won[-1])

        def ahead(n):
            for r in ROWS[len(signed):n]:
                sign(r)
                signed.append(r)

        def srow(c):
            ahead(ROWS.index(c) + 2)
            beats(c)

        def low():
            tt(w("T1", 0, C0), w("EXR", 3, WV // 4, 4), w("EXV", 3, WV // 4, 4), OP.subtract)

        def high():
            tt(w("T3", C0, 32), w("RS", C0, 32), w("RD", 15, 512 - WV, 16), OP.add)

        def twin(a): act(w("EA", a, a + 256), ind(w(tb), w(ll, a // 16, a // 16 + 16)), AF.Copy, -1.0, 2048.0)
        def pay(a, b): scan(w("PAY", a, b), w("OW", a, b), w("EA", a, b), OP.max, OP.subtract)

        steps = {
            "in0": lambda: inside(0), "in1": lambda: inside(1), "ahead": lambda: ahead(1), "low": low, "high": high,
            "mask": lambda: half(t, 0, 1), "hold": lambda: half(t, 0, 2), "full": lambda: half(t, 0, 4), "bits": bits, "links": links,
            "turn": lambda: op("v", lambda: V.transpose(w("NX")[0], w("NT")[0]), [w("NT")], [w("NX")]) if t else None,
            "ones": lambda: ts(w("OB"), w("OA"), 4.0, w("U4"), OP.is_lt, OP.mult) if t == 0 else None,
            "F": lambda: [unpack(b) for b in range(EARLY if t else 0)],
            "AQ": lambda: quant(w("AQ"), w("AQS"), w("OB")) if t == 0 else None,
            "OQ": lambda: quant(w("OQ"), w("OQS"), w("OC")) if t == 0 else None,
            "RDU": lambda: scan(w("RD"), w("RD0"), slot(32, WV, 512), OP.min, OP.add),
            "RDL": lambda: scan(w("EXR", 0, WV // 4), w("RM"), w("PA", 0, WV // 4), OP.min, OP.add),
            "CV": lambda: scan(w("EXV", 0, WV // 4), w("C4", 0, WV // 4), w("P3", 0, WV // 4), OP.mult, OP.add),
            "twin0": lambda: twin(0), "twin1": lambda: twin(256), "PAY0": lambda: pay(0, 256), "PAY1": lambda: pay(256, 512),
            "OW": lambda: scan(w("OW"), w("I1"), w(br), OP.max, OP.subtract),
            "u0": lambda: unit(0) if t == 0 else None, "u1": lambda: unit(1) if t == 0 else None, "u2": lambda: (unit(2), unpack(2)) if t == 0 else None,
            "lifted": lambda: ts(w("T1", C0, 32), w("T3", C0, 32), w("U4"), None, OP.mult),
            "small": lambda: ts(w("RM"), w("RM"), w("U4"), None, OP.mult) if t == 0 else None,
            "LR": lambda: act(w(lr), ind(w("IOTA", 0, 512), w(ll)), AF.Copy),
            "EXS": lambda: (scan(w("EXS"), w("C4"), w("PD", 0, 128), OP.mult, OP.add), [unpack(b) for b in (range(EARLY, 4) if t else (0, 1))]),
            "RK": lambda: tt(w("RK"), w("EXS", 3, 128, 4), w("T1"), OP.subtract),
            "RKU": lambda: ts(w("RKU"), w("RK"), w("M4"), w("R15"), OP.mult, OP.add),
            "POS": lambda: cp(ind(w("POS"), w("RKU")), w("PAY")),
            "spare0": lambda: quant(w("VQ"), w("VQS"), w("VB")) if last else (unit(3), unpack(3)),
            "spare1": lambda: ts(w("CY"), w("CX", 0, 256), 2.0, None, OP.min) if t == 0 else None,
        }
        needs = {"full": ["hold"], "twin0": ["links"], "PAY0": ["twin0"], "PAY1": ["LR"]}
        needs.update({"T%d" % k: [c for c in r if c < 32] for k, r in enumerate(TILES) if k >= NV})
        needs.update({(d, h): ["full"] for d in range(1, D + 1) for h in (0, 1)})
        issued = []

        def issue(plan, upto):
            for step in plan[:plan.index(upto) + 1]:
                if step in issued: continue
                for other in needs.get(step, ()): issue(VPLAN if other in VPLAN else SPLAN, other)
                issued.append(step)
                if step in steps: steps[step]()
                elif step in column: column[step]() if t == 0 else None
                elif isinstance(step, str): done(int(step[1:]))
                elif isinstance(step, tuple): apart(*step)
                else: srow(step)

        issue(VPLAN, VPLAN[-1])
        if t == 0: act(w("JS"), w("IOTA", 0, 256, 16), AF.Identity, w("U2"), w("PU"))
        for b in range(4): halved(b)
        ts(w("F5", 0, 256), w("POS", 1, 512, 2), WHOLE, WHOLE - 1024.0, OP.add, OP.not_equal)

        def pair(i): scan(w("PKD", CUTS[i], CUTS[i + 1]), w("PK", 0, CUTS[i + 1] - CUTS[i]), w("POS", CUTS[i], CUTS[i + 1]), OP.mult, OP.add)

        def spare(*names):
            for n in names if t == 0 else (): column[n]()

        pair(0)
        spare("NUP")
        ts(w("FM", 1, 257), w("F5", 0, 256), -511.0 / 512, None, OP.mult)
        pair(1)
        spare("M2")
        scan(w("VP", 0, 257), w("FM", 0, 257), w("F5", 0, 257), OP.add, OP.add, 2.0)
        pair(2)
        spare("MC")
        lift("EXB", "VP", 0, 256, "CY")
        ts(w("TOT"), w("VP", 256, 257), 0.5, w("NUP"), OP.add, OP.mult)
        pair(3)
        tt(w("NB"), w("JS"), top("EXB", 0, 256), OP.subtract)
        ts(w("NA"), top("EXB", 0, 256), w("TOT"), None, OP.add)
        pair(4)
        tt(w("NN"), w("NA"), w("NB"), OP.max)
        pair(5)
        ts(w("NU"), w("NN"), w("M2"), 512.0, OP.mult, OP.mult)
        cp(ind(w("FO"), w("NU")), w("PKD", 1, 512, 2))
        (va, ve), (sa, se) = ((0, VW), (VW, 512)) if last else ((512 - VW, 512), (0, 512 - VW))
        for b in range(4): act(w("FB", VW * b, VW * b + VW), w("P%d" % b, va, ve), AF.Copy)
        act(w("DR", 1, 512, 2), ind(w("SL"), w("NU")), AF.Copy)
        act(w("EW"), ind(w("DR"), w("RKU")), AF.Copy)
        def ks(h): ts(w("KQI", 16 * h, 16 * h + 8), w("KQV", 8 * h, 8 * h + 8), 12, 511, OP.logical_shift_right, OP.bitwise_and)
        def qs(h): ts(w("KQI", 16 * h + 8, 16 * h + 16), w("KQV", 8 * h, 8 * h + 8), 511, None, OP.bitwise_and)

        for h in range(2): lift("EXK", "FO", 128 * h, 128 * h + 128)
        for h in range(2): ts(w("KQV", 8 * h, 8 * h + 8), top("EXK", 128 * h, 128 * h + 128), w("MC"), 2048.0 * 4097, OP.mult, OP.add)
        ks(0)
        qs(0)
        ks(1)
        cp(w(kq, 0, 16), w("KQI", 0, 16))
        qs(1)

        def first(h, b):
            o, i = (16, 512) if h == "L" else (0, 0)
            act(w("KB", i + 128 * b, i + 128 * b + 128), ind(w("FH", 512 * b, 512 * b + 512), w(kq, o, o + 8)), AF.Copy)

        def second(h, b):
            o, i = (24, 512) if h == "L" else (8, 0)
            tt(w("A%s%d" % (h, t), b, 512, 4), ind(w("FH", 512 * b, 512 * b + 512), w(kq, o, o + 8)), w("KB", i + 128 * b, i + 128 * b + 128), OP.add)

        def pack(h): quant(w("A%sQ%d" % (h, t)), w("A%sS%d" % (h, t)), w("A%s%d" % (h, t)))

        def turn_rows():
            act(w("LQK%d" % t, 0, 128), ind(w(lr), w(kq, 24, 32)), AF.Copy)
            act(w("LQK%d" % t, 128, 256), ind(w(lr), w(kq, 16, 24)), AF.Copy)

        for b in (1, 2, 3): first("K", b)
        act(w("NMR"), ind(w(lr), w(kq, 8, 16)), AF.Copy)
        cp(w("KB", 0, 128), ind(w("FH", 0, 512), w(kq, 0, 8)))
        cp(w(kq, 16, 32), w("KQI", 16, 32))
        for b in (1, 0, 2, 3): second("K", b)
        lift("EXN", "NMR", 0, 128)
        pack("K")
        down(w("NL%d" % t), "EXN", 0, 128)
        vq, vs = "SQ%d" % t, "SS%d" % t
        send(nxt[t], cast(w(vq, 0, 128), dt.uint8), cast(w("AKQ%d" % t), dt.uint8), "cda%d" % t, "cdl%d" % t, 2)
        send(nxt[t], w(vs, 0, 128), w("AKS%d" % t), "cda%d" % t, "cdl%d" % t, 2)
        send(nxt[t], w("NLI%d" % t), w("NL%d" % t), "nma%d" % t, "nml%d" % t)
        lands(prv[t], [w("NLI%d" % t)], "nma%d" % t)
        lands(prv[t], [w(vq, 0, 128), w(vs, 0, 128)], "cda%d" % t)

        def layer():
            quant(w(vq, 128, 256), w(vs, 128, 256), w("AL%d" % t))
            for a, e in SLOTS:
                for b in range(4):
                    mm(w("P" + "ABCD"[b], 0, e - a), w("WQ", 128 * b, 128 * b + 128), w("WS", 128 * b, 128 * b + 128), w(vq, a, e), w(vs, a, e))
                    act(w("HS", HW * b + a, HW * b + e), w("P" + "ABCD"[b], 0, e - a), AF.Copy, 0.03125)

        def turn(a, e): cp(ind(w(lr), w(kq, 16 + a, 16 + e)), w("LQK%d" % t, 16 * a, 16 * e))

        after = {
            "rows": turn_rows, "k": lambda: [first("L", b) for b in range(4)], "q": lambda: [second("L", b) for b in range(4)], "layer": layer,
            "turn": lambda: turn(0, 16), "turn0": lambda: turn(0, 8), "turn1": lambda: turn(8, 16), "turned": lambda: turned(t),
            "came": lambda: cp(ind(w("EW"), w("NLI%d" % t)), w("IOTA", 0, 128)),
        }
        for step in AFTER[t]: after[step]()
        for a, e in ((va, ve), (sa, se)): lift("EXE", "EW", a, e)
        for a, e in ((va, ve), (sa, se)): down(w("EL", a // 16, e // 16), "EXE", a, e)
        xn = "XN%d" % t

        def picked(b, a, e): return ind(w("HS", HW * b, HW * b + HW), w("EL", a // 16, e // 16))
        for b in range(4): act(w("GB", 256 * b, 256 * b + se - sa), picked(b, sa, se), AF.Copy)
        if "turned" not in AFTER[t]: turned(t)
        for b in range(4): tt(w(xn, 4 * va + b, 4 * ve, 4), picked(b, va, ve), w("FB", VW * b, VW * b + VW), OP.add)

        def upper(b, a=sa, e=se): tt(w(xn, 4 * a + b, 4 * e, 4), w("GB", 256 * b + a - sa, 256 * b + e - sa), w("P%d" % b, a, e), OP.add)

        if not last:
            upper(0)
            pack_x(t + 1, 1)
            half(t + 1, 1, 0)
            for step in BETWEEN: upper(step) if step else half(t + 1, 1, 1)

    t, o = ROUNDS - 1, 512 * ROUNDS
    pieces = [(0, 256)] + list(TAIL)
    stores, sp = 9, 256

    def store(i):
        a, e = pieces[i]
        q, s = w("XQ", o + a, o + e), w("XS", o + a, o + e)
        quant(q, s, w(xn, 4 * a, 4 * e))
        mm(w("P" + "ABC"[i], 0, e - a), w("VQ"), w("VQS"), q, s)
        if i: a = sp
        if e in (sp, 512): dma("y", hbm(T.oc[:, 4 * a:4 * e]), cast(w("XQ", o + a, o + e), dt.uint8), "st", stores)

    def result(i):
        a, e = pieces[i]
        if i + 1 < len(pieces): act(w("YS", a, e), w("P" + "ABC"[i], 0, e - a), AF.Copy)
        else: cp(w("YS", a, e), w("P" + "ABC"[i], 0, e - a))
        if i: a = sp
        if e in (sp, 512): dma("s", hbm(T.y[:, a:e]), w("YS", a, e), "st", stores)

    upper(0)
    store(0)
    lands(nxt[t], [w("TRX")], "tra%d" % t)
    dma("y", hbm(T.lk[:, :]), w("TRX"), "st", stores)
    upper(1)
    upper(2)
    for a, e in TAIL: upper(3, max(a, VW), e)
    for i in range(len(TAIL)): store(i + 1)
    for k in range(4): dma("y", hbm(T.osc[4 * k:4 * k + 4, :]), w("XS", o, o + 512, rows=slice(32 * k, 32 * k + 4)), "st", stores)
    for i in range(len(pieces)): result(i)
    for sem in total:
        if know["g"].get(sem, 0) < total[sem]: g.wait_ge(T.sem[sem], total[sem])
